import numpy as np
import ml_dtypes


def mxq(x, axis, fmt="e4m3"):
    dtype, down = {"e4m3": (ml_dtypes.float8_e4m3fn, 7), "e5m2": (ml_dtypes.float8_e5m2, 14)}[fmt]
    v = np.moveaxis(np.asarray(x, np.float32).astype(ml_dtypes.bfloat16).astype(np.float64), axis, -1)
    blocks = v.reshape(v.shape[:-1] + (-1, 32))
    amax = np.abs(blocks).max(-1, keepdims=True)
    byte = np.maximum(np.where(amax > 0, np.frexp(amax)[1] - 1 + 127, 0) - down, 1)
    scale = np.exp2(byte - 127.0)
    codes = (blocks / scale).astype(np.float32).astype(dtype).astype(np.float64)
    return np.moveaxis((codes * scale).reshape(v.shape), -1, axis)


WIDE = False


def mx_kscale(k):
    if not WIDE:
        return np.ones(k)
    levels = np.array([10, -10, 5, -5, 0])
    if k % 512:
        return np.exp2(np.random.permutation(np.resize(levels, k // 32))).repeat(32)
    a = np.empty((k // 512, 16))
    for p in range(k // 512):
        a[p, :8] = np.random.permutation(np.resize(levels, 8))
        for g in range(8):
            far = levels[np.abs(levels - a[p, g]) >= 10]
            a[p, g + 8] = far[np.random.randint(len(far))]
    return np.exp2(a.ravel()).repeat(32)


def f64(x):
    return np.asarray(x).astype(np.float64)


def striped(idx):
    return np.tile(idx.reshape(-1, 16).T, (8, 1)).astype(np.uint16)


def unstriped(offs):
    return offs[:16].T.reshape(-1).astype(np.int64)


def striped8(idx):
    return np.concatenate([x.reshape(-1, 16).T for x in idx]).astype(np.uint16)


def runs(offs, k):
    lists = np.stack([offs[16 * r : 16 * r + 16].T.reshape(-1) for r in range(8)]).astype(np.int64)
    return lists[np.arange(k) % 512 // 64]


def pack_weight(w):
    k, n = w.shape
    w = f64(np.asarray(w, np.float32).astype(ml_dtypes.bfloat16)).reshape(k // 32, 32, n)
    amax = np.abs(w).max(1)
    byte = np.clip(np.where(amax > 0, np.frexp(amax)[1] - 1 + 127 - 7, 1), 1, 254)
    scaled = (w * np.exp2(127.0 - byte)[:, None, :]).reshape(k, n).astype(np.float32)
    words = np.ascontiguousarray(scaled.reshape(k // 512, 128, 4, n).transpose(0, 1, 3, 2)).astype(ml_dtypes.float8_e4m3fn).view(np.uint8)
    return words, np.ascontiguousarray(byte.astype(np.uint8).reshape(k // 512, 16, n))


def unpack_weight(words, scales):
    g, p, n, _ = words.shape
    vals = np.ascontiguousarray(words).view(ml_dtypes.float8_e4m3fn).astype(np.float64) * np.repeat(np.exp2(scales.astype(np.float64) - 127.0), 8, axis=1)[..., None]
    return vals.transpose(0, 1, 3, 2).reshape(g * 512, n)


E2M1 = np.array([0.0, 0.5, 1.0, 1.5, 2.0, 3.0, 4.0, 6.0, -0.0, -0.5, -1.0, -1.5, -2.0, -3.0, -4.0, -6.0])


def pack_fp4(w):
    k, n = w.shape
    w = f64(np.asarray(w, np.float32).astype(ml_dtypes.bfloat16)).reshape(k // 32, 32, n)
    amax = np.abs(w).max(1)
    mant, ex = np.frexp(amax / 6.0)
    byte = np.clip(np.where(amax > 0, np.where(mant > 0.5, ex, ex - 1) + 127, 1), 1, 254)
    scaled = (w * np.exp2(127.0 - byte)[:, None, :]).reshape(k, n).astype(np.float32)
    c = np.ascontiguousarray(scaled.reshape(k // 512, 128, 4, n).transpose(0, 1, 3, 2)).astype(ml_dtypes.float4_e2m1fn).view(np.uint8) & 0xF
    words = (c[..., 0::2] | (c[..., 1::2] << 4)).reshape(k // 512, 128, 2 * n)
    return np.ascontiguousarray(words), np.ascontiguousarray(byte.astype(np.uint8).reshape(k // 512, 16, n))


def unpack_fp4(words, scales):
    g, _, n = scales.shape
    words = np.ascontiguousarray(words).reshape(g, 128, n, 2)
    nib = np.empty((g, 128, n, 4), np.uint8)
    nib[..., 0::2] = words & 0xF
    nib[..., 1::2] = words >> 4
    vals = E2M1[nib] * np.repeat(np.exp2(scales.astype(np.float64) - 127.0), 8, axis=1)[..., None]
    return vals.transpose(0, 1, 3, 2).reshape(g * 512, n)


def gelu(v):
    return 0.5 * v * (1.0 + np.tanh(np.sqrt(2.0 / np.pi) * (v + 0.044715 * v**3)))

def planes(y):
    n, m = y.shape
    v = y.astype(np.float32).astype(ml_dtypes.bfloat16).astype(np.float64).reshape(n // 32, 32, m)
    top = np.abs(v).max(1)
    byte = np.clip(np.where(top > 0, np.frexp(top)[1] - 1 + 127 - 7, 1), 1, 254)
    codes = (v * np.exp2(127.0 - byte)[:, None, :]).reshape(n, m).astype(np.float32).astype(ml_dtypes.float8_e4m3fn).view(np.uint8)
    words = codes.reshape(n // 512, 128, 4, m).transpose(0, 1, 3, 2)
    return np.ascontiguousarray(words), np.ascontiguousarray(byte.astype(np.uint8).reshape(n // 512, 16, m))


K, T, S, N, H = 512, 2048, 512, 512, 512


def setup_inputs():
    n = np.random.standard_normal
    s = mx_kscale(K)[:, None]
    u = mx_kscale(H)
    packed_xT = pack_weight(n((K, T)) * s)
    packed_w3 = pack_fp4(n((H, N)) / np.sqrt(H) / u[:, None])
    return {
        "x_words": packed_xT[0],
        "x_scales": packed_xT[1],
        "w1": (n((K, H)) / np.sqrt(K) / s * u).astype(np.float32),
        "eps": np.random.uniform(1.0, 1.5, (H, 1)).astype(np.float32),
        "w2": (n((H, H)) / np.sqrt(H) / u[:, None] * u).astype(np.float32),
        "res": (2 * n((N, S))).astype(np.float32),
        "w3_words": packed_w3[0],
        "w3_scales": packed_w3[1],
        "offs": striped(np.random.permutation(T)[:S]),
        "p1": striped8(np.stack([np.random.permutation(S) for _ in range(8)])),
        "p2": striped8(np.stack([np.random.permutation(S) for _ in range(8)])),
    }


def reference(x_words, x_scales, w1, eps, w2, res, w3_words, w3_scales, offs, p1, p2):
    xq = unpack_weight(x_words, x_scales)[:, unstriped(offs)]
    y = mxq(f64(w1), 0, "e4m3").T @ xq
    z = f64(eps) * y + y[np.arange(H)[:, None], runs(p1, H)] + y[np.arange(H)[:, None], runs(p2, H)]
    h = gelu(mxq(f64(w2), 0, "e4m3").T @ mxq(z, 0, "e4m3"))
    out_0 = f64(res) + (unpack_fp4(w3_words, w3_scales).T @ mxq(h, 0, "e4m3"))
    return (out_0,) + planes(out_0)

@@ -1,0 +1,220 @@
+from contextlib import ExitStack
+
+import concourse.mybir as mybir
+
+F32 = mybir.dt.float32
+BF16 = mybir.dt.bfloat16
+I32 = mybir.dt.int32
+U32 = mybir.dt.uint32
+U16 = mybir.dt.uint16
+U8 = mybir.dt.uint8
+FP8X4 = mybir.dt.float8_e4m3fn_x4
+FP4X4 = mybir.dt.float4_e2m1fn_x4
+ADD = mybir.AluOpType.add
+COPY = mybir.ActivationFunctionType.Copy
+GELU = mybir.ActivationFunctionType.Gelu_apprx_tanh
+
+P = 128
+PACK = 4
+T = 2048
+S = 512
+D = 512
+STRIPE = 16
+BLOCK = 128
+HALVES = ((0, S // 2), (S // 2, S // 2))
+
+FLOPS = 3 * 2 * D * D * S
+
+
+def tile_picked_gin8_gelu_po_kernel(tc, x_words, x_scales, w1, eps, w2, res, w3_words, w3_scales, offs, p1, p2, out_0, out_1, out_2):
+    nc = tc.nc
+    with ExitStack() as ctx:
+        keep = ctx.enter_context(tc.tile_pool(name="keep", bufs=1))
+        psum = ctx.enter_context(tc.psum_pool(name="psum", bufs=1))
+
+        def load_scale_rows(queue, plane, rows):
+            for q in range(4):
+                queue.dma_start(out=plane[32 * q : 32 * q + 4, :].bitcast(I32), in_=rows[4 * q : 4 * q + 4, :].bitcast(I32))
+
+        def deal(tile_bf16):
+            return tile_bf16[:].rearrange("p (t m j) -> p m j t", t=PACK, j=PACK)
+
+        def dealt_source(raw):
+            return raw[:].rearrange("p j (m t) -> p m j t", t=PACK)
+
+        offs_t = keep.tile([P, S // STRIPE], U16, name="offs_t")
+        p1_t = keep.tile([P, S // STRIPE], U16, name="p1_t")
+        p2_t = keep.tile([P, S // STRIPE], U16, name="p2_t")
+        xs_all = keep.tile([P, T], U8, name="xs_all", tag="xs_all", align_bytes=64)
+        warm_in = keep.tile([P, 1], F32, name="warm_in", tag="warm_in", align_bytes=64)
+        warm_out = keep.tile([P, 1], F32, name="warm_out", tag="warm_out", align_bytes=64)
+        w1_raw = keep.tile([P, PACK, D], F32, name="w1_raw", tag="w_raw")
+        xw_all = keep.tile([P, T], U32, name="xw_all", tag="xw_all", align_bytes=64)
+
+        nc.vector.memset(xs_all[:].bitcast(I32), 0)
+        nc.vector.memset(warm_in[:], 0.0)
+
+        nc.sync.dma_start(offs_t[:], offs)
+        nc.sync.dma_start(out=w1_raw[:], in_=w1.rearrange("(p j) c -> p j c", j=PACK))
+        nc.sync.dma_start(out=xw_all[:].bitcast(I32), in_=x_words[0].rearrange("p n t -> p (n t)").bitcast(I32))
+        nc.sync.dma_start(p1_t[:], p1)
+        nc.sync.dma_start(p2_t[:], p2)
+        load_scale_rows(nc.scalar, xs_all, x_scales[0])
+        nc.scalar.activation(out=warm_out[:], in_=warm_in[:], func=GELU)
+
+        eps_t = keep.tile([P, PACK], F32, name="eps_t", tag="warm_in", align_bytes=64)
+        nc.scalar.dma_start(out=eps_t[:], in_=eps.rearrange("(p t) o -> p (t o)", t=PACK))
+        w3s_raw = keep.tile([P, D], U8, name="w3s_raw", tag="warm_out", align_bytes=64)
+        nc.gpsimd.memset(w3s_raw[:].bitcast(I32), 0)
+        load_scale_rows(nc.scalar, w3s_raw, w3_scales[0])
+
+        xs = keep.tile([P, S], U8, name="xs", align_bytes=64)
+        nc.vector.tensor_copy(out=xs[:], in_=xs_all[:].indirect(offs_t[:]))
+        w3w_raw = keep.tile([P, 2 * D], U8, name="w3w_raw", tag="xs_all", align_bytes=64)
+        nc.sync.dma_start(out=w3w_raw[:].bitcast(I32), in_=w3_words[0].bitcast(I32))
+
+        w1_bf = keep.tile([P, PACK * D], BF16, name="w1_bf", tag="w1_bf", align_bytes=64)
+        nc.vector.tensor_copy(out=deal(w1_bf), in_=dealt_source(w1_raw))
+        w1_c = keep.tile([P, D], U32, name="w1_c", align_bytes=64)
+        w1_s = keep.tile([P, D], U8, name="w1_s", align_bytes=64)
+        nc.vector.quantize_mx(out=w1_c[:].bitcast(FP8X4), scales=w1_s[:], in_=w1_bf[:])
+
+        w2_raw = keep.tile([P, PACK, D], F32, name="w2_raw", tag="w_raw")
+        nc.sync.dma_start(out=w2_raw[:], in_=w2.rearrange("(p j) c -> p j c", j=PACK))
+        res_t = keep.tile([P, PACK, S], F32, name="res_t", tag="w1_bf", align_bytes=64)
+        nc.sync.dma_start(out=res_t[:], in_=res.rearrange("(p t) j -> p t j", t=PACK))
+
+        xw = keep.tile([P, S], U32, name="xw", align_bytes=64)
+        for j0, n in HALVES:
+            nc.vector.tensor_copy(out=xw[:, j0 : j0 + n], in_=xw_all[:].indirect(offs_t[:, j0 // STRIPE : (j0 + n) // STRIPE]))
+
+        w3w = keep.tile([P, 2 * D], U8, name="w3w", tag="xw_all", align_bytes=64)
+        nc.vector.tensor_copy(
+            out=w3w[:].rearrange("p (t m e) -> p t m e", t=PACK, e=2),
+            in_=w3w_raw[:].rearrange("p (m t e) -> p t m e", t=PACK, e=2),
+        )
+        w3s = keep.tile([P, D], U8, name="w3s", tag="xs_all", align_bytes=64)
+        nc.vector.tensor_copy(
+            out=w3s[:].rearrange("p (t m) -> p t m", t=PACK),
+            in_=w3s_raw[:].rearrange("p (m t) -> p t m", t=PACK),
+        )
+
+        def product(out, lhs_c, lhs_s, rhs_c, rhs_s):
+            nc.tensor.matmul_mx(out=out, lhsT=lhs_c, lhsT_scale=lhs_s, rhs=rhs_c.bitcast(FP8X4), rhs_scale=rhs_s, start=True, stop=True)
+
+        def bank(name, number, shape):
+            return psum.tile(shape, F32, name=name, tag="bank%d" % number)
+
+        first = [bank("y0_%d" % u, u, [P, S // 2]) for u in range(2)]
+        y_ps = [[first[0][:], first[1][:]]]
+        for u, (j0, n) in enumerate(HALVES):
+            product(first[u][:], w1_c[:, :P].bitcast(FP8X4), w1_s[:, :P], xw[:, j0 : j0 + n], xs[:, j0 : j0 + n])
+        whole = [None]
+        for t in range(1, PACK):
+            cols = slice(t * P, (t + 1) * P)
+            whole.append(bank("y%d_ps" % t, t + 1, [P, S]))
+            product(whole[t][:], w1_c[:, cols].bitcast(FP8X4), w1_s[:, cols], xw[:], xs[:])
+            y_ps.append([whole[t][:, j0 : j0 + n] for j0, n in HALVES])
+
+        y = [keep.tile([P, S], F32, name="y%d" % t) for t in range(PACK)]
+        ey = [[keep.tile([P, S // 2], F32, name="ey%d_%d" % (u, t)) for t in range(PACK)] for u in range(2)]
+
+        def scale_own(u, t):
+            nc.scalar.activation(out=ey[u][t][:], in_=y_ps[t][u], func=COPY, scale=eps_t[:, t : t + 1])
+
+        nc.scalar.copy(out=y[0][:, : S // 2], in_=y_ps[0][0])
+        scale_own(0, 0)
+        nc.scalar.copy(out=y[0][:, S // 2 :], in_=y_ps[0][1])
+        for t in range(1, PACK):
+            nc.scalar.copy(out=y[t][:], in_=whole[t][:])
+            scale_own(0, t)
+        for t in range(PACK):
+            scale_own(1, t)
+
+        w2_bf = keep.tile([P, PACK * D], BF16, name="w2_bf", tag="warm_in", align_bytes=64)
+        nc.scalar.copy(out=deal(w2_bf), in_=dealt_source(w2_raw))
+        w2_c = keep.tile([P, D], U32, name="w2_c", align_bytes=64)
+        w2_s = keep.tile([P, D], U8, name="w2_s", align_bytes=64)
+
+        out_c = keep.tile([P, S], U32, name="out_c", align_bytes=64)
+        out_s = keep.tile([P, S], U8, name="out_s", align_bytes=64)
+        out_rows = out_0.rearrange("(p t) j -> p t j", t=PACK)
+        out_words = out_1[0].rearrange("p n t -> p (n t)").bitcast(I32)
+
+        def interleave(copy, dst, src):
+            copy(out=dst.rearrange("p (c i t) -> p c t i", t=PACK, i=4), in_=src.rearrange("p t (c i) -> p c t i", i=4))
+
+        def gather_pair(z, j0, n, pair, tag):
+            lists = slice(j0 // STRIPE, (j0 + n) // STRIPE)
+            u, at = divmod(j0, S // 2)
+            part = keep.tile([P, 2, n], F32, name="part%d_%d" % (j0, pair), tag=tag, align_bytes=64)
+            for e in range(2):
+                t = pair + e
+                nc.vector.tensor_tensor(part[:, e, :], y[t][:].indirect(p1_t[:, lists]), ey[u][t][:, at : at + n], ADD)
+            for e in range(2):
+                t = pair + e
+                nc.vector.tensor_tensor(z[:, t, :], y[t][:].indirect(p2_t[:, lists]), part[:, e, :], ADD)
+
+        def gather(j0, n, tags):
+            z = keep.tile([P, PACK, n], F32, name="z%d" % j0)
+            for pair in (0, 2):
+                gather_pair(z, j0, n, pair, tags[pair // 2])
+            return z
+
+        def quantize(name, width, src):
+            codes = keep.tile([P, width], U32, name=name + "_c", align_bytes=64)
+            scales = keep.tile([P, width], U8, name=name + "_s", align_bytes=64)
+            nc.vector.quantize_mx(out=codes[:].bitcast(FP8X4), scales=scales[:], in_=src)
+            return codes, scales
+
+        def quantize_z(copy, j0, n, z):
+            z_bf = keep.tile([P, PACK * n], BF16, name="z_bf%d" % j0, tag="z_bf%d" % j0, align_bytes=64)
+            interleave(copy, z_bf[:], z[:])
+            return quantize("z%d" % j0, n, z_bf[:])
+
+        H_BANKS = (5, 6, 0, 1)
+        O_BANKS = (7, 2, 3, 4)
+
+        def hidden(b, z_c, z_s):
+            h_ps = bank("h_ps%d" % b, H_BANKS[b], [P, PACK, BLOCK])
+            for t in range(PACK):
+                cols = slice(t * P, (t + 1) * P)
+                product(h_ps[:, t, :], w2_c[:, cols].bitcast(FP8X4), w2_s[:, cols], z_c, z_s)
+            h_bf = keep.tile([P, BLOCK, PACK], BF16, name="h_bf%d" % b, align_bytes=64)
+            nc.scalar.activation(out=h_bf[:], in_=h_ps[:].rearrange("p t j -> p j t"), func=GELU)
+            return h_bf
+
+        def result(b, h_bf, copy):
+            cols_b = slice(b * BLOCK, (b + 1) * BLOCK)
+            h_c, h_s = quantize("h%d" % b, BLOCK, h_bf[:].rearrange("p j t -> p (j t)"))
+            o_ps = bank("o_ps%d" % b, O_BANKS[b], [P, PACK, BLOCK])
+            for t in range(PACK):
+                product(o_ps[:, t, :], w3w[:, 2 * t * P : 2 * (t + 1) * P].bitcast(FP4X4), w3s[:, t * P : (t + 1) * P], h_c[:], h_s[:])
+            o = keep.tile([P, PACK, BLOCK], F32, name="o%d" % b)
+            nc.vector.tensor_tensor(o[:], o_ps[:], res_t[:, :, cols_b], ADD)
+            nc.sync.dma_start(out=out_rows[:, :, cols_b], in_=o[:])
+            o_bf = keep.tile([P, PACK * BLOCK], BF16, name="o_bf%d" % b, align_bytes=64)
+            interleave(copy, o_bf[:], o[:])
+            nc.vector.quantize_mx(out=out_c[:, cols_b].bitcast(FP8X4), scales=out_s[:, cols_b], in_=o_bf[:])
+
+        z01 = gather(0, 2 * BLOCK, ("part_a", "part_b"))
+        z2 = gather(2 * BLOCK, BLOCK, ("part_c", "part_d"))
+        nc.vector.quantize_mx(out=w2_c[:].bitcast(FP8X4), scales=w2_s[:], in_=w2_bf[:])
+        z01_c, z01_s = quantize_z(nc.scalar.copy, 0, 2 * BLOCK, z01)
+        z2_c, z2_s = quantize_z(nc.scalar.copy, 2 * BLOCK, BLOCK, z2)
+        z3 = gather(3 * BLOCK, BLOCK, ("z_bf0", "z_bf%d" % (2 * BLOCK)))
+        h_bf = [hidden(b, z01_c[:, b * BLOCK : (b + 1) * BLOCK], z01_s[:, b * BLOCK : (b + 1) * BLOCK]) for b in range(2)]
+        h_bf.append(hidden(2, z2_c[:], z2_s[:]))
+        z3_c, z3_s = quantize_z(nc.vector.tensor_copy, 3 * BLOCK, BLOCK, z3)
+        result(0, h_bf[0], nc.scalar.copy)
+        h_bf.append(hidden(3, z3_c[:], z3_s[:]))
+        result(1, h_bf[1], nc.scalar.copy)
+        result(2, h_bf[2], nc.scalar.copy)
+        result(3, h_bf[3], nc.vector.tensor_copy)
+
+        last = S - BLOCK
+        nc.sync.dma_start(out=out_words[:, :last], in_=out_c[:, :last].bitcast(I32))
+        nc.sync.dma_start(out=out_words[:, last:], in_=out_c[:, last:].bitcast(I32))
+        for q in range(4):
+            queue = nc.scalar if q % 2 else nc.sync
+            queue.dma_start(out=out_2[0][4 * q : 4 * q + 4, :].bitcast(I32), in_=out_s[32 * q : 32 * q + 4, :].bitcast(I32))

@@ -21,6 +21,7 @@ S = 512
 D = 512
 STRIPE = 16
 BLOCK = 128
+SPLIT = 40
 HALVES = ((0, S // 2), (S // 2, S // 2))
 
 FLOPS = 3 * 2 * D * D * S
@@ -46,42 +47,44 @@ def tile_picked_gin8_gelu_po_kernel(tc, x_words, x_scales, w1, eps, w2, res, w3_
         p1_t = keep.tile([P, S // STRIPE], U16, name="p1_t")
         p2_t = keep.tile([P, S // STRIPE], U16, name="p2_t")
         xs_all = keep.tile([P, T], U8, name="xs_all", tag="xs_all", align_bytes=64)
-        warm_in = keep.tile([P, 1], F32, name="warm_in", tag="warm_in", align_bytes=64)
-        warm_out = keep.tile([P, 1], F32, name="warm_out", tag="warm_out", align_bytes=64)
-        w1_raw = keep.tile([P, PACK, D], F32, name="w1_raw", tag="w_raw")
+        w3s_raw = keep.tile([P, D], U8, name="w3s_raw", align_bytes=64)
+        w3w_raw = keep.tile([P, 2 * D], U8, name="w3w_raw", tag="w3w_raw", align_bytes=64)
+        warm_in = keep.tile([P, 1], F32, name="warm_in")
+        warm_out = keep.tile([P, 1], F32, name="warm_out")
+        eps_t = keep.tile([P, PACK], F32, name="eps_t", tag="eps", align_bytes=64)
+        w1_raw = keep.tile([P, PACK, D], F32, name="w1_raw", tag="w_raw", align_bytes=64)
         xw_all = keep.tile([P, T], U32, name="xw_all", tag="xw_all", align_bytes=64)
 
         nc.vector.memset(xs_all[:].bitcast(I32), 0)
         nc.vector.memset(warm_in[:], 0.0)
+        nc.vector.memset(w3s_raw[:].bitcast(I32), 0)
+        nc.scalar.activation(out=warm_out[:], in_=warm_in[:], func=GELU)
 
+        w1_rows = w1.rearrange("(p j) c -> p j c", j=PACK)
         nc.sync.dma_start(offs_t[:], offs)
-        nc.sync.dma_start(out=w1_raw[:], in_=w1.rearrange("(p j) c -> p j c", j=PACK))
+        nc.sync.dma_start(out=w1_raw[:, :2, :], in_=w1_rows[:, :2, :])
+        load_scale_rows(nc.sync, xs_all, x_scales[0])
+        nc.sync.dma_start(out=w1_raw[:, 2:, :], in_=w1_rows[:, 2:, :])
         nc.sync.dma_start(out=xw_all[:].bitcast(I32), in_=x_words[0].rearrange("p n t -> p (n t)").bitcast(I32))
         nc.sync.dma_start(p1_t[:], p1)
         nc.sync.dma_start(p2_t[:], p2)
-        load_scale_rows(nc.scalar, xs_all, x_scales[0])
-        nc.scalar.activation(out=warm_out[:], in_=warm_in[:], func=GELU)
-
-        eps_t = keep.tile([P, PACK], F32, name="eps_t", tag="warm_in", align_bytes=64)
         nc.scalar.dma_start(out=eps_t[:], in_=eps.rearrange("(p t) o -> p (t o)", t=PACK))
-        w3s_raw = keep.tile([P, D], U8, name="w3s_raw", tag="warm_out", align_bytes=64)
-        nc.gpsimd.memset(w3s_raw[:].bitcast(I32), 0)
-        load_scale_rows(nc.scalar, w3s_raw, w3_scales[0])
+        nc.sync.dma_start(out=w3w_raw[:].bitcast(I32), in_=w3_words[0].bitcast(I32))
+        load_scale_rows(nc.sync, w3s_raw, w3_scales[0])
 
         xs = keep.tile([P, S], U8, name="xs", align_bytes=64)
         nc.vector.tensor_copy(out=xs[:], in_=xs_all[:].indirect(offs_t[:]))
-        w3w_raw = keep.tile([P, 2 * D], U8, name="w3w_raw", tag="xs_all", align_bytes=64)
-        nc.sync.dma_start(out=w3w_raw[:].bitcast(I32), in_=w3_words[0].bitcast(I32))
 
-        w1_bf = keep.tile([P, PACK * D], BF16, name="w1_bf", tag="w1_bf", align_bytes=64)
-        nc.vector.tensor_copy(out=deal(w1_bf), in_=dealt_source(w1_raw))
+        w1_bf = keep.tile([P, PACK * D], BF16, name="w1_bf", tag="xs_all", align_bytes=64)
+        nc.vector.tensor_copy(out=deal(w1_bf)[:, SPLIT:], in_=dealt_source(w1_raw)[:, SPLIT:])
+        nc.scalar.copy(out=deal(w1_bf)[:, :SPLIT], in_=dealt_source(w1_raw)[:, :SPLIT])
         w1_c = keep.tile([P, D], U32, name="w1_c", align_bytes=64)
         w1_s = keep.tile([P, D], U8, name="w1_s", align_bytes=64)
         nc.vector.quantize_mx(out=w1_c[:].bitcast(FP8X4), scales=w1_s[:], in_=w1_bf[:])
 
-        w2_raw = keep.tile([P, PACK, D], F32, name="w2_raw", tag="w_raw")
+        w2_raw = keep.tile([P, PACK, D], F32, name="w2_raw", tag="w_raw", align_bytes=64)
         nc.sync.dma_start(out=w2_raw[:], in_=w2.rearrange("(p j) c -> p j c", j=PACK))
-        res_t = keep.tile([P, PACK, S], F32, name="res_t", tag="w1_bf", align_bytes=64)
+        res_t = keep.tile([P, PACK, S], F32, name="res_t", tag="xs_all", align_bytes=64)
         nc.sync.dma_start(out=res_t[:], in_=res.rearrange("(p t) j -> p t j", t=PACK))
 
         xw = keep.tile([P, S], U32, name="xw", align_bytes=64)
@@ -93,7 +96,8 @@ def tile_picked_gin8_gelu_po_kernel(tc, x_words, x_scales, w1, eps, w2, res, w3_
             out=w3w[:].rearrange("p (t m e) -> p t m e", t=PACK, e=2),
             in_=w3w_raw[:].rearrange("p (m t e) -> p t m e", t=PACK, e=2),
         )
-        w3s = keep.tile([P, D], U8, name="w3s", tag="xs_all", align_bytes=64)
+
+        w3s = keep.tile([P, D], U8, name="w3s", tag="w3w_raw", align_bytes=64)
         nc.vector.tensor_copy(
             out=w3s[:].rearrange("p (t m) -> p t m", t=PACK),
             in_=w3s_raw[:].rearrange("p (m t) -> p t m", t=PACK),
@@ -116,7 +120,7 @@ def tile_picked_gin8_gelu_po_kernel(tc, x_words, x_scales, w1, eps, w2, res, w3_
             product(whole[t][:], w1_c[:, cols].bitcast(FP8X4), w1_s[:, cols], xw[:], xs[:])
             y_ps.append([whole[t][:, j0 : j0 + n] for j0, n in HALVES])
 
-        y = [keep.tile([P, S], F32, name="y%d" % t) for t in range(PACK)]
+        y = [keep.tile([P, S], F32, name="y%d" % t, tag="y%d" % t, align_bytes=64) for t in range(PACK)]
         ey = [[keep.tile([P, S // 2], F32, name="ey%d_%d" % (u, t)) for t in range(PACK)] for u in range(2)]
 
         def scale_own(u, t):
@@ -131,7 +135,7 @@ def tile_picked_gin8_gelu_po_kernel(tc, x_words, x_scales, w1, eps, w2, res, w3_
         for t in range(PACK):
             scale_own(1, t)
 
-        w2_bf = keep.tile([P, PACK * D], BF16, name="w2_bf", tag="warm_in", align_bytes=64)
+        w2_bf = keep.tile([P, PACK * D], BF16, name="w2_bf", tag="eps", align_bytes=64)
         nc.scalar.copy(out=deal(w2_bf), in_=dealt_source(w2_raw))
         w2_c = keep.tile([P, D], U32, name="w2_c", align_bytes=64)
         w2_s = keep.tile([P, D], U8, name="w2_s", align_bytes=64)
@@ -144,10 +148,9 @@ def tile_picked_gin8_gelu_po_kernel(tc, x_words, x_scales, w1, eps, w2, res, w3_
         def interleave(copy, dst, src):
             copy(out=dst.rearrange("p (c i t) -> p c t i", t=PACK, i=4), in_=src.rearrange("p t (c i) -> p c t i", i=4))
 
-        def gather_pair(z, j0, n, pair, tag):
+        def gather_pair(z, j0, n, pair, part):
             lists = slice(j0 // STRIPE, (j0 + n) // STRIPE)
             u, at = divmod(j0, S // 2)
-            part = keep.tile([P, 2, n], F32, name="part%d_%d" % (j0, pair), tag=tag, align_bytes=64)
             for e in range(2):
                 t = pair + e
                 nc.vector.tensor_tensor(part[:, e, :], y[t][:].indirect(p1_t[:, lists]), ey[u][t][:, at : at + n], ADD)
@@ -155,22 +158,28 @@ def tile_picked_gin8_gelu_po_kernel(tc, x_words, x_scales, w1, eps, w2, res, w3_
                 t = pair + e
                 nc.vector.tensor_tensor(z[:, t, :], y[t][:].indirect(p2_t[:, lists]), part[:, e, :], ADD)
 
-        def gather(j0, n, tags):
-            z = keep.tile([P, PACK, n], F32, name="z%d" % j0)
+        def scratch(name, n):
+            return keep.tile([P, 2, n], F32, name=name)[:]
+
+        def reuse(z_bf):
+            return z_bf[:, : PACK * BLOCK].bitcast(F32).rearrange("p (e j) -> p e j", e=2)
+
+        def gather(j0, n, parts):
+            z = keep.tile([P, PACK, n], F32, name="z%d" % j0, tag="z%d" % j0, align_bytes=64)
             for pair in (0, 2):
-                gather_pair(z, j0, n, pair, tags[pair // 2])
+                gather_pair(z, j0, n, pair, parts[pair // 2])
             return z
 
-        def quantize(name, width, src):
-            codes = keep.tile([P, width], U32, name=name + "_c", align_bytes=64)
+        def quantize(name, width, src, tag=None):
+            codes = keep.tile([P, width], U32, name=name + "_c", tag=tag or name + "_c", align_bytes=64)
             scales = keep.tile([P, width], U8, name=name + "_s", align_bytes=64)
             nc.vector.quantize_mx(out=codes[:].bitcast(FP8X4), scales=scales[:], in_=src)
             return codes, scales
 
-        def quantize_z(copy, j0, n, z):
-            z_bf = keep.tile([P, PACK * n], BF16, name="z_bf%d" % j0, tag="z_bf%d" % j0, align_bytes=64)
+        def quantize_z(copy, j0, n, z, tag, codes_tag=None):
+            z_bf = keep.tile([P, PACK * n], BF16, name="z_bf%d" % j0, tag=tag, align_bytes=64)
             interleave(copy, z_bf[:], z[:])
-            return quantize("z%d" % j0, n, z_bf[:])
+            return quantize("z%d" % j0, n, z_bf[:], codes_tag) + (z_bf,)
 
         H_BANKS = (5, 6, 0, 1)
         O_BANKS = (7, 2, 3, 4)
@@ -186,7 +195,7 @@ def tile_picked_gin8_gelu_po_kernel(tc, x_words, x_scales, w1, eps, w2, res, w3_
 
         def result(b, h_bf, copy):
             cols_b = slice(b * BLOCK, (b + 1) * BLOCK)
-            h_c, h_s = quantize("h%d" % b, BLOCK, h_bf[:].rearrange("p j t -> p (j t)"))
+            h_c, h_s = quantize("h%d" % b, BLOCK, h_bf[:].rearrange("p j t -> p (j t)"), "y3" if b == 0 else None)
             o_ps = bank("o_ps%d" % b, O_BANKS[b], [P, PACK, BLOCK])
             for t in range(PACK):
                 product(o_ps[:, t, :], w3w[:, 2 * t * P : 2 * (t + 1) * P].bitcast(FP4X4), w3s[:, t * P : (t + 1) * P], h_c[:], h_s[:])
@@ -197,15 +206,15 @@ def tile_picked_gin8_gelu_po_kernel(tc, x_words, x_scales, w1, eps, w2, res, w3_
             interleave(copy, o_bf[:], o[:])
             nc.vector.quantize_mx(out=out_c[:, cols_b].bitcast(FP8X4), scales=out_s[:, cols_b], in_=o_bf[:])
 
-        z01 = gather(0, 2 * BLOCK, ("part_a", "part_b"))
-        z2 = gather(2 * BLOCK, BLOCK, ("part_c", "part_d"))
+        z01 = gather(0, 2 * BLOCK, (scratch("part_a", 2 * BLOCK), scratch("part_b", 2 * BLOCK)))
+        z2 = gather(2 * BLOCK, BLOCK, (scratch("part_c", BLOCK), scratch("part_d", BLOCK)))
         nc.vector.quantize_mx(out=w2_c[:].bitcast(FP8X4), scales=w2_s[:], in_=w2_bf[:])
-        z01_c, z01_s = quantize_z(nc.scalar.copy, 0, 2 * BLOCK, z01)
-        z2_c, z2_s = quantize_z(nc.scalar.copy, 2 * BLOCK, BLOCK, z2)
-        z3 = gather(3 * BLOCK, BLOCK, ("z_bf0", "z_bf%d" % (2 * BLOCK)))
+        z01_c, z01_s, z01_bf = quantize_z(nc.scalar.copy, 0, 2 * BLOCK, z01, "w_raw", "eps")
+        z2_c, z2_s, z2_bf = quantize_z(nc.scalar.copy, 2 * BLOCK, BLOCK, z2, "z0")
+        z3 = gather(3 * BLOCK, BLOCK, (reuse(z2_bf), z2[:, :2, :]))
         h_bf = [hidden(b, z01_c[:, b * BLOCK : (b + 1) * BLOCK], z01_s[:, b * BLOCK : (b + 1) * BLOCK]) for b in range(2)]
         h_bf.append(hidden(2, z2_c[:], z2_s[:]))
-        z3_c, z3_s = quantize_z(nc.vector.tensor_copy, 3 * BLOCK, BLOCK, z3)
+        z3_c, z3_s, z3_bf = quantize_z(nc.vector.tensor_copy, 3 * BLOCK, BLOCK, z3, "z_bf3")
         result(0, h_bf[0], nc.scalar.copy)
         h_bf.append(hidden(3, z3_c[:], z3_s[:]))
         result(1, h_bf[1], nc.scalar.copy)

@@ -20,9 +20,13 @@ T = 2048
 S = 512
 D = 512
 STRIPE = 16
+QUADS = 4
+LINE = 4
 BLOCK = 128
 SPLIT = 40
 HALVES = ((0, S // 2), (S // 2, S // 2))
+H_BANKS = (5, 6, 0, 1)
+O_BANKS = (7, 2, 3, 4)
 
 FLOPS = 3 * 2 * D * D * S
 
@@ -33,15 +37,15 @@ def tile_picked_gin8_gelu_po_kernel(tc, x_words, x_scales, w1, eps, w2, res, w3_
         keep = ctx.enter_context(tc.tile_pool(name="keep", bufs=1))
         psum = ctx.enter_context(tc.psum_pool(name="psum", bufs=1))
 
-        def load_scale_rows(queue, plane, rows):
-            for q in range(4):
-                queue.dma_start(out=plane[32 * q : 32 * q + 4, :].bitcast(I32), in_=rows[4 * q : 4 * q + 4, :].bitcast(I32))
+        def load_scale_rows(scale_tile, rows):
+            for q in range(QUADS):
+                nc.sync.dma_start(out=scale_tile[32 * q : 32 * q + 4, :].bitcast(I32), in_=rows[4 * q : 4 * q + 4, :].bitcast(I32))
 
-        def deal(tile_bf16):
-            return tile_bf16[:].rearrange("p (t m j) -> p m j t", t=PACK, j=PACK)
+        def dealt_view(w_bf):
+            return w_bf[:].rearrange("p (t m j) -> p m j t", t=PACK, j=PACK)
 
-        def dealt_source(raw):
-            return raw[:].rearrange("p j (m t) -> p m j t", t=PACK)
+        def raw_view(w_raw):
+            return w_raw[:].rearrange("p j (m t) -> p m j t", t=PACK)
 
         offs_t = keep.tile([P, S // STRIPE], U16, name="offs_t")
         p1_t = keep.tile([P, S // STRIPE], U16, name="p1_t")
@@ -49,35 +53,31 @@ def tile_picked_gin8_gelu_po_kernel(tc, x_words, x_scales, w1, eps, w2, res, w3_
         xs_all = keep.tile([P, T], U8, name="xs_all", tag="xs_all", align_bytes=64)
         w3s_raw = keep.tile([P, D], U8, name="w3s_raw", align_bytes=64)
         w3w_raw = keep.tile([P, 2 * D], U8, name="w3w_raw", tag="w3w_raw", align_bytes=64)
-        warm_in = keep.tile([P, 1], F32, name="warm_in")
-        warm_out = keep.tile([P, 1], F32, name="warm_out")
         eps_t = keep.tile([P, PACK], F32, name="eps_t", tag="eps", align_bytes=64)
         w1_raw = keep.tile([P, PACK, D], F32, name="w1_raw", tag="w_raw", align_bytes=64)
         xw_all = keep.tile([P, T], U32, name="xw_all", tag="xw_all", align_bytes=64)
 
         nc.vector.memset(xs_all[:].bitcast(I32), 0)
-        nc.vector.memset(warm_in[:], 0.0)
         nc.vector.memset(w3s_raw[:].bitcast(I32), 0)
-        nc.scalar.activation(out=warm_out[:], in_=warm_in[:], func=GELU)
 
         w1_rows = w1.rearrange("(p j) c -> p j c", j=PACK)
         nc.sync.dma_start(offs_t[:], offs)
         nc.sync.dma_start(out=w1_raw[:, :2, :], in_=w1_rows[:, :2, :])
-        load_scale_rows(nc.sync, xs_all, x_scales[0])
+        load_scale_rows(xs_all, x_scales[0])
         nc.sync.dma_start(out=w1_raw[:, 2:, :], in_=w1_rows[:, 2:, :])
         nc.sync.dma_start(out=xw_all[:].bitcast(I32), in_=x_words[0].rearrange("p n t -> p (n t)").bitcast(I32))
         nc.sync.dma_start(p1_t[:], p1)
         nc.sync.dma_start(p2_t[:], p2)
         nc.scalar.dma_start(out=eps_t[:], in_=eps.rearrange("(p t) o -> p (t o)", t=PACK))
         nc.sync.dma_start(out=w3w_raw[:].bitcast(I32), in_=w3_words[0].bitcast(I32))
-        load_scale_rows(nc.sync, w3s_raw, w3_scales[0])
+        load_scale_rows(w3s_raw, w3_scales[0])
 
         xs = keep.tile([P, S], U8, name="xs", align_bytes=64)
         nc.vector.tensor_copy(out=xs[:], in_=xs_all[:].indirect(offs_t[:]))
 
         w1_bf = keep.tile([P, PACK * D], BF16, name="w1_bf", tag="xs_all", align_bytes=64)
-        nc.vector.tensor_copy(out=deal(w1_bf)[:, SPLIT:], in_=dealt_source(w1_raw)[:, SPLIT:])
-        nc.scalar.copy(out=deal(w1_bf)[:, :SPLIT], in_=dealt_source(w1_raw)[:, :SPLIT])
+        nc.vector.tensor_copy(out=dealt_view(w1_bf)[:, SPLIT:], in_=raw_view(w1_raw)[:, SPLIT:])
+        nc.scalar.copy(out=dealt_view(w1_bf)[:, :SPLIT], in_=raw_view(w1_raw)[:, :SPLIT])
         w1_c = keep.tile([P, D], U32, name="w1_c", align_bytes=64)
         w1_s = keep.tile([P, D], U8, name="w1_s", align_bytes=64)
         nc.vector.quantize_mx(out=w1_c[:].bitcast(FP8X4), scales=w1_s[:], in_=w1_bf[:])
@@ -96,7 +96,6 @@ def tile_picked_gin8_gelu_po_kernel(tc, x_words, x_scales, w1, eps, w2, res, w3_
             out=w3w[:].rearrange("p (t m e) -> p t m e", t=PACK, e=2),
             in_=w3w_raw[:].rearrange("p (m t e) -> p t m e", t=PACK, e=2),
         )
-
         w3s = keep.tile([P, D], U8, name="w3s", tag="w3w_raw", align_bytes=64)
         nc.vector.tensor_copy(
             out=w3s[:].rearrange("p (t m) -> p t m", t=PACK),
@@ -109,16 +108,16 @@ def tile_picked_gin8_gelu_po_kernel(tc, x_words, x_scales, w1, eps, w2, res, w3_
         def bank(name, number, shape):
             return psum.tile(shape, F32, name=name, tag="bank%d" % number)
 
-        first = [bank("y0_%d" % u, u, [P, S // 2]) for u in range(2)]
-        y_ps = [[first[0][:], first[1][:]]]
+        plane0_ps = [bank("y0_%d" % u, u, [P, S // 2]) for u in range(2)]
+        y_ps = [[plane0_ps[0][:], plane0_ps[1][:]]]
         for u, (j0, n) in enumerate(HALVES):
-            product(first[u][:], w1_c[:, :P].bitcast(FP8X4), w1_s[:, :P], xw[:, j0 : j0 + n], xs[:, j0 : j0 + n])
-        whole = [None]
+            product(plane0_ps[u][:], w1_c[:, :P].bitcast(FP8X4), w1_s[:, :P], xw[:, j0 : j0 + n], xs[:, j0 : j0 + n])
+        plane_ps = {}
         for t in range(1, PACK):
-            cols = slice(t * P, (t + 1) * P)
-            whole.append(bank("y%d_ps" % t, t + 1, [P, S]))
-            product(whole[t][:], w1_c[:, cols].bitcast(FP8X4), w1_s[:, cols], xw[:], xs[:])
-            y_ps.append([whole[t][:, j0 : j0 + n] for j0, n in HALVES])
+            places = slice(t * P, (t + 1) * P)
+            plane_ps[t] = bank("y%d_ps" % t, t + 1, [P, S])
+            product(plane_ps[t][:], w1_c[:, places].bitcast(FP8X4), w1_s[:, places], xw[:], xs[:])
+            y_ps.append([plane_ps[t][:, j0 : j0 + n] for j0, n in HALVES])
 
         y = [keep.tile([P, S], F32, name="y%d" % t, tag="y%d" % t, align_bytes=64) for t in range(PACK)]
         ey = [[keep.tile([P, S // 2], F32, name="ey%d_%d" % (u, t)) for t in range(PACK)] for u in range(2)]
@@ -130,13 +129,13 @@ def tile_picked_gin8_gelu_po_kernel(tc, x_words, x_scales, w1, eps, w2, res, w3_
         scale_own(0, 0)
         nc.scalar.copy(out=y[0][:, S // 2 :], in_=y_ps[0][1])
         for t in range(1, PACK):
-            nc.scalar.copy(out=y[t][:], in_=whole[t][:])
+            nc.scalar.copy(out=y[t][:], in_=plane_ps[t][:])
             scale_own(0, t)
         for t in range(PACK):
             scale_own(1, t)
 
         w2_bf = keep.tile([P, PACK * D], BF16, name="w2_bf", tag="eps", align_bytes=64)
-        nc.scalar.copy(out=deal(w2_bf), in_=dealt_source(w2_raw))
+        nc.scalar.copy(out=dealt_view(w2_bf), in_=raw_view(w2_raw))
         w2_c = keep.tile([P, D], U32, name="w2_c", align_bytes=64)
         w2_s = keep.tile([P, D], U8, name="w2_s", align_bytes=64)
 
@@ -146,84 +145,78 @@ def tile_picked_gin8_gelu_po_kernel(tc, x_words, x_scales, w1, eps, w2, res, w3_
         out_words = out_1[0].rearrange("p n t -> p (n t)").bitcast(I32)
 
         def interleave(copy, dst, src):
-            copy(out=dst.rearrange("p (c i t) -> p c t i", t=PACK, i=4), in_=src.rearrange("p t (c i) -> p c t i", i=4))
+            copy(out=dst.rearrange("p (c i t) -> p c t i", t=PACK, i=LINE), in_=src.rearrange("p t (c i) -> p c t i", i=LINE))
 
-        def gather_pair(z, j0, n, pair, part):
-            lists = slice(j0 // STRIPE, (j0 + n) // STRIPE)
-            u, at = divmod(j0, S // 2)
-            for e in range(2):
-                t = pair + e
-                nc.vector.tensor_tensor(part[:, e, :], y[t][:].indirect(p1_t[:, lists]), ey[u][t][:, at : at + n], ADD)
-            for e in range(2):
-                t = pair + e
-                nc.vector.tensor_tensor(z[:, t, :], y[t][:].indirect(p2_t[:, lists]), part[:, e, :], ADD)
-
-        def scratch(name, n):
+        def partial_sums(name, n):
             return keep.tile([P, 2, n], F32, name=name)[:]
 
-        def reuse(z_bf):
-            return z_bf[:, : PACK * BLOCK].bitcast(F32).rearrange("p (e j) -> p e j", e=2)
-
-        def gather(j0, n, parts):
+        def look_up(j0, n, parts):
             z = keep.tile([P, PACK, n], F32, name="z%d" % j0, tag="z%d" % j0, align_bytes=64)
-            for pair in (0, 2):
-                gather_pair(z, j0, n, pair, parts[pair // 2])
+            entries = slice(j0 // STRIPE, (j0 + n) // STRIPE)
+            u, at = divmod(j0, S // 2)
+            for pair, part in enumerate(parts):
+                for e in range(2):
+                    t = 2 * pair + e
+                    nc.vector.tensor_tensor(part[:, e, :], y[t][:].indirect(p1_t[:, entries]), ey[u][t][:, at : at + n], ADD)
+                for e in range(2):
+                    t = 2 * pair + e
+                    nc.vector.tensor_tensor(z[:, t, :], y[t][:].indirect(p2_t[:, entries]), part[:, e, :], ADD)
             return z
 
-        def quantize(name, width, src, tag=None):
-            codes = keep.tile([P, width], U32, name=name + "_c", tag=tag or name + "_c", align_bytes=64)
+        def quantize(name, width, src, codes_tag):
+            codes = keep.tile([P, width], U32, name=name + "_c", tag=codes_tag, align_bytes=64)
             scales = keep.tile([P, width], U8, name=name + "_s", align_bytes=64)
             nc.vector.quantize_mx(out=codes[:].bitcast(FP8X4), scales=scales[:], in_=src)
             return codes, scales
 
-        def quantize_z(copy, j0, n, z, tag, codes_tag=None):
+        def round_z(copy, j0, n, z, tag):
             z_bf = keep.tile([P, PACK * n], BF16, name="z_bf%d" % j0, tag=tag, align_bytes=64)
             interleave(copy, z_bf[:], z[:])
-            return quantize("z%d" % j0, n, z_bf[:], codes_tag) + (z_bf,)
-
-        H_BANKS = (5, 6, 0, 1)
-        O_BANKS = (7, 2, 3, 4)
+            return z_bf
 
         def hidden(b, z_c, z_s):
             h_ps = bank("h_ps%d" % b, H_BANKS[b], [P, PACK, BLOCK])
             for t in range(PACK):
-                cols = slice(t * P, (t + 1) * P)
-                product(h_ps[:, t, :], w2_c[:, cols].bitcast(FP8X4), w2_s[:, cols], z_c, z_s)
+                places = slice(t * P, (t + 1) * P)
+                product(h_ps[:, t, :], w2_c[:, places].bitcast(FP8X4), w2_s[:, places], z_c, z_s)
             h_bf = keep.tile([P, BLOCK, PACK], BF16, name="h_bf%d" % b, align_bytes=64)
             nc.scalar.activation(out=h_bf[:], in_=h_ps[:].rearrange("p t j -> p j t"), func=GELU)
             return h_bf
 
-        def result(b, h_bf, copy):
-            cols_b = slice(b * BLOCK, (b + 1) * BLOCK)
-            h_c, h_s = quantize("h%d" % b, BLOCK, h_bf[:].rearrange("p j t -> p (j t)"), "y3" if b == 0 else None)
+        def result(b, h_bf, copy, codes_tag):
+            nodes = slice(b * BLOCK, (b + 1) * BLOCK)
+            h_c, h_s = quantize("h%d" % b, BLOCK, h_bf[:].rearrange("p j t -> p (j t)"), codes_tag)
             o_ps = bank("o_ps%d" % b, O_BANKS[b], [P, PACK, BLOCK])
             for t in range(PACK):
                 product(o_ps[:, t, :], w3w[:, 2 * t * P : 2 * (t + 1) * P].bitcast(FP4X4), w3s[:, t * P : (t + 1) * P], h_c[:], h_s[:])
             o = keep.tile([P, PACK, BLOCK], F32, name="o%d" % b)
-            nc.vector.tensor_tensor(o[:], o_ps[:], res_t[:, :, cols_b], ADD)
-            nc.sync.dma_start(out=out_rows[:, :, cols_b], in_=o[:])
+            nc.vector.tensor_tensor(o[:], o_ps[:], res_t[:, :, nodes], ADD)
+            nc.sync.dma_start(out=out_rows[:, :, nodes], in_=o[:])
             o_bf = keep.tile([P, PACK * BLOCK], BF16, name="o_bf%d" % b, align_bytes=64)
             interleave(copy, o_bf[:], o[:])
-            nc.vector.quantize_mx(out=out_c[:, cols_b].bitcast(FP8X4), scales=out_s[:, cols_b], in_=o_bf[:])
+            nc.vector.quantize_mx(out=out_c[:, nodes].bitcast(FP8X4), scales=out_s[:, nodes], in_=o_bf[:])
 
-        z01 = gather(0, 2 * BLOCK, (scratch("part_a", 2 * BLOCK), scratch("part_b", 2 * BLOCK)))
-        z2 = gather(2 * BLOCK, BLOCK, (scratch("part_c", BLOCK), scratch("part_d", BLOCK)))
+        z01 = look_up(0, 2 * BLOCK, (partial_sums("part_a", 2 * BLOCK), partial_sums("part_b", 2 * BLOCK)))
+        z2 = look_up(2 * BLOCK, BLOCK, (partial_sums("part_c", BLOCK), partial_sums("part_d", BLOCK)))
         nc.vector.quantize_mx(out=w2_c[:].bitcast(FP8X4), scales=w2_s[:], in_=w2_bf[:])
-        z01_c, z01_s, z01_bf = quantize_z(nc.scalar.copy, 0, 2 * BLOCK, z01, "w_raw", "eps")
-        z2_c, z2_s, z2_bf = quantize_z(nc.scalar.copy, 2 * BLOCK, BLOCK, z2, "z0")
-        z3 = gather(3 * BLOCK, BLOCK, (reuse(z2_bf), z2[:, :2, :]))
+        z01_bf = round_z(nc.scalar.copy, 0, 2 * BLOCK, z01, "w_raw")
+        z01_c, z01_s = quantize("z0", 2 * BLOCK, z01_bf[:], "eps")
+        z2_bf = round_z(nc.scalar.copy, 2 * BLOCK, BLOCK, z2, "z0")
+        z2_c, z2_s = quantize("z256", BLOCK, z2_bf[:], "z256_c")
+        z3 = look_up(3 * BLOCK, BLOCK, (z2_bf[:].bitcast(F32).rearrange("p (e j) -> p e j", e=2), z2[:, :2, :]))
         h_bf = [hidden(b, z01_c[:, b * BLOCK : (b + 1) * BLOCK], z01_s[:, b * BLOCK : (b + 1) * BLOCK]) for b in range(2)]
         h_bf.append(hidden(2, z2_c[:], z2_s[:]))
-        z3_c, z3_s, z3_bf = quantize_z(nc.vector.tensor_copy, 3 * BLOCK, BLOCK, z3, "z_bf3")
-        result(0, h_bf[0], nc.scalar.copy)
+        z3_bf = round_z(nc.vector.tensor_copy, 3 * BLOCK, BLOCK, z3, "z_bf3")
+        z3_c, z3_s = quantize("z384", BLOCK, z3_bf[:], "z384_c")
+        result(0, h_bf[0], nc.scalar.copy, "y3")
         h_bf.append(hidden(3, z3_c[:], z3_s[:]))
-        result(1, h_bf[1], nc.scalar.copy)
-        result(2, h_bf[2], nc.scalar.copy)
-        result(3, h_bf[3], nc.vector.tensor_copy)
+        result(1, h_bf[1], nc.scalar.copy, "h1_c")
+        result(2, h_bf[2], nc.scalar.copy, "h2_c")
+        result(3, h_bf[3], nc.vector.tensor_copy, "h3_c")
 
         last = S - BLOCK
         nc.sync.dma_start(out=out_words[:, :last], in_=out_c[:, :last].bitcast(I32))
         nc.sync.dma_start(out=out_words[:, last:], in_=out_c[:, last:].bitcast(I32))
-        for q in range(4):
+        for q in range(QUADS):
             queue = nc.scalar if q % 2 else nc.sync
             queue.dma_start(out=out_2[0][4 * q : 4 * q + 4, :].bitcast(I32), in_=out_s[32 * q : 32 * q + 4, :].bitcast(I32))

@@ -38,8 +38,11 @@ def tile_picked_gin8_gelu_po_kernel(tc, x_words, x_scales, w1, eps, w2, res, w3_
         psum = ctx.enter_context(tc.psum_pool(name="psum", bufs=1))
 
         def load_scale_rows(scale_tile, rows):
+            nc.sync.dma_start(out=scale_tile[0:P:8, :].bitcast(I32), in_=rows.bitcast(I32))
+
+        def place_scale_rows(queue, scale_tile, spread):
             for q in range(QUADS):
-                nc.sync.dma_start(out=scale_tile[32 * q : 32 * q + 4, :].bitcast(I32), in_=rows[4 * q : 4 * q + 4, :].bitcast(I32))
+                queue.dma_start(out=scale_tile[32 * q : 32 * q + 4, :].bitcast(I32), in_=spread[32 * q : 32 * q + 32 : 8, :].bitcast(I32))
 
         def dealt_view(w_bf):
             return w_bf[:].rearrange("p (t m j) -> p m j t", t=PACK, j=PACK)
@@ -59,23 +62,34 @@ def tile_picked_gin8_gelu_po_kernel(tc, x_words, x_scales, w1, eps, w2, res, w3_
 
         nc.vector.memset(xs_all[:].bitcast(I32), 0)
         nc.vector.memset(w3s_raw[:].bitcast(I32), 0)
+        xs = keep.tile([P, S], U8, name="xs", align_bytes=64)
+        w3s = keep.tile([P, D], U8, name="w3s", align_bytes=64)
+        nc.vector.memset(xs[:].bitcast(I32), 0)
+        nc.vector.memset(w3s[:].bitcast(I32), 0)
 
         w1_rows = w1.rearrange("(p j) c -> p j c", j=PACK)
         nc.sync.dma_start(offs_t[:], offs)
-        nc.sync.dma_start(out=w1_raw[:, :2, :], in_=w1_rows[:, :2, :])
+        nc.scalar.dma_start(out=eps_t[:], in_=eps.rearrange("(p t) o -> p (t o)", t=PACK))
+        nc.sync.dma_start(out=w1_raw[:, :1, :], in_=w1_rows[:, :1, :])
         load_scale_rows(xs_all, x_scales[0])
-        nc.sync.dma_start(out=w1_raw[:, 2:, :], in_=w1_rows[:, 2:, :])
-        nc.sync.dma_start(out=xw_all[:].bitcast(I32), in_=x_words[0].rearrange("p n t -> p (n t)").bitcast(I32))
         nc.sync.dma_start(p1_t[:], p1)
         nc.sync.dma_start(p2_t[:], p2)
-        nc.scalar.dma_start(out=eps_t[:], in_=eps.rearrange("(p t) o -> p (t o)", t=PACK))
+        nc.sync.dma_start(out=w1_raw[:, 1:, :], in_=w1_rows[:, 1:, :])
+        nc.sync.dma_start(out=xw_all[:].bitcast(I32), in_=x_words[0].rearrange("p n t -> p (n t)").bitcast(I32))
         nc.sync.dma_start(out=w3w_raw[:].bitcast(I32), in_=w3_words[0].bitcast(I32))
         load_scale_rows(w3s_raw, w3_scales[0])
 
-        xs = keep.tile([P, S], U8, name="xs", align_bytes=64)
-        nc.vector.tensor_copy(out=xs[:], in_=xs_all[:].indirect(offs_t[:]))
+        xs_spread = keep.tile([P, S], U8, name="xs_spread", align_bytes=64)
+        nc.vector.tensor_copy(out=xs_spread[:], in_=xs_all[:].indirect(offs_t[:]))
+        place_scale_rows(nc.scalar, xs, xs_spread)
+        w3s_spread = keep.tile([P, D], U8, name="w3s_spread", tag="xs_all", align_bytes=64)
+        nc.vector.tensor_copy(
+            out=w3s_spread[:].rearrange("p (t m) -> p t m", t=PACK),
+            in_=w3s_raw[:].rearrange("p (m t) -> p t m", t=PACK),
+        )
+        place_scale_rows(nc.sync, w3s, w3s_spread)
 
-        w1_bf = keep.tile([P, PACK * D], BF16, name="w1_bf", tag="xs_all", align_bytes=64)
+        w1_bf = keep.tile([P, PACK * D], BF16, name="w1_bf", tag="w1_bf", align_bytes=64)
         nc.vector.tensor_copy(out=dealt_view(w1_bf)[:, SPLIT:], in_=raw_view(w1_raw)[:, SPLIT:])
         nc.scalar.copy(out=dealt_view(w1_bf)[:, :SPLIT], in_=raw_view(w1_raw)[:, :SPLIT])
         w1_c = keep.tile([P, D], U32, name="w1_c", align_bytes=64)
@@ -84,7 +98,7 @@ def tile_picked_gin8_gelu_po_kernel(tc, x_words, x_scales, w1, eps, w2, res, w3_
 
         w2_raw = keep.tile([P, PACK, D], F32, name="w2_raw", tag="w_raw", align_bytes=64)
         nc.sync.dma_start(out=w2_raw[:], in_=w2.rearrange("(p j) c -> p j c", j=PACK))
-        res_t = keep.tile([P, PACK, S], F32, name="res_t", tag="xs_all", align_bytes=64)
+        res_t = keep.tile([P, PACK, S], F32, name="res_t", tag="w1_bf", align_bytes=64)
         nc.sync.dma_start(out=res_t[:], in_=res.rearrange("(p t) j -> p t j", t=PACK))
 
         xw = keep.tile([P, S], U32, name="xw", align_bytes=64)
@@ -95,11 +109,6 @@ def tile_picked_gin8_gelu_po_kernel(tc, x_words, x_scales, w1, eps, w2, res, w3_
         nc.vector.tensor_copy(
             out=w3w[:].rearrange("p (t m e) -> p t m e", t=PACK, e=2),
             in_=w3w_raw[:].rearrange("p (m t e) -> p t m e", t=PACK, e=2),
-        )
-        w3s = keep.tile([P, D], U8, name="w3s", tag="w3w_raw", align_bytes=64)
-        nc.vector.tensor_copy(
-            out=w3s[:].rearrange("p (t m) -> p t m", t=PACK),
-            in_=w3s_raw[:].rearrange("p (m t) -> p t m", t=PACK),
         )
 
         def product(out, lhs_c, lhs_s, rhs_c, rhs_s):

@@ -23,10 +23,10 @@ STRIPE = 16
 QUADS = 4
 LINE = 4
 BLOCK = 128
-SPLIT = 40
+SPLIT = 16
 HALVES = ((0, S // 2), (S // 2, S // 2))
 H_BANKS = (5, 6, 0, 1)
-O_BANKS = (7, 2, 3, 4)
+O_BANKS = ((7,), (2,), (3,), (4, 5))
 
 FLOPS = 3 * 2 * D * D * S
 
@@ -38,11 +38,8 @@ def tile_picked_gin8_gelu_po_kernel(tc, x_words, x_scales, w1, eps, w2, res, w3_
         psum = ctx.enter_context(tc.psum_pool(name="psum", bufs=1))
 
         def load_scale_rows(scale_tile, rows):
-            nc.sync.dma_start(out=scale_tile[0:P:8, :].bitcast(I32), in_=rows.bitcast(I32))
-
-        def place_scale_rows(queue, scale_tile, spread):
             for q in range(QUADS):
-                queue.dma_start(out=scale_tile[32 * q : 32 * q + 4, :].bitcast(I32), in_=spread[32 * q : 32 * q + 32 : 8, :].bitcast(I32))
+                nc.sync.dma_start(out=scale_tile[32 * q : 32 * q + 4, :].bitcast(I32), in_=rows[4 * q : 4 * q + 4, :].bitcast(I32))
 
         def dealt_view(w_bf):
             return w_bf[:].rearrange("p (t m j) -> p m j t", t=PACK, j=PACK)
@@ -57,58 +54,56 @@ def tile_picked_gin8_gelu_po_kernel(tc, x_words, x_scales, w1, eps, w2, res, w3_
         w3s_raw = keep.tile([P, D], U8, name="w3s_raw", align_bytes=64)
         w3w_raw = keep.tile([P, 2 * D], U8, name="w3w_raw", tag="w3w_raw", align_bytes=64)
         eps_t = keep.tile([P, PACK], F32, name="eps_t", tag="eps", align_bytes=64)
-        w1_raw = keep.tile([P, PACK, D], F32, name="w1_raw", tag="w_raw", align_bytes=64)
+        w1_half = [keep.tile([P, PACK, D // 2], F32, name="w1_half%d" % u, tag=tag, align_bytes=64) for u, tag in enumerate(("w_raw", "w1_half1"))]
         xw_all = keep.tile([P, T], U32, name="xw_all", tag="xw_all", align_bytes=64)
 
         nc.vector.memset(xs_all[:].bitcast(I32), 0)
         nc.vector.memset(w3s_raw[:].bitcast(I32), 0)
-        xs = keep.tile([P, S], U8, name="xs", align_bytes=64)
-        w3s = keep.tile([P, D], U8, name="w3s", align_bytes=64)
-        nc.vector.memset(xs[:].bitcast(I32), 0)
-        nc.vector.memset(w3s[:].bitcast(I32), 0)
 
         w1_rows = w1.rearrange("(p j) c -> p j c", j=PACK)
-        nc.sync.dma_start(offs_t[:], offs)
         nc.scalar.dma_start(out=eps_t[:], in_=eps.rearrange("(p t) o -> p (t o)", t=PACK))
-        nc.sync.dma_start(out=w1_raw[:, :1, :], in_=w1_rows[:, :1, :])
+        xw_rows = x_words[0].rearrange("p n t -> p (n t)").bitcast(I32)
+        nc.sync.dma_start(out=xw_all[:, : T // 4].bitcast(I32), in_=xw_rows[:, : T // 4])
+        nc.sync.dma_start(offs_t[:], offs)
         load_scale_rows(xs_all, x_scales[0])
+        nc.sync.dma_start(out=xw_all[:, T // 4 :].bitcast(I32), in_=xw_rows[:, T // 4 :])
+        for u in range(2):
+            nc.sync.dma_start(out=w1_half[u][:], in_=w1_rows[:, :, u * D // 2 : (u + 1) * D // 2])
         nc.sync.dma_start(p1_t[:], p1)
         nc.sync.dma_start(p2_t[:], p2)
-        nc.sync.dma_start(out=w1_raw[:, 1:, :], in_=w1_rows[:, 1:, :])
-        nc.sync.dma_start(out=xw_all[:].bitcast(I32), in_=x_words[0].rearrange("p n t -> p (n t)").bitcast(I32))
         nc.sync.dma_start(out=w3w_raw[:].bitcast(I32), in_=w3_words[0].bitcast(I32))
         load_scale_rows(w3s_raw, w3_scales[0])
 
-        xs_spread = keep.tile([P, S], U8, name="xs_spread", align_bytes=64)
-        nc.vector.tensor_copy(out=xs_spread[:], in_=xs_all[:].indirect(offs_t[:]))
-        place_scale_rows(nc.scalar, xs, xs_spread)
-        w3s_spread = keep.tile([P, D], U8, name="w3s_spread", tag="xs_all", align_bytes=64)
-        nc.vector.tensor_copy(
-            out=w3s_spread[:].rearrange("p (t m) -> p t m", t=PACK),
-            in_=w3s_raw[:].rearrange("p (m t) -> p t m", t=PACK),
-        )
-        place_scale_rows(nc.sync, w3s, w3s_spread)
+        xs = keep.tile([P, S], U8, name="xs", align_bytes=64)
+        nc.vector.tensor_copy(out=xs[:], in_=xs_all[:].indirect(offs_t[:]))
 
         w1_bf = keep.tile([P, PACK * D], BF16, name="w1_bf", tag="w1_bf", align_bytes=64)
-        nc.vector.tensor_copy(out=dealt_view(w1_bf)[:, SPLIT:], in_=raw_view(w1_raw)[:, SPLIT:])
-        nc.scalar.copy(out=dealt_view(w1_bf)[:, :SPLIT], in_=raw_view(w1_raw)[:, :SPLIT])
+        xw = keep.tile([P, S], U32, name="xw", align_bytes=64)
+        nc.vector.tensor_copy(out=xw[:], in_=xw_all[:].indirect(offs_t[:]))
+        nc.scalar.copy(out=dealt_view(w1_bf)[:, : P // 2], in_=raw_view(w1_half[0]))
+        nc.vector.tensor_copy(out=dealt_view(w1_bf)[:, P // 2 + SPLIT :], in_=raw_view(w1_half[1])[:, SPLIT:])
+        nc.scalar.copy(out=dealt_view(w1_bf)[:, P // 2 : P // 2 + SPLIT], in_=raw_view(w1_half[1])[:, :SPLIT])
         w1_c = keep.tile([P, D], U32, name="w1_c", align_bytes=64)
         w1_s = keep.tile([P, D], U8, name="w1_s", align_bytes=64)
-        nc.vector.quantize_mx(out=w1_c[:].bitcast(FP8X4), scales=w1_s[:], in_=w1_bf[:])
+        nc.vector.quantize_mx(out=w1_c[:, :P].bitcast(FP8X4), scales=w1_s[:, :P], in_=w1_bf[:, : PACK * P])
+        nc.vector.quantize_mx(out=w1_c[:, P : 2 * P].bitcast(FP8X4), scales=w1_s[:, P : 2 * P], in_=w1_bf[:, PACK * P : 2 * PACK * P])
+        nc.vector.quantize_mx(out=w1_c[:, 2 * P :].bitcast(FP8X4), scales=w1_s[:, 2 * P :], in_=w1_bf[:, 2 * PACK * P :])
 
         w2_raw = keep.tile([P, PACK, D], F32, name="w2_raw", tag="w_raw", align_bytes=64)
         nc.sync.dma_start(out=w2_raw[:], in_=w2.rearrange("(p j) c -> p j c", j=PACK))
-        res_t = keep.tile([P, PACK, S], F32, name="res_t", tag="w1_bf", align_bytes=64)
+        res_t = keep.tile([P, PACK, S], F32, name="res_t", tag="w1_half1", align_bytes=64)
         nc.sync.dma_start(out=res_t[:], in_=res.rearrange("(p t) j -> p t j", t=PACK))
 
-        xw = keep.tile([P, S], U32, name="xw", align_bytes=64)
-        for j0, n in HALVES:
-            nc.vector.tensor_copy(out=xw[:, j0 : j0 + n], in_=xw_all[:].indirect(offs_t[:, j0 // STRIPE : (j0 + n) // STRIPE]))
 
-        w3w = keep.tile([P, 2 * D], U8, name="w3w", tag="xw_all", align_bytes=64)
+        w3w = keep.tile([P, 2 * D], U8, name="w3w", tag="w1_bf", align_bytes=64)
         nc.vector.tensor_copy(
             out=w3w[:].rearrange("p (t m e) -> p t m e", t=PACK, e=2),
             in_=w3w_raw[:].rearrange("p (m t e) -> p t m e", t=PACK, e=2),
+        )
+        w3s = keep.tile([P, D], U8, name="w3s", tag="w3w_raw", align_bytes=64)
+        nc.vector.tensor_copy(
+            out=w3s[:].rearrange("p (t m) -> p t m", t=PACK),
+            in_=w3s_raw[:].rearrange("p (m t) -> p t m", t=PACK),
         )
 
         def product(out, lhs_c, lhs_s, rhs_c, rhs_s):
@@ -180,7 +175,7 @@ def tile_picked_gin8_gelu_po_kernel(tc, x_words, x_scales, w1, eps, w2, res, w3_
 
         def round_z(copy, j0, n, z, tag):
             z_bf = keep.tile([P, PACK * n], BF16, name="z_bf%d" % j0, tag=tag, align_bytes=64)
-            interleave(copy, z_bf[:], z[:])
+            interleave(copy, z_bf[:], z)
             return z_bf
 
         def hidden(b, z_c, z_s):
@@ -195,28 +190,40 @@ def tile_picked_gin8_gelu_po_kernel(tc, x_words, x_scales, w1, eps, w2, res, w3_
         def result(b, h_bf, copy, codes_tag):
             nodes = slice(b * BLOCK, (b + 1) * BLOCK)
             h_c, h_s = quantize("h%d" % b, BLOCK, h_bf[:].rearrange("p j t -> p (j t)"), codes_tag)
-            o_ps = bank("o_ps%d" % b, O_BANKS[b], [P, PACK, BLOCK])
-            for t in range(PACK):
-                product(o_ps[:, t, :], w3w[:, 2 * t * P : 2 * (t + 1) * P].bitcast(FP4X4), w3s[:, t * P : (t + 1) * P], h_c[:], h_s[:])
             o = keep.tile([P, PACK, BLOCK], F32, name="o%d" % b)
-            nc.vector.tensor_tensor(o[:], o_ps[:], res_t[:, :, nodes], ADD)
+            planes = PACK // len(O_BANKS[b])
+            for i, number in enumerate(O_BANKS[b]):
+                o_ps = bank("o_ps%d_%d" % (b, i), number, [P, planes, BLOCK])
+                for e in range(planes):
+                    t = i * planes + e
+                    product(o_ps[:, e, :], w3w[:, 2 * t * P : 2 * (t + 1) * P].bitcast(FP4X4), w3s[:, t * P : (t + 1) * P], h_c[:], h_s[:])
+                mine = slice(i * planes, (i + 1) * planes)
+                nc.vector.tensor_tensor(o[:, mine, :], o_ps[:], res_t[:, mine, nodes], ADD)
             nc.sync.dma_start(out=out_rows[:, :, nodes], in_=o[:])
-            o_bf = keep.tile([P, PACK * BLOCK], BF16, name="o_bf%d" % b, align_bytes=64)
-            interleave(copy, o_bf[:], o[:])
-            nc.vector.quantize_mx(out=out_c[:, nodes].bitcast(FP8X4), scales=out_s[:, nodes], in_=o_bf[:])
+            width = BLOCK // len(O_BANKS[b])
+            o_bf = [keep.tile([P, PACK * width], BF16, name="o_bf%d_%d" % (b, i), align_bytes=64) for i in range(len(O_BANKS[b]))]
+            for i in range(len(o_bf)):
+                interleave(copy, o_bf[i][:], o[:, :, i * width : (i + 1) * width])
+            for i in range(len(o_bf)):
+                cols = slice(b * BLOCK + i * width, b * BLOCK + (i + 1) * width)
+                nc.vector.quantize_mx(out=out_c[:, cols].bitcast(FP8X4), scales=out_s[:, cols], in_=o_bf[i][:])
 
         z01 = look_up(0, 2 * BLOCK, (partial_sums("part_a", 2 * BLOCK), partial_sums("part_b", 2 * BLOCK)))
         z2 = look_up(2 * BLOCK, BLOCK, (partial_sums("part_c", BLOCK), partial_sums("part_d", BLOCK)))
         nc.vector.quantize_mx(out=w2_c[:].bitcast(FP8X4), scales=w2_s[:], in_=w2_bf[:])
-        z01_bf = round_z(nc.scalar.copy, 0, 2 * BLOCK, z01, "w_raw")
+        z01_bf = round_z(nc.scalar.copy, 0, 2 * BLOCK, z01[:], "w_raw")
         z01_c, z01_s = quantize("z0", 2 * BLOCK, z01_bf[:], "eps")
-        z2_bf = round_z(nc.scalar.copy, 2 * BLOCK, BLOCK, z2, "z0")
+        z2_bf = round_z(nc.scalar.copy, 2 * BLOCK, BLOCK, z2[:], "z0")
         z2_c, z2_s = quantize("z256", BLOCK, z2_bf[:], "z256_c")
         z3 = look_up(3 * BLOCK, BLOCK, (z2_bf[:].bitcast(F32).rearrange("p (e j) -> p e j", e=2), z2[:, :2, :]))
         h_bf = [hidden(b, z01_c[:, b * BLOCK : (b + 1) * BLOCK], z01_s[:, b * BLOCK : (b + 1) * BLOCK]) for b in range(2)]
         h_bf.append(hidden(2, z2_c[:], z2_s[:]))
-        z3_bf = round_z(nc.vector.tensor_copy, 3 * BLOCK, BLOCK, z3, "z_bf3")
-        z3_c, z3_s = quantize("z384", BLOCK, z3_bf[:], "z384_c")
+        half = BLOCK // 2
+        z3_bf = [round_z(nc.vector.tensor_copy, 3 * BLOCK + i * half, half, z3[:, :, i * half : (i + 1) * half], "z3_bf%d" % i) for i in range(2)]
+        z3_c = keep.tile([P, BLOCK], U32, name="z3_c", align_bytes=64)
+        z3_s = keep.tile([P, BLOCK], U8, name="z3_s", align_bytes=64)
+        for i in range(2):
+            nc.vector.quantize_mx(out=z3_c[:, i * half : (i + 1) * half].bitcast(FP8X4), scales=z3_s[:, i * half : (i + 1) * half], in_=z3_bf[i][:])
         result(0, h_bf[0], nc.scalar.copy, "y3")
         h_bf.append(hidden(3, z3_c[:], z3_s[:]))
         result(1, h_bf[1], nc.scalar.copy, "h1_c")

@@ -23,10 +23,9 @@ STRIPE = 16
 QUADS = 4
 LINE = 4
 BLOCK = 128
-SPLIT = 16
 HALVES = ((0, S // 2), (S // 2, S // 2))
-H_BANKS = (5, 6, 0, 1)
-O_BANKS = ((7,), (2,), (3,), (4, 5))
+H_BANKS = (6, 7, 0, 1)
+O_BANKS = ((2,), (3,), (4,), (5, 6))
 
 FLOPS = 3 * 2 * D * D * S
 
@@ -77,17 +76,18 @@ def tile_picked_gin8_gelu_po_kernel(tc, x_words, x_scales, w1, eps, w2, res, w3_
         xs = keep.tile([P, S], U8, name="xs", align_bytes=64)
         nc.vector.tensor_copy(out=xs[:], in_=xs_all[:].indirect(offs_t[:]))
 
-        w1_bf = keep.tile([P, PACK * D], BF16, name="w1_bf", tag="w1_bf", align_bytes=64)
+        w1_bf = [keep.tile([P, 2 * PACK * P], BF16, name="w1_bf%d" % i, tag="w1_bf%d" % i, align_bytes=64) for i in range(2)]
         xw = keep.tile([P, S], U32, name="xw", align_bytes=64)
         nc.vector.tensor_copy(out=xw[:], in_=xw_all[:].indirect(offs_t[:]))
-        nc.scalar.copy(out=dealt_view(w1_bf)[:, : P // 2], in_=raw_view(w1_half[0]))
-        nc.vector.tensor_copy(out=dealt_view(w1_bf)[:, P // 2 + SPLIT :], in_=raw_view(w1_half[1])[:, SPLIT:])
-        nc.scalar.copy(out=dealt_view(w1_bf)[:, P // 2 : P // 2 + SPLIT], in_=raw_view(w1_half[1])[:, :SPLIT])
+        for u in range(2):
+            for i, copy in enumerate((nc.vector.tensor_copy, nc.scalar.copy)):
+                dealt = w1_bf[i][:].rearrange("p (t m j) -> p m j t", t=2, j=PACK)
+                copy(out=dealt[:, u * P // 2 : (u + 1) * P // 2], in_=raw_view(w1_half[u])[:, :, :, 2 * i : 2 * i + 2])
         w1_c = keep.tile([P, D], U32, name="w1_c", align_bytes=64)
         w1_s = keep.tile([P, D], U8, name="w1_s", align_bytes=64)
-        nc.vector.quantize_mx(out=w1_c[:, :P].bitcast(FP8X4), scales=w1_s[:, :P], in_=w1_bf[:, : PACK * P])
-        nc.vector.quantize_mx(out=w1_c[:, P : 2 * P].bitcast(FP8X4), scales=w1_s[:, P : 2 * P], in_=w1_bf[:, PACK * P : 2 * PACK * P])
-        nc.vector.quantize_mx(out=w1_c[:, 2 * P :].bitcast(FP8X4), scales=w1_s[:, 2 * P :], in_=w1_bf[:, 2 * PACK * P :])
+        nc.vector.quantize_mx(out=w1_c[:, :P].bitcast(FP8X4), scales=w1_s[:, :P], in_=w1_bf[0][:, : PACK * P])
+        nc.vector.quantize_mx(out=w1_c[:, P : 2 * P].bitcast(FP8X4), scales=w1_s[:, P : 2 * P], in_=w1_bf[0][:, PACK * P :])
+        nc.vector.quantize_mx(out=w1_c[:, 2 * P :].bitcast(FP8X4), scales=w1_s[:, 2 * P :], in_=w1_bf[1][:])
 
         w2_raw = keep.tile([P, PACK, D], F32, name="w2_raw", tag="w_raw", align_bytes=64)
         nc.sync.dma_start(out=w2_raw[:], in_=w2.rearrange("(p j) c -> p j c", j=PACK))
@@ -95,7 +95,7 @@ def tile_picked_gin8_gelu_po_kernel(tc, x_words, x_scales, w1, eps, w2, res, w3_
         nc.sync.dma_start(out=res_t[:], in_=res.rearrange("(p t) j -> p t j", t=PACK))
 
 
-        w3w = keep.tile([P, 2 * D], U8, name="w3w", tag="w1_bf", align_bytes=64)
+        w3w = keep.tile([P, 2 * D], U8, name="w3w", tag="w1_bf1", align_bytes=64)
         nc.vector.tensor_copy(
             out=w3w[:].rearrange("p (t m e) -> p t m e", t=PACK, e=2),
             in_=w3w_raw[:].rearrange("p (m t e) -> p t m e", t=PACK, e=2),
@@ -112,14 +112,16 @@ def tile_picked_gin8_gelu_po_kernel(tc, x_words, x_scales, w1, eps, w2, res, w3_
         def bank(name, number, shape):
             return psum.tile(shape, F32, name=name, tag="bank%d" % number)
 
-        plane0_ps = [bank("y0_%d" % u, u, [P, S // 2]) for u in range(2)]
-        y_ps = [[plane0_ps[0][:], plane0_ps[1][:]]]
-        for u, (j0, n) in enumerate(HALVES):
-            product(plane0_ps[u][:], w1_c[:, :P].bitcast(FP8X4), w1_s[:, :P], xw[:, j0 : j0 + n], xs[:, j0 : j0 + n])
-        plane_ps = {}
-        for t in range(1, PACK):
+        y_ps = []
+        for t in range(2):
             places = slice(t * P, (t + 1) * P)
-            plane_ps[t] = bank("y%d_ps" % t, t + 1, [P, S])
+            y_ps.append([bank("y%d_%d" % (t, u), 2 * t + u, [P, S // 2])[:] for u in range(2)])
+            for u, (j0, n) in enumerate(HALVES):
+                product(y_ps[t][u], w1_c[:, places].bitcast(FP8X4), w1_s[:, places], xw[:, j0 : j0 + n], xs[:, j0 : j0 + n])
+        plane_ps = {}
+        for t in range(2, PACK):
+            places = slice(t * P, (t + 1) * P)
+            plane_ps[t] = bank("y%d_ps" % t, t + 2, [P, S])
             product(plane_ps[t][:], w1_c[:, places].bitcast(FP8X4), w1_s[:, places], xw[:], xs[:])
             y_ps.append([plane_ps[t][:, j0 : j0 + n] for j0, n in HALVES])
 
@@ -131,8 +133,11 @@ def tile_picked_gin8_gelu_po_kernel(tc, x_words, x_scales, w1, eps, w2, res, w3_
 
         nc.scalar.copy(out=y[0][:, : S // 2], in_=y_ps[0][0])
         scale_own(0, 0)
-        nc.scalar.copy(out=y[0][:, S // 2 :], in_=y_ps[0][1])
-        for t in range(1, PACK):
+        nc.vector.tensor_copy(out=y[0][:, S // 2 :], in_=y_ps[0][1])
+        nc.scalar.copy(out=y[1][:, : S // 2], in_=y_ps[1][0])
+        scale_own(0, 1)
+        nc.scalar.copy(out=y[1][:, S // 2 :], in_=y_ps[1][1])
+        for t in range(2, PACK):
             nc.scalar.copy(out=y[t][:], in_=plane_ps[t][:])
             scale_own(0, t)
         for t in range(PACK):
@@ -203,7 +208,7 @@ def tile_picked_gin8_gelu_po_kernel(tc, x_words, x_scales, w1, eps, w2, res, w3_
             width = BLOCK // len(O_BANKS[b])
             o_bf = [keep.tile([P, PACK * width], BF16, name="o_bf%d_%d" % (b, i), align_bytes=64) for i in range(len(O_BANKS[b]))]
             for i in range(len(o_bf)):
-                interleave(copy, o_bf[i][:], o[:, :, i * width : (i + 1) * width])
+                interleave(copy[i], o_bf[i][:], o[:, :, i * width : (i + 1) * width])
             for i in range(len(o_bf)):
                 cols = slice(b * BLOCK + i * width, b * BLOCK + (i + 1) * width)
                 nc.vector.quantize_mx(out=out_c[:, cols].bitcast(FP8X4), scales=out_s[:, cols], in_=o_bf[i][:])
@@ -219,16 +224,17 @@ def tile_picked_gin8_gelu_po_kernel(tc, x_words, x_scales, w1, eps, w2, res, w3_
         h_bf = [hidden(b, z01_c[:, b * BLOCK : (b + 1) * BLOCK], z01_s[:, b * BLOCK : (b + 1) * BLOCK]) for b in range(2)]
         h_bf.append(hidden(2, z2_c[:], z2_s[:]))
         half = BLOCK // 2
-        z3_bf = [round_z(nc.vector.tensor_copy, 3 * BLOCK + i * half, half, z3[:, :, i * half : (i + 1) * half], "z3_bf%d" % i) for i in range(2)]
+        both = (nc.vector.tensor_copy, nc.scalar.copy)
+        z3_bf = [round_z(copy, 3 * BLOCK + i * half, half, z3[:, :, i * half : (i + 1) * half], "z3_bf%d" % i) for i, copy in enumerate(both[:1] * 2)]
         z3_c = keep.tile([P, BLOCK], U32, name="z3_c", align_bytes=64)
         z3_s = keep.tile([P, BLOCK], U8, name="z3_s", align_bytes=64)
         for i in range(2):
             nc.vector.quantize_mx(out=z3_c[:, i * half : (i + 1) * half].bitcast(FP8X4), scales=z3_s[:, i * half : (i + 1) * half], in_=z3_bf[i][:])
-        result(0, h_bf[0], nc.scalar.copy, "y3")
+        result(0, h_bf[0], both[1:], "y3")
         h_bf.append(hidden(3, z3_c[:], z3_s[:]))
-        result(1, h_bf[1], nc.scalar.copy, "h1_c")
-        result(2, h_bf[2], nc.scalar.copy, "h2_c")
-        result(3, h_bf[3], nc.vector.tensor_copy, "h3_c")
+        result(1, h_bf[1], both[1:], "h1_c")
+        result(2, h_bf[2], both[1:], "h2_c")
+        result(3, h_bf[3], both, "h3_c")
 
         last = S - BLOCK
         nc.sync.dma_start(out=out_words[:, :last], in_=out_c[:, :last].bitcast(I32))

@@ -144,7 +144,9 @@ def tile_picked_gin8_gelu_po_kernel(tc, x_words, x_scales, w1, eps, w2, res, w3_
             scale_own(1, t)
 
         w2_bf = keep.tile([P, PACK * D], BF16, name="w2_bf", tag="eps", align_bytes=64)
-        nc.scalar.copy(out=dealt_view(w2_bf), in_=raw_view(w2_raw))
+        for i in range(2):
+            pair = slice(2 * i, 2 * i + 2)
+            nc.scalar.copy(out=dealt_view(w2_bf)[:, :, :, pair], in_=raw_view(w2_raw)[:, :, :, pair])
         w2_c = keep.tile([P, D], U32, name="w2_c", align_bytes=64)
         w2_s = keep.tile([P, D], U8, name="w2_s", align_bytes=64)
 
@@ -236,7 +238,7 @@ def tile_picked_gin8_gelu_po_kernel(tc, x_words, x_scales, w1, eps, w2, res, w3_
         result(2, h_bf[2], both[1:], "h2_c")
         result(3, h_bf[3], both, "h3_c")
 
-        last = S - BLOCK
+        last = S // 2
         nc.sync.dma_start(out=out_words[:, :last], in_=out_c[:, :last].bitcast(I32))
         nc.sync.dma_start(out=out_words[:, last:], in_=out_c[:, last:].bitcast(I32))
         for q in range(QUADS):

@@ -225,6 +225,9 @@ def tile_picked_gin8_gelu_po_kernel(tc, x_words, x_scales, w1, eps, w2, res, w3_
         z3 = look_up(3 * BLOCK, BLOCK, (z2_bf[:].bitcast(F32).rearrange("p (e j) -> p e j", e=2), z2[:, :2, :]))
         h_bf = [hidden(b, z01_c[:, b * BLOCK : (b + 1) * BLOCK], z01_s[:, b * BLOCK : (b + 1) * BLOCK]) for b in range(2)]
         h_bf.append(hidden(2, z2_c[:], z2_s[:]))
+        for b in range(2):
+            warm_ps = bank("warm_ps%d" % b, H_BANKS[b], [P, S])
+            product(warm_ps[:], w2_c[:, :P].bitcast(FP8X4), w2_s[:, :P], xw[:], xs[:])
         half = BLOCK // 2
         both = (nc.vector.tensor_copy, nc.scalar.copy)
         z3_bf = [round_z(copy, 3 * BLOCK + i * half, half, z3[:, :, i * half : (i + 1) * half], "z3_bf%d" % i) for i, copy in enumerate(both[:1] * 2)]

@@ -37,8 +37,11 @@ def tile_picked_gin8_gelu_po_kernel(tc, x_words, x_scales, w1, eps, w2, res, w3_
         psum = ctx.enter_context(tc.psum_pool(name="psum", bufs=1))
 
         def load_scale_rows(scale_tile, rows):
+            nc.sync.dma_start(out=scale_tile[0:P:8, :].bitcast(I32), in_=rows.bitcast(I32))
+
+        def place_scale_rows(queue, scale_tile, spread):
             for q in range(QUADS):
-                nc.sync.dma_start(out=scale_tile[32 * q : 32 * q + 4, :].bitcast(I32), in_=rows[4 * q : 4 * q + 4, :].bitcast(I32))
+                queue.dma_start(out=scale_tile[32 * q : 32 * q + 4, :].bitcast(I32), in_=spread[32 * q : 32 * q + 32 : 8, :].bitcast(I32))
 
         def dealt_view(w_bf):
             return w_bf[:].rearrange("p (t m j) -> p m j t", t=PACK, j=PACK)
@@ -58,6 +61,10 @@ def tile_picked_gin8_gelu_po_kernel(tc, x_words, x_scales, w1, eps, w2, res, w3_
 
         nc.vector.memset(xs_all[:].bitcast(I32), 0)
         nc.vector.memset(w3s_raw[:].bitcast(I32), 0)
+        xs = keep.tile([P, S], U8, name="xs", align_bytes=64)
+        w3s = keep.tile([P, D], U8, name="w3s", align_bytes=64)
+        nc.vector.memset(xs[:].bitcast(I32), 0)
+        nc.vector.memset(w3s[:].bitcast(I32), 0)
 
         w1_rows = w1.rearrange("(p j) c -> p j c", j=PACK)
         nc.scalar.dma_start(out=eps_t[:], in_=eps.rearrange("(p t) o -> p (t o)", t=PACK))
@@ -65,16 +72,23 @@ def tile_picked_gin8_gelu_po_kernel(tc, x_words, x_scales, w1, eps, w2, res, w3_
         nc.sync.dma_start(out=xw_all[:, : T // 4].bitcast(I32), in_=xw_rows[:, : T // 4])
         nc.sync.dma_start(offs_t[:], offs)
         load_scale_rows(xs_all, x_scales[0])
+        load_scale_rows(w3s_raw, w3_scales[0])
+        nc.sync.dma_start(p1_t[:], p1)
         nc.sync.dma_start(out=xw_all[:, T // 4 :].bitcast(I32), in_=xw_rows[:, T // 4 :])
         for u in range(2):
             nc.sync.dma_start(out=w1_half[u][:], in_=w1_rows[:, :, u * D // 2 : (u + 1) * D // 2])
-        nc.sync.dma_start(p1_t[:], p1)
         nc.sync.dma_start(p2_t[:], p2)
         nc.sync.dma_start(out=w3w_raw[:].bitcast(I32), in_=w3_words[0].bitcast(I32))
-        load_scale_rows(w3s_raw, w3_scales[0])
 
-        xs = keep.tile([P, S], U8, name="xs", align_bytes=64)
-        nc.vector.tensor_copy(out=xs[:], in_=xs_all[:].indirect(offs_t[:]))
+        xs_spread = keep.tile([P, S], U8, name="xs_spread", align_bytes=64)
+        nc.vector.tensor_copy(out=xs_spread[:], in_=xs_all[:].indirect(offs_t[:]))
+        place_scale_rows(nc.scalar, xs, xs_spread)
+        w3s_spread = keep.tile([P, D], U8, name="w3s_spread", tag="xs_all", align_bytes=64)
+        nc.vector.tensor_copy(
+            out=w3s_spread[:].rearrange("p (t m) -> p t m", t=PACK),
+            in_=w3s_raw[:].rearrange("p (m t) -> p t m", t=PACK),
+        )
+        place_scale_rows(nc.sync, w3s, w3s_spread)
 
         w1_bf = [keep.tile([P, 2 * PACK * P], BF16, name="w1_bf%d" % i, tag="w1_bf%d" % i, align_bytes=64) for i in range(2)]
         xw = keep.tile([P, S], U32, name="xw", align_bytes=64)
@@ -99,11 +113,6 @@ def tile_picked_gin8_gelu_po_kernel(tc, x_words, x_scales, w1, eps, w2, res, w3_
         nc.vector.tensor_copy(
             out=w3w[:].rearrange("p (t m e) -> p t m e", t=PACK, e=2),
             in_=w3w_raw[:].rearrange("p (m t e) -> p t m e", t=PACK, e=2),
-        )
-        w3s = keep.tile([P, D], U8, name="w3s", tag="w3w_raw", align_bytes=64)
-        nc.vector.tensor_copy(
-            out=w3s[:].rearrange("p (t m) -> p t m", t=PACK),
-            in_=w3s_raw[:].rearrange("p (m t) -> p t m", t=PACK),
         )
 
         def product(out, lhs_c, lhs_s, rhs_c, rhs_s):
@@ -225,9 +234,6 @@ def tile_picked_gin8_gelu_po_kernel(tc, x_words, x_scales, w1, eps, w2, res, w3_
         z3 = look_up(3 * BLOCK, BLOCK, (z2_bf[:].bitcast(F32).rearrange("p (e j) -> p e j", e=2), z2[:, :2, :]))
         h_bf = [hidden(b, z01_c[:, b * BLOCK : (b + 1) * BLOCK], z01_s[:, b * BLOCK : (b + 1) * BLOCK]) for b in range(2)]
         h_bf.append(hidden(2, z2_c[:], z2_s[:]))
-        for b in range(2):
-            warm_ps = bank("warm_ps%d" % b, H_BANKS[b], [P, S])
-            product(warm_ps[:], w2_c[:, :P].bitcast(FP8X4), w2_s[:, :P], xw[:], xs[:])
         half = BLOCK // 2
         both = (nc.vector.tensor_copy, nc.scalar.copy)
         z3_bf = [round_z(copy, 3 * BLOCK + i * half, half, z3[:, :, i * half : (i + 1) * half], "z3_bf%d" % i) for i, copy in enumerate(both[:1] * 2)]

@@ -21,11 +21,16 @@ S = 512
 D = 512
 STRIPE = 16
 QUADS = 4
+SPREAD = 8
+PAIRS = (slice(0, 2), slice(2, 4))
+FIRST = T // 4
 LINE = 4
-BLOCK = 128
+CHUNK = 128
 HALVES = ((0, S // 2), (S // 2, S // 2))
 H_BANKS = (6, 7, 0, 1)
 O_BANKS = ((2,), (3,), (4,), (5, 6))
+H_TAGS = ("y0", "y1", "h2_c", "h3_c")
+O_TAGS = ("y2", "y3", "o2", "o3")
 
 FLOPS = 3 * 2 * D * D * S
 
@@ -37,14 +42,14 @@ def tile_picked_gin8_gelu_po_kernel(tc, x_words, x_scales, w1, eps, w2, res, w3_
         psum = ctx.enter_context(tc.psum_pool(name="psum", bufs=1))
 
         def load_scale_rows(scale_tile, rows):
-            nc.sync.dma_start(out=scale_tile[0:P:8, :].bitcast(I32), in_=rows.bitcast(I32))
+            nc.sync.dma_start(out=scale_tile[0:P:SPREAD, :].bitcast(I32), in_=rows.bitcast(I32))
 
         def place_scale_rows(queue, scale_tile, spread):
-            for q in range(QUADS):
-                queue.dma_start(out=scale_tile[32 * q : 32 * q + 4, :].bitcast(I32), in_=spread[32 * q : 32 * q + 32 : 8, :].bitcast(I32))
+            for g in range(QUADS):
+                queue.dma_start(out=scale_tile[32 * g : 32 * g + 4, :].bitcast(I32), in_=spread[32 * g : 32 * g + 32 : SPREAD, :].bitcast(I32))
 
         def dealt_view(w_bf):
-            return w_bf[:].rearrange("p (t m j) -> p m j t", t=PACK, j=PACK)
+            return w_bf[:].rearrange("p (t m j) -> p m j t", m=P, j=PACK)
 
         def raw_view(w_raw):
             return w_raw[:].rearrange("p j (m t) -> p m j t", t=PACK)
@@ -54,10 +59,10 @@ def tile_picked_gin8_gelu_po_kernel(tc, x_words, x_scales, w1, eps, w2, res, w3_
         p2_t = keep.tile([P, S // STRIPE], U16, name="p2_t")
         xs_all = keep.tile([P, T], U8, name="xs_all", tag="xs_all", align_bytes=64)
         w3s_raw = keep.tile([P, D], U8, name="w3s_raw", align_bytes=64)
-        w3w_raw = keep.tile([P, 2 * D], U8, name="w3w_raw", tag="w3w_raw", align_bytes=64)
+        w3w_raw = keep.tile([P, 2 * D], U8, name="w3w_raw", align_bytes=64)
         eps_t = keep.tile([P, PACK], F32, name="eps_t", tag="eps", align_bytes=64)
         w1_half = [keep.tile([P, PACK, D // 2], F32, name="w1_half%d" % u, tag=tag, align_bytes=64) for u, tag in enumerate(("w_raw", "w1_half1"))]
-        xw_all = keep.tile([P, T], U32, name="xw_all", tag="xw_all", align_bytes=64)
+        xw_all = keep.tile([P, T], U32, name="xw_all", align_bytes=64)
 
         nc.vector.memset(xs_all[:].bitcast(I32), 0)
         nc.vector.memset(w3s_raw[:].bitcast(I32), 0)
@@ -69,12 +74,12 @@ def tile_picked_gin8_gelu_po_kernel(tc, x_words, x_scales, w1, eps, w2, res, w3_
         w1_rows = w1.rearrange("(p j) c -> p j c", j=PACK)
         nc.scalar.dma_start(out=eps_t[:], in_=eps.rearrange("(p t) o -> p (t o)", t=PACK))
         xw_rows = x_words[0].rearrange("p n t -> p (n t)").bitcast(I32)
-        nc.sync.dma_start(out=xw_all[:, : T // 4].bitcast(I32), in_=xw_rows[:, : T // 4])
+        nc.sync.dma_start(out=xw_all[:, :FIRST].bitcast(I32), in_=xw_rows[:, :FIRST])
         nc.sync.dma_start(offs_t[:], offs)
         load_scale_rows(xs_all, x_scales[0])
         load_scale_rows(w3s_raw, w3_scales[0])
         nc.sync.dma_start(p1_t[:], p1)
-        nc.sync.dma_start(out=xw_all[:, T // 4 :].bitcast(I32), in_=xw_rows[:, T // 4 :])
+        nc.sync.dma_start(out=xw_all[:, FIRST:].bitcast(I32), in_=xw_rows[:, FIRST:])
         for u in range(2):
             nc.sync.dma_start(out=w1_half[u][:], in_=w1_rows[:, :, u * D // 2 : (u + 1) * D // 2])
         nc.sync.dma_start(p2_t[:], p2)
@@ -95,8 +100,7 @@ def tile_picked_gin8_gelu_po_kernel(tc, x_words, x_scales, w1, eps, w2, res, w3_
         nc.vector.tensor_copy(out=xw[:], in_=xw_all[:].indirect(offs_t[:]))
         for u in range(2):
             for i, copy in enumerate((nc.vector.tensor_copy, nc.scalar.copy)):
-                dealt = w1_bf[i][:].rearrange("p (t m j) -> p m j t", t=2, j=PACK)
-                copy(out=dealt[:, u * P // 2 : (u + 1) * P // 2], in_=raw_view(w1_half[u])[:, :, :, 2 * i : 2 * i + 2])
+                copy(out=dealt_view(w1_bf[i])[:, u * P // 2 : (u + 1) * P // 2], in_=raw_view(w1_half[u])[:, :, :, PAIRS[i]])
         w1_c = keep.tile([P, D], U32, name="w1_c", align_bytes=64)
         w1_s = keep.tile([P, D], U8, name="w1_s", align_bytes=64)
         nc.vector.quantize_mx(out=w1_c[:, :P].bitcast(FP8X4), scales=w1_s[:, :P], in_=w1_bf[0][:, : PACK * P])
@@ -107,7 +111,6 @@ def tile_picked_gin8_gelu_po_kernel(tc, x_words, x_scales, w1, eps, w2, res, w3_
         nc.sync.dma_start(out=w2_raw[:], in_=w2.rearrange("(p j) c -> p j c", j=PACK))
         res_t = keep.tile([P, PACK, S], F32, name="res_t", tag="w1_half1", align_bytes=64)
         nc.sync.dma_start(out=res_t[:], in_=res.rearrange("(p t) j -> p t j", t=PACK))
-
 
         w3w = keep.tile([P, 2 * D], U8, name="w3w", tag="w1_bf1", align_bytes=64)
         nc.vector.tensor_copy(
@@ -153,8 +156,7 @@ def tile_picked_gin8_gelu_po_kernel(tc, x_words, x_scales, w1, eps, w2, res, w3_
             scale_own(1, t)
 
         w2_bf = keep.tile([P, PACK * D], BF16, name="w2_bf", tag="eps", align_bytes=64)
-        for i in range(2):
-            pair = slice(2 * i, 2 * i + 2)
+        for pair in PAIRS:
             nc.scalar.copy(out=dealt_view(w2_bf)[:, :, :, pair], in_=raw_view(w2_raw)[:, :, :, pair])
         w2_c = keep.tile([P, D], U32, name="w2_c", align_bytes=64)
         w2_s = keep.tile([P, D], U8, name="w2_s", align_bytes=64)
@@ -195,61 +197,59 @@ def tile_picked_gin8_gelu_po_kernel(tc, x_words, x_scales, w1, eps, w2, res, w3_
             return z_bf
 
         def hidden(b, z_c, z_s):
-            h_ps = bank("h_ps%d" % b, H_BANKS[b], [P, PACK, BLOCK])
+            h_ps = bank("h_ps%d" % b, H_BANKS[b], [P, PACK, CHUNK])
             for t in range(PACK):
                 places = slice(t * P, (t + 1) * P)
                 product(h_ps[:, t, :], w2_c[:, places].bitcast(FP8X4), w2_s[:, places], z_c, z_s)
-            h_bf = keep.tile([P, BLOCK, PACK], BF16, name="h_bf%d" % b, align_bytes=64)
+            h_bf = keep.tile([P, CHUNK, PACK], BF16, name="h_bf%d" % b, align_bytes=64)
             nc.scalar.activation(out=h_bf[:], in_=h_ps[:].rearrange("p t j -> p j t"), func=GELU)
             return h_bf
 
-        def result(b, h_bf, copy, codes_tag):
-            nodes = slice(b * BLOCK, (b + 1) * BLOCK)
-            h_c, h_s = quantize("h%d" % b, BLOCK, h_bf[:].rearrange("p j t -> p (j t)"), codes_tag)
-            o = keep.tile([P, PACK, BLOCK], F32, name="o%d" % b)
+        def result(b, h_bf, copies):
+            nodes = slice(b * CHUNK, (b + 1) * CHUNK)
+            h_c, h_s = quantize("h%d" % b, CHUNK, h_bf[:].rearrange("p j t -> p (j t)"), H_TAGS[b])
+            o = keep.tile([P, PACK, CHUNK], F32, name="o%d" % b, tag=O_TAGS[b], align_bytes=64)
             planes = PACK // len(O_BANKS[b])
             for i, number in enumerate(O_BANKS[b]):
-                o_ps = bank("o_ps%d_%d" % (b, i), number, [P, planes, BLOCK])
+                o_ps = bank("o_ps%d_%d" % (b, i), number, [P, planes, CHUNK])
                 for e in range(planes):
                     t = i * planes + e
                     product(o_ps[:, e, :], w3w[:, 2 * t * P : 2 * (t + 1) * P].bitcast(FP4X4), w3s[:, t * P : (t + 1) * P], h_c[:], h_s[:])
                 mine = slice(i * planes, (i + 1) * planes)
                 nc.vector.tensor_tensor(o[:, mine, :], o_ps[:], res_t[:, mine, nodes], ADD)
             nc.sync.dma_start(out=out_rows[:, :, nodes], in_=o[:])
-            width = BLOCK // len(O_BANKS[b])
-            o_bf = [keep.tile([P, PACK * width], BF16, name="o_bf%d_%d" % (b, i), align_bytes=64) for i in range(len(O_BANKS[b]))]
-            for i in range(len(o_bf)):
-                interleave(copy[i], o_bf[i][:], o[:, :, i * width : (i + 1) * width])
-            for i in range(len(o_bf)):
-                cols = slice(b * BLOCK + i * width, b * BLOCK + (i + 1) * width)
+            width = CHUNK // len(copies)
+            o_bf = [keep.tile([P, PACK * width], BF16, name="o_bf%d_%d" % (b, i), align_bytes=64) for i in range(len(copies))]
+            for i, copy in enumerate(copies):
+                interleave(copy, o_bf[i][:], o[:, :, i * width : (i + 1) * width])
+            for i in range(len(copies)):
+                cols = slice(b * CHUNK + i * width, b * CHUNK + (i + 1) * width)
                 nc.vector.quantize_mx(out=out_c[:, cols].bitcast(FP8X4), scales=out_s[:, cols], in_=o_bf[i][:])
 
-        z01 = look_up(0, 2 * BLOCK, (partial_sums("part_a", 2 * BLOCK), partial_sums("part_b", 2 * BLOCK)))
-        z2 = look_up(2 * BLOCK, BLOCK, (partial_sums("part_c", BLOCK), partial_sums("part_d", BLOCK)))
+        z01 = look_up(0, 2 * CHUNK, (partial_sums("part_a", 2 * CHUNK), partial_sums("part_b", 2 * CHUNK)))
+        z2 = look_up(2 * CHUNK, CHUNK, (partial_sums("part_c", CHUNK), partial_sums("part_d", CHUNK)))
         nc.vector.quantize_mx(out=w2_c[:].bitcast(FP8X4), scales=w2_s[:], in_=w2_bf[:])
-        z01_bf = round_z(nc.scalar.copy, 0, 2 * BLOCK, z01[:], "w_raw")
-        z01_c, z01_s = quantize("z0", 2 * BLOCK, z01_bf[:], "eps")
-        z2_bf = round_z(nc.scalar.copy, 2 * BLOCK, BLOCK, z2[:], "z0")
-        z2_c, z2_s = quantize("z256", BLOCK, z2_bf[:], "z256_c")
-        z3 = look_up(3 * BLOCK, BLOCK, (z2_bf[:].bitcast(F32).rearrange("p (e j) -> p e j", e=2), z2[:, :2, :]))
-        h_bf = [hidden(b, z01_c[:, b * BLOCK : (b + 1) * BLOCK], z01_s[:, b * BLOCK : (b + 1) * BLOCK]) for b in range(2)]
+        z01_bf = round_z(nc.scalar.copy, 0, 2 * CHUNK, z01[:], "w_raw")
+        z01_c, z01_s = quantize("z0", 2 * CHUNK, z01_bf[:], "eps")
+        z2_bf = round_z(nc.scalar.copy, 2 * CHUNK, CHUNK, z2[:], "z0")
+        z2_c, z2_s = quantize("z256", CHUNK, z2_bf[:], "z256_c")
+        z3 = look_up(3 * CHUNK, CHUNK, (z2_bf[:].bitcast(F32).rearrange("p (e j) -> p e j", e=2), z2[:, :2, :]))
+        h_bf = [hidden(b, z01_c[:, b * CHUNK : (b + 1) * CHUNK], z01_s[:, b * CHUNK : (b + 1) * CHUNK]) for b in range(2)]
         h_bf.append(hidden(2, z2_c[:], z2_s[:]))
-        half = BLOCK // 2
-        both = (nc.vector.tensor_copy, nc.scalar.copy)
-        z3_bf = [round_z(copy, 3 * BLOCK + i * half, half, z3[:, :, i * half : (i + 1) * half], "z3_bf%d" % i) for i, copy in enumerate(both[:1] * 2)]
-        z3_c = keep.tile([P, BLOCK], U32, name="z3_c", align_bytes=64)
-        z3_s = keep.tile([P, BLOCK], U8, name="z3_s", align_bytes=64)
+        half = CHUNK // 2
+        z3_bf = [round_z(nc.vector.tensor_copy, 3 * CHUNK + i * half, half, z3[:, :, i * half : (i + 1) * half], "z3_bf%d" % i) for i in range(2)]
+        z3_c = keep.tile([P, CHUNK], U32, name="z3_c", align_bytes=64)
+        z3_s = keep.tile([P, CHUNK], U8, name="z3_s", align_bytes=64)
         for i in range(2):
             nc.vector.quantize_mx(out=z3_c[:, i * half : (i + 1) * half].bitcast(FP8X4), scales=z3_s[:, i * half : (i + 1) * half], in_=z3_bf[i][:])
-        result(0, h_bf[0], both[1:], "y3")
+        result(0, h_bf[0], (nc.scalar.copy,))
         h_bf.append(hidden(3, z3_c[:], z3_s[:]))
-        result(1, h_bf[1], both[1:], "h1_c")
-        result(2, h_bf[2], both[1:], "h2_c")
-        result(3, h_bf[3], both, "h3_c")
+        result(1, h_bf[1], (nc.scalar.copy,))
+        result(2, h_bf[2], (nc.scalar.copy,))
+        result(3, h_bf[3], (nc.vector.tensor_copy, nc.scalar.copy))
 
-        last = S // 2
-        nc.sync.dma_start(out=out_words[:, :last], in_=out_c[:, :last].bitcast(I32))
-        nc.sync.dma_start(out=out_words[:, last:], in_=out_c[:, last:].bitcast(I32))
-        for q in range(QUADS):
-            queue = nc.scalar if q % 2 else nc.sync
-            queue.dma_start(out=out_2[0][4 * q : 4 * q + 4, :].bitcast(I32), in_=out_s[32 * q : 32 * q + 4, :].bitcast(I32))
+        for j0, n in HALVES:
+            nc.sync.dma_start(out=out_words[:, j0 : j0 + n], in_=out_c[:, j0 : j0 + n].bitcast(I32))
+        for g in range(QUADS):
+            queue = nc.scalar if g % 2 else nc.sync
+            queue.dma_start(out=out_2[0][4 * g : 4 * g + 4, :].bitcast(I32), in_=out_s[32 * g : 32 * g + 4, :].bitcast(I32))

@@ -29,8 +29,8 @@ CHUNK = 128
 HALVES = ((0, S // 2), (S // 2, S // 2))
 H_BANKS = (6, 7, 0, 1)
 O_BANKS = ((2,), (3,), (4,), (5, 6))
-H_TAGS = ("y0", "y1", "h2_c", "h3_c")
-O_TAGS = ("y2", "y3", "o2", "o3")
+H_TAGS = ("h0_c", "h1_c", "h2_c", "h3_c")
+O_TAGS = ("z", "z2_c", "o2", "o3")
 
 FLOPS = 3 * 2 * D * D * S
 
@@ -39,6 +39,7 @@ def tile_picked_gin8_gelu_po_kernel(tc, x_words, x_scales, w1, eps, w2, res, w3_
     nc = tc.nc
     with ExitStack() as ctx:
         keep = ctx.enter_context(tc.tile_pool(name="keep", bufs=1))
+        turn = ctx.enter_context(tc.tile_pool(name="turn", bufs=1))
         psum = ctx.enter_context(tc.psum_pool(name="psum", bufs=1))
 
         def load_scale_rows(scale_tile, rows):
@@ -60,8 +61,9 @@ def tile_picked_gin8_gelu_po_kernel(tc, x_words, x_scales, w1, eps, w2, res, w3_
         xs_all = keep.tile([P, T], U8, name="xs_all", tag="xs_all", align_bytes=64)
         w3s_raw = keep.tile([P, D], U8, name="w3s_raw", align_bytes=64)
         w3w_raw = keep.tile([P, 2 * D], U8, name="w3w_raw", align_bytes=64)
-        eps_t = keep.tile([P, PACK], F32, name="eps_t", tag="eps", align_bytes=64)
-        w1_half = [keep.tile([P, PACK, D // 2], F32, name="w1_half%d" % u, tag=tag, align_bytes=64) for u, tag in enumerate(("w_raw", "w1_half1"))]
+        z_a = keep.tile([P, PACK, S // 2], F32, name="z_a", tag="z", align_bytes=64)
+        eps_t = z_a[:].rearrange("p s (h c) -> p (s h) c", h=2)[:, 1 : 1 + PACK, 0:1]
+        w1_half = [turn.tile([P, PACK, D // 2], F32, name="w1_half0", offset=0, align_bytes=64), keep.tile([P, PACK, D // 2], F32, name="w1_half1", tag="w1_half1", align_bytes=64)]
         xw_all = keep.tile([P, T], U32, name="xw_all", align_bytes=64)
 
         nc.vector.memset(xs_all[:].bitcast(I32), 0)
@@ -72,7 +74,8 @@ def tile_picked_gin8_gelu_po_kernel(tc, x_words, x_scales, w1, eps, w2, res, w3_
         nc.vector.memset(w3s[:].bitcast(I32), 0)
 
         w1_rows = w1.rearrange("(p j) c -> p j c", j=PACK)
-        nc.scalar.dma_start(out=eps_t[:], in_=eps.rearrange("(p t) o -> p (t o)", t=PACK))
+        with nc.allow_non_contiguous_dma(reason="one value of eps for each plane"):
+            nc.scalar.dma_start(out=eps_t, in_=eps.rearrange("(p t) o -> p t o", t=PACK))
         xw_rows = x_words[0].rearrange("p n t -> p (n t)").bitcast(I32)
         nc.sync.dma_start(out=xw_all[:, :FIRST].bitcast(I32), in_=xw_rows[:, :FIRST])
         nc.sync.dma_start(offs_t[:], offs)
@@ -107,15 +110,15 @@ def tile_picked_gin8_gelu_po_kernel(tc, x_words, x_scales, w1, eps, w2, res, w3_
         nc.vector.quantize_mx(out=w1_c[:, P : 2 * P].bitcast(FP8X4), scales=w1_s[:, P : 2 * P], in_=w1_bf[0][:, PACK * P :])
         nc.vector.quantize_mx(out=w1_c[:, 2 * P :].bitcast(FP8X4), scales=w1_s[:, 2 * P :], in_=w1_bf[1][:])
 
-        w2_raw = keep.tile([P, PACK, D], F32, name="w2_raw", tag="w_raw", align_bytes=64)
+        w2_raw = turn.tile([P, PACK, D], F32, name="w2_raw", offset=0, align_bytes=64)
         nc.sync.dma_start(out=w2_raw[:], in_=w2.rearrange("(p j) c -> p j c", j=PACK))
         res_t = keep.tile([P, PACK, S], F32, name="res_t", tag="w1_half1", align_bytes=64)
         nc.sync.dma_start(out=res_t[:], in_=res.rearrange("(p t) j -> p t j", t=PACK))
 
         w3w = keep.tile([P, 2 * D], U8, name="w3w", tag="w1_bf1", align_bytes=64)
         nc.vector.tensor_copy(
-            out=w3w[:].rearrange("p (t m e) -> p t m e", t=PACK, e=2),
-            in_=w3w_raw[:].rearrange("p (m t e) -> p t m e", t=PACK, e=2),
+            out=w3w[:].bitcast(U16).rearrange("p (t m) -> p t m", t=PACK),
+            in_=w3w_raw[:].bitcast(U16).rearrange("p (m t) -> p t m", t=PACK),
         )
 
         def product(out, lhs_c, lhs_s, rhs_c, rhs_s):
@@ -138,24 +141,25 @@ def tile_picked_gin8_gelu_po_kernel(tc, x_words, x_scales, w1, eps, w2, res, w3_
             y_ps.append([plane_ps[t][:, j0 : j0 + n] for j0, n in HALVES])
 
         y = [keep.tile([P, S], F32, name="y%d" % t, tag="y%d" % t, align_bytes=64) for t in range(PACK)]
-        ey = [[keep.tile([P, S // 2], F32, name="ey%d_%d" % (u, t)) for t in range(PACK)] for u in range(2)]
+        ey = [keep.tile([P, S], F32, name="ey%d" % t, align_bytes=64) for t in range(PACK)]
+        half = S // 2
 
-        def scale_own(u, t):
-            nc.scalar.activation(out=ey[u][t][:], in_=y_ps[t][u], func=COPY, scale=eps_t[:, t : t + 1])
+        def scale_own(out, bank_ap, t):
+            nc.scalar.activation(out=out, in_=bank_ap, func=COPY, scale=eps_t[:, t, :])
 
-        nc.scalar.copy(out=y[0][:, : S // 2], in_=y_ps[0][0])
-        scale_own(0, 0)
-        nc.vector.tensor_copy(out=y[0][:, S // 2 :], in_=y_ps[0][1])
-        nc.scalar.copy(out=y[1][:, : S // 2], in_=y_ps[1][0])
-        scale_own(0, 1)
-        nc.scalar.copy(out=y[1][:, S // 2 :], in_=y_ps[1][1])
+        nc.scalar.copy(out=y[0][:, :half], in_=y_ps[0][0])
+        scale_own(ey[0][:, :half], y_ps[0][0], 0)
+        nc.vector.tensor_copy(out=y[0][:, half:], in_=y_ps[0][1])
+        scale_own(ey[0][:, half:], y_ps[0][1], 0)
+        for u in range(2):
+            nc.scalar.copy(out=y[1][:, u * half : (u + 1) * half], in_=y_ps[1][u])
+        for u in range(2):
+            scale_own(ey[1][:, u * half : (u + 1) * half], y_ps[1][u], 1)
         for t in range(2, PACK):
             nc.scalar.copy(out=y[t][:], in_=plane_ps[t][:])
-            scale_own(0, t)
-        for t in range(PACK):
-            scale_own(1, t)
+            scale_own(ey[t][:], plane_ps[t][:], t)
 
-        w2_bf = keep.tile([P, PACK * D], BF16, name="w2_bf", tag="eps", align_bytes=64)
+        w2_bf = keep.tile([P, PACK * D], BF16, name="w2_bf", tag="w1_bf0", align_bytes=64)
         for pair in PAIRS:
             nc.scalar.copy(out=dealt_view(w2_bf)[:, :, :, pair], in_=raw_view(w2_raw)[:, :, :, pair])
         w2_c = keep.tile([P, D], U32, name="w2_c", align_bytes=64)
@@ -169,21 +173,11 @@ def tile_picked_gin8_gelu_po_kernel(tc, x_words, x_scales, w1, eps, w2, res, w3_
         def interleave(copy, dst, src):
             copy(out=dst.rearrange("p (c i t) -> p c t i", t=PACK, i=LINE), in_=src.rearrange("p t (c i) -> p c t i", i=LINE))
 
-        def partial_sums(name, n):
-            return keep.tile([P, 2, n], F32, name=name)[:]
+        part = [[keep.tile([P, half], F32, name="part%d_%d" % (u, t))[:] for t in range(PACK - 2 * u)] for u in range(2)]
+        part[1].extend([ey[3][:, :half], ey[2][:, :half]])
 
-        def look_up(j0, n, parts):
-            z = keep.tile([P, PACK, n], F32, name="z%d" % j0, tag="z%d" % j0, align_bytes=64)
-            entries = slice(j0 // STRIPE, (j0 + n) // STRIPE)
-            u, at = divmod(j0, S // 2)
-            for pair, part in enumerate(parts):
-                for e in range(2):
-                    t = 2 * pair + e
-                    nc.vector.tensor_tensor(part[:, e, :], y[t][:].indirect(p1_t[:, entries]), ey[u][t][:, at : at + n], ADD)
-                for e in range(2):
-                    t = 2 * pair + e
-                    nc.vector.tensor_tensor(z[:, t, :], y[t][:].indirect(p2_t[:, entries]), part[:, e, :], ADD)
-            return z
+        def look_up(out, t, list_t, j0, n, plain):
+            nc.vector.tensor_tensor(out, y[t][:].indirect(list_t[:, j0 // STRIPE : (j0 + n) // STRIPE]), plain, ADD)
 
         def quantize(name, width, src, codes_tag):
             codes = keep.tile([P, width], U32, name=name + "_c", tag=codes_tag, align_bytes=64)
@@ -196,18 +190,15 @@ def tile_picked_gin8_gelu_po_kernel(tc, x_words, x_scales, w1, eps, w2, res, w3_
             interleave(copy, z_bf[:], z)
             return z_bf
 
-        def hidden(b, z_c, z_s):
+        def hidden(b, z_c, z_s, h_bf):
             h_ps = bank("h_ps%d" % b, H_BANKS[b], [P, PACK, CHUNK])
             for t in range(PACK):
                 places = slice(t * P, (t + 1) * P)
                 product(h_ps[:, t, :], w2_c[:, places].bitcast(FP8X4), w2_s[:, places], z_c, z_s)
-            h_bf = keep.tile([P, CHUNK, PACK], BF16, name="h_bf%d" % b, align_bytes=64)
-            nc.scalar.activation(out=h_bf[:], in_=h_ps[:].rearrange("p t j -> p j t"), func=GELU)
-            return h_bf
+            nc.scalar.activation(out=h_bf.rearrange("p (j t) -> p j t", t=PACK), in_=h_ps[:].rearrange("p t j -> p j t"), func=GELU)
 
-        def result(b, h_bf, copies):
+        def third(b, h_c, h_s):
             nodes = slice(b * CHUNK, (b + 1) * CHUNK)
-            h_c, h_s = quantize("h%d" % b, CHUNK, h_bf[:].rearrange("p j t -> p (j t)"), H_TAGS[b])
             o = keep.tile([P, PACK, CHUNK], F32, name="o%d" % b, tag=O_TAGS[b], align_bytes=64)
             planes = PACK // len(O_BANKS[b])
             for i, number in enumerate(O_BANKS[b]):
@@ -218,6 +209,9 @@ def tile_picked_gin8_gelu_po_kernel(tc, x_words, x_scales, w1, eps, w2, res, w3_
                 mine = slice(i * planes, (i + 1) * planes)
                 nc.vector.tensor_tensor(o[:, mine, :], o_ps[:], res_t[:, mine, nodes], ADD)
             nc.sync.dma_start(out=out_rows[:, :, nodes], in_=o[:])
+            return o
+
+        def hand_on(b, o, copies):
             width = CHUNK // len(copies)
             o_bf = [keep.tile([P, PACK * width], BF16, name="o_bf%d_%d" % (b, i), align_bytes=64) for i in range(len(copies))]
             for i, copy in enumerate(copies):
@@ -226,27 +220,55 @@ def tile_picked_gin8_gelu_po_kernel(tc, x_words, x_scales, w1, eps, w2, res, w3_
                 cols = slice(b * CHUNK + i * width, b * CHUNK + (i + 1) * width)
                 nc.vector.quantize_mx(out=out_c[:, cols].bitcast(FP8X4), scales=out_s[:, cols], in_=o_bf[i][:])
 
-        z01 = look_up(0, 2 * CHUNK, (partial_sums("part_a", 2 * CHUNK), partial_sums("part_b", 2 * CHUNK)))
-        z2 = look_up(2 * CHUNK, CHUNK, (partial_sums("part_c", CHUNK), partial_sums("part_d", CHUNK)))
+        def first(u, t):
+            look_up(part[u][t], t, p1_t, u * half, half, ey[t][:, u * half : (u + 1) * half])
+
+        def second(t):
+            look_up(z_a[:, t, :], t, p2_t, 0, half, part[0][t])
+
+        first(0, 0)
+        first(1, 0)
+        second(0)
+        first(0, 1)
+        first(1, 1)
+        for t in range(2, PACK):
+            first(0, t)
+            second(t - 1)
+        second(3)
+        first(1, 2)
+        first(1, 3)
         nc.vector.quantize_mx(out=w2_c[:].bitcast(FP8X4), scales=w2_s[:], in_=w2_bf[:])
-        z01_bf = round_z(nc.scalar.copy, 0, 2 * CHUNK, z01[:], "w_raw")
-        z01_c, z01_s = quantize("z0", 2 * CHUNK, z01_bf[:], "eps")
-        z2_bf = round_z(nc.scalar.copy, 2 * CHUNK, CHUNK, z2[:], "z0")
-        z2_c, z2_s = quantize("z256", CHUNK, z2_bf[:], "z256_c")
-        z3 = look_up(3 * CHUNK, CHUNK, (z2_bf[:].bitcast(F32).rearrange("p (e j) -> p e j", e=2), z2[:, :2, :]))
-        h_bf = [hidden(b, z01_c[:, b * CHUNK : (b + 1) * CHUNK], z01_s[:, b * CHUNK : (b + 1) * CHUNK]) for b in range(2)]
-        h_bf.append(hidden(2, z2_c[:], z2_s[:]))
-        half = CHUNK // 2
-        z3_bf = [round_z(nc.vector.tensor_copy, 3 * CHUNK + i * half, half, z3[:, :, i * half : (i + 1) * half], "z3_bf%d" % i) for i in range(2)]
-        z3_c = keep.tile([P, CHUNK], U32, name="z3_c", align_bytes=64)
-        z3_s = keep.tile([P, CHUNK], U8, name="z3_s", align_bytes=64)
-        for i in range(2):
-            nc.vector.quantize_mx(out=z3_c[:, i * half : (i + 1) * half].bitcast(FP8X4), scales=z3_s[:, i * half : (i + 1) * half], in_=z3_bf[i][:])
-        result(0, h_bf[0], (nc.scalar.copy,))
-        h_bf.append(hidden(3, z3_c[:], z3_s[:]))
-        result(1, h_bf[1], (nc.scalar.copy,))
-        result(2, h_bf[2], (nc.scalar.copy,))
-        result(3, h_bf[3], (nc.vector.tensor_copy, nc.scalar.copy))
+        za_bf = turn.tile([P, PACK * half], BF16, name="za_bf", offset=4 * PACK * half, align_bytes=64)
+        interleave(nc.scalar.copy, za_bf[:], z_a[:])
+        z_b = keep.tile([P, PACK, 3 * CHUNK], F32, name="z_b", tag="z", align_bytes=64)
+        za_c, za_s = quantize("za", half, za_bf[:], "za_c")
+        for t in (2, 3):
+            look_up(z_b[:, t, :half], t, p2_t, half, half, part[1][t])
+        def last(c, t):
+            look_up(z_b[:, t, c * CHUNK : (c + 1) * CHUNK], t, p2_t, half + c * CHUNK, CHUNK, part[1][t][:, c * CHUNK : (c + 1) * CHUNK])
+
+        h_bf = [z_b[:, b, CHUNK:].bitcast(BF16) for b in range(2)]
+        h_bf.extend([keep.tile([P, PACK * CHUNK], BF16, name="h_bf%d" % b, align_bytes=64)[:] for b in (2, 3)])
+        for t in range(2):
+            last(0, t)
+        for b in range(2):
+            hidden(b, za_c[:, b * CHUNK : (b + 1) * CHUNK], za_s[:, b * CHUNK : (b + 1) * CHUNK], h_bf[b])
+        z2_bf = round_z(nc.scalar.copy, 2 * CHUNK, CHUNK, z_b[:, :, :CHUNK], "za_c")
+        h_q = []
+        for b in range(2):
+            h_q.append(quantize("h%d" % b, CHUNK, h_bf[b], H_TAGS[b]))
+            last(1, b)
+        z3_bf = round_z(nc.vector.tensor_copy, 3 * CHUNK, CHUNK, z_b[:, :, CHUNK:half], "z3_bf")
+        z2_c, z2_s = quantize("z2", CHUNK, z2_bf[:], "z2_c")
+        z3_c, z3_s = quantize("z3", CHUNK, z3_bf[:], "z3_c")
+        hidden(2, z2_c[:], z2_s[:], h_bf[2])
+        hidden(3, z3_c[:], z3_s[:], h_bf[3])
+        for b in (2, 3):
+            h_q.append(quantize("h%d" % b, CHUNK, h_bf[b], H_TAGS[b]))
+        o = [third(b, h_q[b][0], h_q[b][1]) for b in range(4)]
+        hand_on(3, o[3], (nc.vector.tensor_copy, nc.scalar.copy))
+        for b in range(3):
+            hand_on(b, o[b], (nc.scalar.copy,))
 
         for j0, n in HALVES:
             nc.sync.dma_start(out=out_words[:, j0 : j0 + n], in_=out_c[:, j0 : j0 + n].bitcast(I32))

@@ -74,8 +74,9 @@ def tile_picked_gin8_gelu_po_kernel(tc, x_words, x_scales, w1, eps, w2, res, w3_
         nc.vector.memset(w3s[:].bitcast(I32), 0)
 
         w1_rows = w1.rearrange("(p j) c -> p j c", j=PACK)
-        with nc.allow_non_contiguous_dma(reason="one value of eps for each plane"):
-            nc.scalar.dma_start(out=eps_t, in_=eps.rearrange("(p t) o -> p t o", t=PACK))
+        eps_raw = keep.tile([P, PACK, 1], F32, name="eps_raw")
+        nc.scalar.dma_start(out=eps_raw[:], in_=eps.rearrange("(p t) o -> p t o", t=PACK))
+        nc.vector.tensor_copy(out=eps_t, in_=eps_raw[:])
         xw_rows = x_words[0].rearrange("p n t -> p (n t)").bitcast(I32)
         nc.sync.dma_start(out=xw_all[:, :FIRST].bitcast(I32), in_=xw_rows[:, :FIRST])
         nc.sync.dma_start(offs_t[:], offs)

@@ -73,6 +73,10 @@ def tile_picked_gin8_gelu_po_kernel(tc, x_words, x_scales, w1, eps, w2, res, w3_
         nc.vector.memset(xs[:].bitcast(I32), 0)
         nc.vector.memset(w3s[:].bitcast(I32), 0)
 
+        warm = keep.tile([P, 2], F32, name="warm")
+        nc.vector.memset(warm[:, 0:1], 0.0)
+        nc.scalar.activation(out=warm[:, 1:2], in_=warm[:, 0:1], func=GELU)
+
         w1_rows = w1.rearrange("(p j) c -> p j c", j=PACK)
         eps_raw = keep.tile([P, PACK, 1], F32, name="eps_raw")
         nc.scalar.dma_start(out=eps_raw[:], in_=eps.rearrange("(p t) o -> p t o", t=PACK))

@@ -23,13 +23,11 @@ STRIPE = 16
 QUADS = 4
 SPREAD = 8
 PAIRS = (slice(0, 2), slice(2, 4))
-FIRST = T // 4
 LINE = 4
 CHUNK = 128
-HALVES = ((0, S // 2), (S // 2, S // 2))
+HALF = S // 2
 H_BANKS = (6, 7, 0, 1)
 O_BANKS = ((2,), (3,), (4,), (5, 6))
-H_TAGS = ("h0_c", "h1_c", "h2_c", "h3_c")
 O_TAGS = ("z", "z2_c", "o2", "o3")
 
 FLOPS = 3 * 2 * D * D * S
@@ -39,8 +37,19 @@ def tile_picked_gin8_gelu_po_kernel(tc, x_words, x_scales, w1, eps, w2, res, w3_
     nc = tc.nc
     with ExitStack() as ctx:
         keep = ctx.enter_context(tc.tile_pool(name="keep", bufs=1))
-        turn = ctx.enter_context(tc.tile_pool(name="turn", bufs=1))
         psum = ctx.enter_context(tc.psum_pool(name="psum", bufs=1))
+
+        def tile(name, shape, dtype, tag=None):
+            return keep.tile(shape, dtype, name=name, tag=tag or name, align_bytes=64)
+
+        def bank(name, number, shape):
+            return psum.tile(shape, F32, name=name, tag="bank%d" % number)
+
+        def half(u):
+            return slice(u * HALF, (u + 1) * HALF)
+
+        def places(t):
+            return slice(t * P, (t + 1) * P)
 
         def load_scale_rows(scale_tile, rows):
             nc.sync.dma_start(out=scale_tile[0:P:SPREAD, :].bitcast(I32), in_=rows.bitcast(I32))
@@ -49,187 +58,126 @@ def tile_picked_gin8_gelu_po_kernel(tc, x_words, x_scales, w1, eps, w2, res, w3_
             for g in range(QUADS):
                 queue.dma_start(out=scale_tile[32 * g : 32 * g + 4, :].bitcast(I32), in_=spread[32 * g : 32 * g + 32 : SPREAD, :].bitcast(I32))
 
-        def dealt_view(w_bf):
-            return w_bf[:].rearrange("p (t m j) -> p m j t", m=P, j=PACK)
-
-        def raw_view(w_raw):
-            return w_raw[:].rearrange("p j (m t) -> p m j t", t=PACK)
-
-        offs_t = keep.tile([P, S // STRIPE], U16, name="offs_t")
-        p1_t = keep.tile([P, S // STRIPE], U16, name="p1_t")
-        p2_t = keep.tile([P, S // STRIPE], U16, name="p2_t")
-        xs_all = keep.tile([P, T], U8, name="xs_all", tag="xs_all", align_bytes=64)
-        w3s_raw = keep.tile([P, D], U8, name="w3s_raw", align_bytes=64)
-        w3w_raw = keep.tile([P, 2 * D], U8, name="w3w_raw", align_bytes=64)
-        z_a = keep.tile([P, PACK, S // 2], F32, name="z_a", tag="z", align_bytes=64)
-        eps_t = z_a[:].rearrange("p s (h c) -> p (s h) c", h=2)[:, 1 : 1 + PACK, 0:1]
-        w1_half = [turn.tile([P, PACK, D // 2], F32, name="w1_half0", offset=0, align_bytes=64), keep.tile([P, PACK, D // 2], F32, name="w1_half1", tag="w1_half1", align_bytes=64)]
-        xw_all = keep.tile([P, T], U32, name="xw_all", align_bytes=64)
-
-        nc.vector.memset(xs_all[:].bitcast(I32), 0)
-        nc.vector.memset(w3s_raw[:].bitcast(I32), 0)
-        xs = keep.tile([P, S], U8, name="xs", align_bytes=64)
-        w3s = keep.tile([P, D], U8, name="w3s", align_bytes=64)
-        nc.vector.memset(xs[:].bitcast(I32), 0)
-        nc.vector.memset(w3s[:].bitcast(I32), 0)
-
-        warm = keep.tile([P, 2], F32, name="warm")
-        nc.vector.memset(warm[:, 0:1], 0.0)
-        nc.scalar.activation(out=warm[:, 1:2], in_=warm[:, 0:1], func=GELU)
-
-        w1_rows = w1.rearrange("(p j) c -> p j c", j=PACK)
-        eps_raw = keep.tile([P, PACK, 1], F32, name="eps_raw")
-        nc.scalar.dma_start(out=eps_raw[:], in_=eps.rearrange("(p t) o -> p t o", t=PACK))
-        nc.vector.tensor_copy(out=eps_t, in_=eps_raw[:])
-        xw_rows = x_words[0].rearrange("p n t -> p (n t)").bitcast(I32)
-        nc.sync.dma_start(out=xw_all[:, :FIRST].bitcast(I32), in_=xw_rows[:, :FIRST])
-        nc.sync.dma_start(offs_t[:], offs)
-        load_scale_rows(xs_all, x_scales[0])
-        load_scale_rows(w3s_raw, w3_scales[0])
-        nc.sync.dma_start(p1_t[:], p1)
-        nc.sync.dma_start(out=xw_all[:, FIRST:].bitcast(I32), in_=xw_rows[:, FIRST:])
-        for u in range(2):
-            nc.sync.dma_start(out=w1_half[u][:], in_=w1_rows[:, :, u * D // 2 : (u + 1) * D // 2])
-        nc.sync.dma_start(p2_t[:], p2)
-        nc.sync.dma_start(out=w3w_raw[:].bitcast(I32), in_=w3_words[0].bitcast(I32))
-
-        xs_spread = keep.tile([P, S], U8, name="xs_spread", align_bytes=64)
-        nc.vector.tensor_copy(out=xs_spread[:], in_=xs_all[:].indirect(offs_t[:]))
-        place_scale_rows(nc.scalar, xs, xs_spread)
-        w3s_spread = keep.tile([P, D], U8, name="w3s_spread", tag="xs_all", align_bytes=64)
-        nc.vector.tensor_copy(
-            out=w3s_spread[:].rearrange("p (t m) -> p t m", t=PACK),
-            in_=w3s_raw[:].rearrange("p (m t) -> p t m", t=PACK),
-        )
-        place_scale_rows(nc.sync, w3s, w3s_spread)
-
-        w1_bf = [keep.tile([P, 2 * PACK * P], BF16, name="w1_bf%d" % i, tag="w1_bf%d" % i, align_bytes=64) for i in range(2)]
-        xw = keep.tile([P, S], U32, name="xw", align_bytes=64)
-        nc.vector.tensor_copy(out=xw[:], in_=xw_all[:].indirect(offs_t[:]))
-        for u in range(2):
-            for i, copy in enumerate((nc.vector.tensor_copy, nc.scalar.copy)):
-                copy(out=dealt_view(w1_bf[i])[:, u * P // 2 : (u + 1) * P // 2], in_=raw_view(w1_half[u])[:, :, :, PAIRS[i]])
-        w1_c = keep.tile([P, D], U32, name="w1_c", align_bytes=64)
-        w1_s = keep.tile([P, D], U8, name="w1_s", align_bytes=64)
-        nc.vector.quantize_mx(out=w1_c[:, :P].bitcast(FP8X4), scales=w1_s[:, :P], in_=w1_bf[0][:, : PACK * P])
-        nc.vector.quantize_mx(out=w1_c[:, P : 2 * P].bitcast(FP8X4), scales=w1_s[:, P : 2 * P], in_=w1_bf[0][:, PACK * P :])
-        nc.vector.quantize_mx(out=w1_c[:, 2 * P :].bitcast(FP8X4), scales=w1_s[:, 2 * P :], in_=w1_bf[1][:])
-
-        w2_raw = turn.tile([P, PACK, D], F32, name="w2_raw", offset=0, align_bytes=64)
-        nc.sync.dma_start(out=w2_raw[:], in_=w2.rearrange("(p j) c -> p j c", j=PACK))
-        res_t = keep.tile([P, PACK, S], F32, name="res_t", tag="w1_half1", align_bytes=64)
-        nc.sync.dma_start(out=res_t[:], in_=res.rearrange("(p t) j -> p t j", t=PACK))
-
-        w3w = keep.tile([P, 2 * D], U8, name="w3w", tag="w1_bf1", align_bytes=64)
-        nc.vector.tensor_copy(
-            out=w3w[:].bitcast(U16).rearrange("p (t m) -> p t m", t=PACK),
-            in_=w3w_raw[:].bitcast(U16).rearrange("p (m t) -> p t m", t=PACK),
-        )
-
-        def product(out, lhs_c, lhs_s, rhs_c, rhs_s):
-            nc.tensor.matmul_mx(out=out, lhsT=lhs_c, lhsT_scale=lhs_s, rhs=rhs_c.bitcast(FP8X4), rhs_scale=rhs_s, start=True, stop=True)
-
-        def bank(name, number, shape):
-            return psum.tile(shape, F32, name=name, tag="bank%d" % number)
-
-        y_ps = []
-        for t in range(2):
-            places = slice(t * P, (t + 1) * P)
-            y_ps.append([bank("y%d_%d" % (t, u), 2 * t + u, [P, S // 2])[:] for u in range(2)])
-            for u, (j0, n) in enumerate(HALVES):
-                product(y_ps[t][u], w1_c[:, places].bitcast(FP8X4), w1_s[:, places], xw[:, j0 : j0 + n], xs[:, j0 : j0 + n])
-        plane_ps = {}
-        for t in range(2, PACK):
-            places = slice(t * P, (t + 1) * P)
-            plane_ps[t] = bank("y%d_ps" % t, t + 2, [P, S])
-            product(plane_ps[t][:], w1_c[:, places].bitcast(FP8X4), w1_s[:, places], xw[:], xs[:])
-            y_ps.append([plane_ps[t][:, j0 : j0 + n] for j0, n in HALVES])
-
-        y = [keep.tile([P, S], F32, name="y%d" % t, tag="y%d" % t, align_bytes=64) for t in range(PACK)]
-        ey = [keep.tile([P, S], F32, name="ey%d" % t, align_bytes=64) for t in range(PACK)]
-        half = S // 2
-
-        def scale_own(out, bank_ap, t):
-            nc.scalar.activation(out=out, in_=bank_ap, func=COPY, scale=eps_t[:, t, :])
-
-        nc.scalar.copy(out=y[0][:, :half], in_=y_ps[0][0])
-        scale_own(ey[0][:, :half], y_ps[0][0], 0)
-        nc.vector.tensor_copy(out=y[0][:, half:], in_=y_ps[0][1])
-        scale_own(ey[0][:, half:], y_ps[0][1], 0)
-        for u in range(2):
-            nc.scalar.copy(out=y[1][:, u * half : (u + 1) * half], in_=y_ps[1][u])
-        for u in range(2):
-            scale_own(ey[1][:, u * half : (u + 1) * half], y_ps[1][u], 1)
-        for t in range(2, PACK):
-            nc.scalar.copy(out=y[t][:], in_=plane_ps[t][:])
-            scale_own(ey[t][:], plane_ps[t][:], t)
-
-        w2_bf = keep.tile([P, PACK * D], BF16, name="w2_bf", tag="w1_bf0", align_bytes=64)
-        for pair in PAIRS:
-            nc.scalar.copy(out=dealt_view(w2_bf)[:, :, :, pair], in_=raw_view(w2_raw)[:, :, :, pair])
-        w2_c = keep.tile([P, D], U32, name="w2_c", align_bytes=64)
-        w2_s = keep.tile([P, D], U8, name="w2_s", align_bytes=64)
-
-        out_c = keep.tile([P, S], U32, name="out_c", align_bytes=64)
-        out_s = keep.tile([P, S], U8, name="out_s", align_bytes=64)
-        out_rows = out_0.rearrange("(p t) j -> p t j", t=PACK)
-        out_words = out_1[0].rearrange("p n t -> p (n t)").bitcast(I32)
+        def round_and_deal(copy, w_bf, w_raw, pair, share=slice(0, P)):
+            copy(out=w_bf.rearrange("p (t m j) -> p m j t", m=P, j=PACK)[:, share], in_=w_raw.rearrange("p j (m t) -> p m j t", t=PACK)[:, share, :, pair])
 
         def interleave(copy, dst, src):
             copy(out=dst.rearrange("p (c i t) -> p c t i", t=PACK, i=LINE), in_=src.rearrange("p t (c i) -> p c t i", i=LINE))
 
-        part = [[keep.tile([P, half], F32, name="part%d_%d" % (u, t))[:] for t in range(PACK - 2 * u)] for u in range(2)]
-        part[1].extend([ey[3][:, :half], ey[2][:, :half]])
+        def quantize_into(codes, scales, src):
+            nc.vector.quantize_mx(out=codes.bitcast(FP8X4), scales=scales, in_=src)
 
-        def look_up(out, t, list_t, j0, n, plain):
-            nc.vector.tensor_tensor(out, y[t][:].indirect(list_t[:, j0 // STRIPE : (j0 + n) // STRIPE]), plain, ADD)
-
-        def quantize(name, width, src, codes_tag):
-            codes = keep.tile([P, width], U32, name=name + "_c", tag=codes_tag, align_bytes=64)
-            scales = keep.tile([P, width], U8, name=name + "_s", align_bytes=64)
-            nc.vector.quantize_mx(out=codes[:].bitcast(FP8X4), scales=scales[:], in_=src)
+        def quantize(name, width, src):
+            codes, scales = tile(name + "_c", [P, width], U32), tile(name + "_s", [P, width], U8)
+            quantize_into(codes[:], scales[:], src)
             return codes, scales
 
-        def round_z(copy, j0, n, z, tag):
-            z_bf = keep.tile([P, PACK * n], BF16, name="z_bf%d" % j0, tag=tag, align_bytes=64)
-            interleave(copy, z_bf[:], z)
-            return z_bf
+        def product(out, lhs_c, lhs_s, rhs_c, rhs_s):
+            nc.tensor.matmul_mx(out=out, lhsT=lhs_c, lhsT_scale=lhs_s, rhs=rhs_c.bitcast(FP8X4), rhs_scale=rhs_s, start=True, stop=True)
 
-        def hidden(b, z_c, z_s, h_bf):
-            h_ps = bank("h_ps%d" % b, H_BANKS[b], [P, PACK, CHUNK])
-            for t in range(PACK):
-                places = slice(t * P, (t + 1) * P)
-                product(h_ps[:, t, :], w2_c[:, places].bitcast(FP8X4), w2_s[:, places], z_c, z_s)
-            nc.scalar.activation(out=h_bf.rearrange("p (j t) -> p j t", t=PACK), in_=h_ps[:].rearrange("p t j -> p j t"), func=GELU)
+        offs_t = keep.tile([P, S // STRIPE], U16, name="offs_t")
+        p1_t = keep.tile([P, S // STRIPE], U16, name="p1_t")
+        p2_t = keep.tile([P, S // STRIPE], U16, name="p2_t")
+        xs_all = tile("xs_all", [P, T], U8)
+        w3s_raw = tile("w3s_raw", [P, D], U8)
+        xs = tile("xs", [P, S], U8)
+        w3s = tile("w3s", [P, D], U8)
+        nc.gpsimd.memset(xs_all[:, : T // 2].bitcast(I32), 0)
+        for zeroed in (xs_all[:, T // 2 :], w3s_raw[:], xs[:], w3s[:]):
+            nc.vector.memset(zeroed.bitcast(I32), 0)
+        warm = keep.tile([P, 2], F32, name="warm")
+        nc.vector.memset(warm[:, 0:1], 0.0)
+        nc.scalar.activation(out=warm[:, 1:2], in_=warm[:, 0:1], func=GELU)
 
-        def third(b, h_c, h_s):
-            nodes = slice(b * CHUNK, (b + 1) * CHUNK)
-            o = keep.tile([P, PACK, CHUNK], F32, name="o%d" % b, tag=O_TAGS[b], align_bytes=64)
-            planes = PACK // len(O_BANKS[b])
-            for i, number in enumerate(O_BANKS[b]):
-                o_ps = bank("o_ps%d_%d" % (b, i), number, [P, planes, CHUNK])
-                for e in range(planes):
-                    t = i * planes + e
-                    product(o_ps[:, e, :], w3w[:, 2 * t * P : 2 * (t + 1) * P].bitcast(FP4X4), w3s[:, t * P : (t + 1) * P], h_c[:], h_s[:])
-                mine = slice(i * planes, (i + 1) * planes)
-                nc.vector.tensor_tensor(o[:, mine, :], o_ps[:], res_t[:, mine, nodes], ADD)
-            nc.sync.dma_start(out=out_rows[:, :, nodes], in_=o[:])
-            return o
+        z_a = tile("z_a", [P, PACK, HALF], F32, "z")
+        eps_t = z_a[:].rearrange("p s (h c) -> p (s h) c", h=2)[:, 1 : 1 + PACK, 0:1]
+        eps_raw = keep.tile([P, PACK, 1], F32, name="eps_raw")
+        nc.scalar.dma_start(out=eps_raw[:], in_=eps.rearrange("(p t) o -> p t o", t=PACK))
+        nc.vector.tensor_copy(out=eps_t, in_=eps_raw[:])
+        w1_raw = tile("w1_raw", [P, PACK, D], F32, "w_raw")
+        w1_rows = w1.rearrange("(p j) c -> p j c", j=PACK)
+        xw_all = tile("xw_all", [P, T], U32)
+        w3w_raw = tile("w3w_raw", [P, 2 * D], U8)
+        nc.sync.dma_start(out=w1_raw[:, :1, :], in_=w1_rows[:, :1, :])
+        nc.sync.dma_start(offs_t[:], offs)
+        nc.sync.dma_start(p1_t[:], p1)
+        nc.sync.dma_start(p2_t[:], p2)
+        load_scale_rows(xs_all, x_scales[0])
+        load_scale_rows(w3s_raw, w3_scales[0])
+        nc.sync.dma_start(out=w1_raw[:, 1:, :], in_=w1_rows[:, 1:, :])
+        nc.sync.dma_start(out=xw_all[:].bitcast(I32), in_=x_words[0].rearrange("p n t -> p (n t)").bitcast(I32))
+        nc.sync.dma_start(out=w3w_raw[:].bitcast(I32), in_=w3_words[0].bitcast(I32))
 
-        def hand_on(b, o, copies):
-            width = CHUNK // len(copies)
-            o_bf = [keep.tile([P, PACK * width], BF16, name="o_bf%d_%d" % (b, i), align_bytes=64) for i in range(len(copies))]
-            for i, copy in enumerate(copies):
-                interleave(copy, o_bf[i][:], o[:, :, i * width : (i + 1) * width])
-            for i in range(len(copies)):
-                cols = slice(b * CHUNK + i * width, b * CHUNK + (i + 1) * width)
-                nc.vector.quantize_mx(out=out_c[:, cols].bitcast(FP8X4), scales=out_s[:, cols], in_=o_bf[i][:])
+        xs_spread = tile("xs_spread", [P, S], U8)
+        nc.vector.tensor_copy(out=xs_spread[:], in_=xs_all[:].indirect(offs_t[:]))
+        place_scale_rows(nc.scalar, xs, xs_spread)
+        w3s_spread = tile("w3s_spread", [P, D], U8, "xs_all")
+        nc.vector.tensor_copy(out=w3s_spread[:].rearrange("p (t m) -> p t m", t=PACK), in_=w3s_raw[:].rearrange("p (m t) -> p t m", t=PACK))
+        place_scale_rows(nc.sync, w3s, w3s_spread)
+
+        w1_bf = [tile("w1_bf%d" % i, [P, 2 * PACK * P], BF16) for i in range(2)]
+        w1_c, w1_s = tile("w1_c", [P, D], U32), tile("w1_s", [P, D], U8)
+        round_and_deal(nc.vector.tensor_copy, w1_bf[0][:], w1_raw[:], PAIRS[0])
+        for i, copy in enumerate((nc.vector.tensor_copy, nc.scalar.copy)):
+            round_and_deal(copy, w1_bf[1][:], w1_raw[:], PAIRS[1], slice(i * P // 2, (i + 1) * P // 2))
+        for i in range(2):
+            quantize_into(w1_c[:, half(i)], w1_s[:, half(i)], w1_bf[i][:])
+
+        w2_raw = tile("w2_raw", [P, PACK, D], F32, "w_raw")
+        nc.sync.dma_start(out=w2_raw[:], in_=w2.rearrange("(p j) c -> p j c", j=PACK))
+        res_t = tile("res_t", [P, PACK, S], F32, "w1_bf0")
+        nc.sync.dma_start(out=res_t[:], in_=res.rearrange("(p t) j -> p t j", t=PACK))
+
+        xw = tile("xw", [P, S], U32)
+        for u in range(2):
+            nc.vector.tensor_copy(out=xw[:, half(u)], in_=xw_all[:].indirect(offs_t[:, u * HALF // STRIPE : (u + 1) * HALF // STRIPE]))
+        y_ps = {}
+        for t, u in ((0, 0), (1, 0), (0, 1), (1, 1)):
+            y_ps[t, u] = bank("y%d_%d" % (t, u), 2 * t + u, [P, HALF])[:]
+            product(y_ps[t, u], w1_c[:, places(t)].bitcast(FP8X4), w1_s[:, places(t)], xw[:, half(u)], xs[:, half(u)])
+        for t in range(2, PACK):
+            y_ps[t] = bank("y%d" % t, t + 2, [P, S])[:]
+            product(y_ps[t], w1_c[:, places(t)].bitcast(FP8X4), w1_s[:, places(t)], xw[:], xs[:])
+
+        w3w = tile("w3w", [P, 2 * D], U8, "xw_all")
+        nc.vector.tensor_copy(out=w3w[:].bitcast(U16).rearrange("p (t m) -> p t m", t=PACK), in_=w3w_raw[:].bitcast(U16).rearrange("p (m t) -> p t m", t=PACK))
+
+        y = [tile("y%d" % t, [P, S], F32) for t in range(PACK)]
+        ey = [tile("ey%d" % t, [P, S], F32) for t in range(PACK)]
+
+        def plain(t, u):
+            nc.scalar.copy(out=y[t][:, half(u)], in_=y_ps[t, u])
+
+        def scaled(t, u):
+            nc.scalar.activation(out=ey[t][:, half(u)], in_=y_ps[t, u], func=COPY, scale=eps_t[:, t, :])
+
+        plain(0, 0)
+        scaled(0, 0)
+        nc.vector.tensor_copy(out=y[0][:, half(1)], in_=y_ps[0, 1])
+        plain(1, 0)
+        scaled(1, 0)
+        scaled(0, 1)
+        plain(1, 1)
+        scaled(1, 1)
+        for t in range(2, PACK):
+            nc.scalar.copy(out=y[t][:], in_=y_ps[t])
+            nc.scalar.activation(out=ey[t][:], in_=y_ps[t], func=COPY, scale=eps_t[:, t, :])
+
+        w2_bf = tile("w2_bf", [P, PACK * D], BF16)
+        for i in range(2):
+            round_and_deal(nc.scalar.copy, w2_bf[:, i * 2 * D : (i + 1) * 2 * D], w2_raw[:], PAIRS[i])
+
+        part = [[tile("part%d_%d" % (u, t), [P, HALF], F32)[:] for t in range(PACK - 2 * u)] for u in range(2)]
+        part[1].extend([ey[3][:, half(0)], ey[2][:, half(0)]])
+
+        def look_up(out, t, list_t, j0, n, other):
+            nc.vector.tensor_tensor(out, y[t][:].indirect(list_t[:, j0 // STRIPE : (j0 + n) // STRIPE]), other, ADD)
 
         def first(u, t):
-            look_up(part[u][t], t, p1_t, u * half, half, ey[t][:, u * half : (u + 1) * half])
+            look_up(part[u][t], t, p1_t, u * HALF, HALF, ey[t][:, half(u)])
 
         def second(t):
-            look_up(z_a[:, t, :], t, p2_t, 0, half, part[0][t])
+            look_up(z_a[:, t, :], t, p2_t, 0, HALF, part[0][t])
 
         first(0, 0)
         first(1, 0)
@@ -242,41 +190,79 @@ def tile_picked_gin8_gelu_po_kernel(tc, x_words, x_scales, w1, eps, w2, res, w3_
         second(3)
         first(1, 2)
         first(1, 3)
-        nc.vector.quantize_mx(out=w2_c[:].bitcast(FP8X4), scales=w2_s[:], in_=w2_bf[:])
-        za_bf = turn.tile([P, PACK * half], BF16, name="za_bf", offset=4 * PACK * half, align_bytes=64)
+        w2_c, w2_s = quantize("w2", D, w2_bf[:])
+        za_bf = tile("za_bf", [P, PACK * HALF], BF16, "w_raw")
         interleave(nc.scalar.copy, za_bf[:], z_a[:])
-        z_b = keep.tile([P, PACK, 3 * CHUNK], F32, name="z_b", tag="z", align_bytes=64)
-        za_c, za_s = quantize("za", half, za_bf[:], "za_c")
+        z_b = tile("z_b", [P, PACK, 3 * CHUNK], F32, "z")
+        za_c, za_s = quantize("za", HALF, za_bf[:])
         for t in (2, 3):
-            look_up(z_b[:, t, :half], t, p2_t, half, half, part[1][t])
-        def last(c, t):
-            look_up(z_b[:, t, c * CHUNK : (c + 1) * CHUNK], t, p2_t, half + c * CHUNK, CHUNK, part[1][t][:, c * CHUNK : (c + 1) * CHUNK])
+            look_up(z_b[:, t, :HALF], t, p2_t, HALF, HALF, part[1][t])
 
-        h_bf = [z_b[:, b, CHUNK:].bitcast(BF16) for b in range(2)]
-        h_bf.extend([keep.tile([P, PACK * CHUNK], BF16, name="h_bf%d" % b, align_bytes=64)[:] for b in (2, 3)])
+        def last(c, t):
+            look_up(z_b[:, t, places(c)], t, p2_t, HALF + c * CHUNK, CHUNK, part[1][t][:, places(c)])
+
+        def hidden(b, z_c, z_s):
+            h_ps = bank("h_ps%d" % b, H_BANKS[b], [P, PACK, CHUNK])
+            for t in range(PACK):
+                product(h_ps[:, t, :], w2_c[:, places(t)].bitcast(FP8X4), w2_s[:, places(t)], z_c, z_s)
+            nc.scalar.activation(out=h_bf[b].rearrange("p (j t) -> p j t", t=PACK), in_=h_ps[:].rearrange("p t j -> p j t"), func=GELU)
+
+        def third(b, h_c, h_s):
+            o = tile("o%d" % b, [P, PACK, CHUNK], F32, O_TAGS[b])
+            planes = PACK // len(O_BANKS[b])
+            for i, number in enumerate(O_BANKS[b]):
+                o_ps = bank("o_ps%d_%d" % (b, i), number, [P, planes, CHUNK])
+                for e in range(planes):
+                    t = i * planes + e
+                    product(o_ps[:, e, :], w3w[:, 2 * t * P : 2 * (t + 1) * P].bitcast(FP4X4), w3s[:, places(t)], h_c[:], h_s[:])
+                mine = slice(i * planes, (i + 1) * planes)
+                nc.vector.tensor_tensor(o[:, mine, :], o_ps[:], res_t[:, mine, places(b)], ADD)
+            nc.sync.dma_start(out=out_0.rearrange("(p t) j -> p t j", t=PACK)[:, :, places(b)], in_=o[:])
+            return o
+
+        h_bf = [z_b[:, 1, CHUNK:].bitcast(BF16)] + [tile("h_bf%d" % b, [P, PACK * CHUNK], BF16)[:] for b in (1, 2, 3)]
         for t in range(2):
             last(0, t)
         for b in range(2):
-            hidden(b, za_c[:, b * CHUNK : (b + 1) * CHUNK], za_s[:, b * CHUNK : (b + 1) * CHUNK], h_bf[b])
-        z2_bf = round_z(nc.scalar.copy, 2 * CHUNK, CHUNK, z_b[:, :, :CHUNK], "za_c")
-        h_q = []
+            hidden(b, za_c[:, places(b)], za_s[:, places(b)])
         for b in range(2):
-            h_q.append(quantize("h%d" % b, CHUNK, h_bf[b], H_TAGS[b]))
-            last(1, b)
-        z3_bf = round_z(nc.vector.tensor_copy, 3 * CHUNK, CHUNK, z_b[:, :, CHUNK:half], "z3_bf")
-        z2_c, z2_s = quantize("z2", CHUNK, z2_bf[:], "z2_c")
-        z3_c, z3_s = quantize("z3", CHUNK, z3_bf[:], "z3_c")
-        hidden(2, z2_c[:], z2_s[:], h_bf[2])
-        hidden(3, z3_c[:], z3_s[:], h_bf[3])
+            product(bank("warm%d" % b, H_BANKS[b], [P, D])[:], w2_c[:, :P].bitcast(FP8X4), w2_s[:, :P], w1_c[:], w1_s[:])
+        z2_bf = tile("z2_bf", [P, PACK * CHUNK], BF16, "za_c")
+        interleave(nc.scalar.copy, z2_bf[:], z_b[:, :, :CHUNK])
+        last(1, 0)
+        h_q = [quantize("h0", CHUNK, h_bf[0])]
+        last(1, 1)
+        h_q.append(quantize("h1", CHUNK, h_bf[1]))
+        z3_bf = tile("z3_bf", [P, PACK * CHUNK], BF16)
+        for i, copy in enumerate((nc.vector.tensor_copy, nc.scalar.copy)):
+            interleave(copy, z3_bf[:, half(i)], z_b[:, :, CHUNK + i * CHUNK // 2 : CHUNK + (i + 1) * CHUNK // 2])
+        z2_c, z2_s = quantize("z2", CHUNK, z2_bf[:])
+        z3_c, z3_s = quantize("z3", CHUNK, z3_bf[:])
+        hidden(2, z2_c[:], z2_s[:])
+        hidden(3, z3_c[:], z3_s[:])
         for b in (2, 3):
-            h_q.append(quantize("h%d" % b, CHUNK, h_bf[b], H_TAGS[b]))
+            h_q.append(quantize("h%d" % b, CHUNK, h_bf[b]))
         o = [third(b, h_q[b][0], h_q[b][1]) for b in range(4)]
-        hand_on(3, o[3], (nc.vector.tensor_copy, nc.scalar.copy))
-        for b in range(3):
-            hand_on(b, o[b], (nc.scalar.copy,))
 
-        for j0, n in HALVES:
-            nc.sync.dma_start(out=out_words[:, j0 : j0 + n], in_=out_c[:, j0 : j0 + n].bitcast(I32))
+        out_c, out_s = tile("out_c", [P, S], U32), tile("out_s", [P, S], U8)
+        width = CHUNK // 2
+        o3_bf = [tile("o3_bf%d" % i, [P, PACK * width], BF16) for i in range(2)]
+        for i, copy in enumerate((nc.vector.tensor_copy, nc.scalar.copy)):
+            interleave(copy, o3_bf[i][:], o[3][:, :, i * width : (i + 1) * width])
+        for i in range(2):
+            cols = slice(3 * CHUNK + i * width, 3 * CHUNK + (i + 1) * width)
+            quantize_into(out_c[:, cols], out_s[:, cols], o3_bf[i][:])
+        o01_bf = tile("o01_bf", [P, PACK * HALF], BF16)
+        for b in range(2):
+            interleave(nc.scalar.copy, o01_bf[:, b * PACK * CHUNK : (b + 1) * PACK * CHUNK], o[b][:])
+        quantize_into(out_c[:, half(0)], out_s[:, half(0)], o01_bf[:])
+        o2_bf = tile("o2_bf", [P, PACK * CHUNK], BF16)
+        interleave(nc.scalar.copy, o2_bf[:], o[2][:])
+        quantize_into(out_c[:, places(2)], out_s[:, places(2)], o2_bf[:])
+
+        out_words = out_1[0].rearrange("p n t -> p (n t)").bitcast(I32)
+        for u in range(2):
+            nc.sync.dma_start(out=out_words[:, half(u)], in_=out_c[:, half(u)].bitcast(I32))
         for g in range(QUADS):
             queue = nc.scalar if g % 2 else nc.sync
             queue.dma_start(out=out_2[0][4 * g : 4 * g + 4, :].bitcast(I32), in_=out_s[32 * g : 32 * g + 4, :].bitcast(I32))

@@ -30,6 +30,9 @@ H_BANKS = (6, 7, 0, 1)
 O_BANKS = ((2,), (3,), (4,), (5, 6))
 O_TAGS = ("z", "z2_c", "o2", "o3")
 
+Z_B = PACK * D - CHUNK
+PITCH = HALF + CHUNK // 2
+
 FLOPS = 3 * 2 * D * D * S
 
 
@@ -82,19 +85,21 @@ def tile_picked_gin8_gelu_po_kernel(tc, x_words, x_scales, w1, eps, w2, res, w3_
         w3s_raw = tile("w3s_raw", [P, D], U8)
         xs = tile("xs", [P, S], U8)
         w3s = tile("w3s", [P, D], U8)
-        nc.gpsimd.memset(xs_all[:, : T // 2].bitcast(I32), 0)
-        for zeroed in (xs_all[:, T // 2 :], w3s_raw[:], xs[:], w3s[:]):
+        for zeroed in (xs_all[:], w3s_raw[:], xs[:], w3s[:]):
             nc.vector.memset(zeroed.bitcast(I32), 0)
         warm = keep.tile([P, 2], F32, name="warm")
         nc.vector.memset(warm[:, 0:1], 0.0)
         nc.scalar.activation(out=warm[:, 1:2], in_=warm[:, 0:1], func=GELU)
 
-        z_a = tile("z_a", [P, PACK, HALF], F32, "z")
-        eps_t = z_a[:].rearrange("p s (h c) -> p (s h) c", h=2)[:, 1 : 1 + PACK, 0:1]
+        stage = tile("stage", [P, Z_B + 3 * PITCH + 3 * CHUNK], F32, "z")
+        z_a = stage[:, PACK * D : PACK * D + PACK * HALF].rearrange("p (s c) -> p s c", s=PACK)
+        z_b = stage[:, Z_B : Z_B + PACK * PITCH].rearrange("p (s c) -> p s c", s=PACK)
+        w_raw = stage[:, : PACK * D].rearrange("p (j c) -> p j c", j=PACK)
+        eps_t = z_a.rearrange("p s (h c) -> p (s h) c", h=2)[:, 1 : 1 + PACK, 0:1]
         eps_raw = keep.tile([P, PACK, 1], F32, name="eps_raw")
         nc.scalar.dma_start(out=eps_raw[:], in_=eps.rearrange("(p t) o -> p t o", t=PACK))
         nc.vector.tensor_copy(out=eps_t, in_=eps_raw[:])
-        w1_raw = tile("w1_raw", [P, PACK, D], F32, "w_raw")
+        w1_raw = w_raw
         w1_rows = w1.rearrange("(p j) c -> p j c", j=PACK)
         xw_all = tile("xw_all", [P, T], U32)
         w3w_raw = tile("w3w_raw", [P, 2 * D], U8)
@@ -117,14 +122,14 @@ def tile_picked_gin8_gelu_po_kernel(tc, x_words, x_scales, w1, eps, w2, res, w3_
 
         w1_bf = [tile("w1_bf%d" % i, [P, 2 * PACK * P], BF16) for i in range(2)]
         w1_c, w1_s = tile("w1_c", [P, D], U32), tile("w1_s", [P, D], U8)
-        round_and_deal(nc.vector.tensor_copy, w1_bf[0][:], w1_raw[:], PAIRS[0])
+        round_and_deal(nc.vector.tensor_copy, w1_bf[0][:], w1_raw, PAIRS[0])
         for i, copy in enumerate((nc.vector.tensor_copy, nc.scalar.copy)):
-            round_and_deal(copy, w1_bf[1][:], w1_raw[:], PAIRS[1], slice(i * P // 2, (i + 1) * P // 2))
+            round_and_deal(copy, w1_bf[1][:], w1_raw, PAIRS[1], slice(i * P // 2, (i + 1) * P // 2))
         for i in range(2):
             quantize_into(w1_c[:, half(i)], w1_s[:, half(i)], w1_bf[i][:])
 
-        w2_raw = tile("w2_raw", [P, PACK, D], F32, "w_raw")
-        nc.sync.dma_start(out=w2_raw[:], in_=w2.rearrange("(p j) c -> p j c", j=PACK))
+        w2_raw = w_raw
+        nc.sync.dma_start(out=w2_raw, in_=w2.rearrange("(p j) c -> p j c", j=PACK))
         res_t = tile("res_t", [P, PACK, S], F32, "w1_bf0")
         nc.sync.dma_start(out=res_t[:], in_=res.rearrange("(p t) j -> p t j", t=PACK))
 
@@ -165,7 +170,7 @@ def tile_picked_gin8_gelu_po_kernel(tc, x_words, x_scales, w1, eps, w2, res, w3_
 
         w2_bf = tile("w2_bf", [P, PACK * D], BF16)
         for i in range(2):
-            round_and_deal(nc.scalar.copy, w2_bf[:, i * 2 * D : (i + 1) * 2 * D], w2_raw[:], PAIRS[i])
+            round_and_deal(nc.scalar.copy, w2_bf[:, i * 2 * D : (i + 1) * 2 * D], w2_raw, PAIRS[i])
 
         part = [[tile("part%d_%d" % (u, t), [P, HALF], F32)[:] for t in range(PACK - 2 * u)] for u in range(2)]
         part[1].extend([ey[3][:, half(0)], ey[2][:, half(0)]])
@@ -191,12 +196,13 @@ def tile_picked_gin8_gelu_po_kernel(tc, x_words, x_scales, w1, eps, w2, res, w3_
         first(1, 2)
         first(1, 3)
         w2_c, w2_s = quantize("w2", D, w2_bf[:])
-        za_bf = tile("za_bf", [P, PACK * HALF], BF16, "w_raw")
-        interleave(nc.scalar.copy, za_bf[:], z_a[:])
-        z_b = tile("z_b", [P, PACK, 3 * CHUNK], F32, "z")
-        za_c, za_s = quantize("za", HALF, za_bf[:])
-        for t in (2, 3):
-            look_up(z_b[:, t, :HALF], t, p2_t, HALF, HALF, part[1][t])
+        za_q = []
+        za_bf = [stage[:, b * HALF : (b + 1) * HALF].bitcast(BF16) for b in range(2)]
+        for b in range(2):
+            interleave(nc.scalar.copy, za_bf[b], z_a[:, :, places(b)])
+        for b in range(2):
+            za_q.append(quantize("z%d" % b, CHUNK, za_bf[b]))
+            look_up(z_b[:, b, :HALF], b, p2_t, HALF, HALF, part[1][b])
 
         def last(c, t):
             look_up(z_b[:, t, places(c)], t, p2_t, HALF + c * CHUNK, CHUNK, part[1][t][:, places(c)])
@@ -220,18 +226,18 @@ def tile_picked_gin8_gelu_po_kernel(tc, x_words, x_scales, w1, eps, w2, res, w3_
             nc.sync.dma_start(out=out_0.rearrange("(p t) j -> p t j", t=PACK)[:, :, places(b)], in_=o[:])
             return o
 
-        h_bf = [z_b[:, 1, CHUNK:].bitcast(BF16)] + [tile("h_bf%d" % b, [P, PACK * CHUNK], BF16)[:] for b in (1, 2, 3)]
-        for t in range(2):
+        h_bf = [stage[:, Z_B + 3 * PITCH + CHUNK :].bitcast(BF16)] + [tile("h_bf%d" % b, [P, PACK * CHUNK], BF16)[:] for b in (1, 2, 3)]
+        for t in (2, 3):
             last(0, t)
         for b in range(2):
-            hidden(b, za_c[:, places(b)], za_s[:, places(b)])
+            hidden(b, za_q[b][0][:], za_q[b][1][:])
         for b in range(2):
             product(bank("warm%d" % b, H_BANKS[b], [P, D])[:], w2_c[:, :P].bitcast(FP8X4), w2_s[:, :P], w1_c[:], w1_s[:])
-        z2_bf = tile("z2_bf", [P, PACK * CHUNK], BF16, "za_c")
+        z2_bf = tile("z2_bf", [P, PACK * CHUNK], BF16, "z1_c")
         interleave(nc.scalar.copy, z2_bf[:], z_b[:, :, :CHUNK])
-        last(1, 0)
+        last(1, 2)
         h_q = [quantize("h0", CHUNK, h_bf[0])]
-        last(1, 1)
+        last(1, 3)
         h_q.append(quantize("h1", CHUNK, h_bf[1]))
         z3_bf = tile("z3_bf", [P, PACK * CHUNK], BF16)
         for i, copy in enumerate((nc.vector.tensor_copy, nc.scalar.copy)):

@@ -26,8 +26,9 @@ PAIRS = (slice(0, 2), slice(2, 4))
 LINE = 4
 CHUNK = 128
 HALF = S // 2
+FIRST = T // 4
 H_BANKS = (6, 7, 0, 1)
-O_BANKS = ((2,), (3,), (4,), (5, 6))
+O_BANKS = ((2,), (3,), (4, 7), (5, 6))
 O_TAGS = ("z", "z2_c", "o2", "o3")
 
 Z_B = PACK * D - CHUNK
@@ -62,7 +63,7 @@ def tile_picked_gin8_gelu_po_kernel(tc, x_words, x_scales, w1, eps, w2, res, w3_
                 queue.dma_start(out=scale_tile[32 * g : 32 * g + 4, :].bitcast(I32), in_=spread[32 * g : 32 * g + 32 : SPREAD, :].bitcast(I32))
 
         def round_and_deal(copy, w_bf, w_raw, pair, share=slice(0, P)):
-            copy(out=w_bf.rearrange("p (t m j) -> p m j t", m=P, j=PACK)[:, share], in_=w_raw.rearrange("p j (m t) -> p m j t", t=PACK)[:, share, :, pair])
+            copy(out=w_bf.rearrange("p (t m j) -> p m j t", m=P, j=PACK)[:, share], in_=w_raw.rearrange("p j (m t) -> p m j t", t=PACK)[:, :, :, pair])
 
         def interleave(copy, dst, src):
             copy(out=dst.rearrange("p (c i t) -> p c t i", t=PACK, i=LINE), in_=src.rearrange("p t (c i) -> p c t i", i=LINE))
@@ -95,22 +96,23 @@ def tile_picked_gin8_gelu_po_kernel(tc, x_words, x_scales, w1, eps, w2, res, w3_
         z_a = stage[:, PACK * D : PACK * D + PACK * HALF].rearrange("p (s c) -> p s c", s=PACK)
         z_b = stage[:, Z_B : Z_B + PACK * PITCH].rearrange("p (s c) -> p s c", s=PACK)
         w_raw = stage[:, : PACK * D].rearrange("p (j c) -> p j c", j=PACK)
-        eps_t = z_a.rearrange("p s (h c) -> p (s h) c", h=2)[:, 1 : 1 + PACK, 0:1]
         eps_raw = keep.tile([P, PACK, 1], F32, name="eps_raw")
         nc.scalar.dma_start(out=eps_raw[:], in_=eps.rearrange("(p t) o -> p t o", t=PACK))
-        nc.vector.tensor_copy(out=eps_t, in_=eps_raw[:])
-        w1_raw = w_raw
+        nc.vector.tensor_copy(out=z_a[:, 0:3:2, 0:1], in_=eps_raw[:, 0:4:3, :])
+        w1_half = [stage[:, : PACK * HALF].rearrange("p (j c) -> p j c", j=PACK), tile("w1_half1", [P, PACK, HALF], F32)[:]]
         w1_rows = w1.rearrange("(p j) c -> p j c", j=PACK)
         xw_all = tile("xw_all", [P, T], U32)
+        xw_rows = x_words[0].rearrange("p n t -> p (n t)").bitcast(I32)
         w3w_raw = tile("w3w_raw", [P, 2 * D], U8)
-        nc.sync.dma_start(out=w1_raw[:, :1, :], in_=w1_rows[:, :1, :])
+        nc.sync.dma_start(out=xw_all[:, :FIRST].bitcast(I32), in_=xw_rows[:, :FIRST])
         nc.sync.dma_start(offs_t[:], offs)
-        nc.sync.dma_start(p1_t[:], p1)
-        nc.sync.dma_start(p2_t[:], p2)
         load_scale_rows(xs_all, x_scales[0])
         load_scale_rows(w3s_raw, w3_scales[0])
-        nc.sync.dma_start(out=w1_raw[:, 1:, :], in_=w1_rows[:, 1:, :])
-        nc.sync.dma_start(out=xw_all[:].bitcast(I32), in_=x_words[0].rearrange("p n t -> p (n t)").bitcast(I32))
+        nc.sync.dma_start(p1_t[:], p1)
+        nc.sync.dma_start(out=xw_all[:, FIRST:].bitcast(I32), in_=xw_rows[:, FIRST:])
+        for u in range(2):
+            nc.sync.dma_start(out=w1_half[u], in_=w1_rows[:, :, half(u)])
+        nc.sync.dma_start(p2_t[:], p2)
         nc.sync.dma_start(out=w3w_raw[:].bitcast(I32), in_=w3_words[0].bitcast(I32))
 
         xs_spread = tile("xs_spread", [P, S], U8)
@@ -120,55 +122,58 @@ def tile_picked_gin8_gelu_po_kernel(tc, x_words, x_scales, w1, eps, w2, res, w3_
         nc.vector.tensor_copy(out=w3s_spread[:].rearrange("p (t m) -> p t m", t=PACK), in_=w3s_raw[:].rearrange("p (m t) -> p t m", t=PACK))
         place_scale_rows(nc.sync, w3s, w3s_spread)
 
+        xw = tile("xw", [P, S], U32)
+        nc.vector.tensor_copy(out=xw[:], in_=xw_all[:].indirect(offs_t[:]))
         w1_bf = [tile("w1_bf%d" % i, [P, 2 * PACK * P], BF16) for i in range(2)]
         w1_c, w1_s = tile("w1_c", [P, D], U32), tile("w1_s", [P, D], U8)
-        round_and_deal(nc.vector.tensor_copy, w1_bf[0][:], w1_raw, PAIRS[0])
-        for i, copy in enumerate((nc.vector.tensor_copy, nc.scalar.copy)):
-            round_and_deal(copy, w1_bf[1][:], w1_raw, PAIRS[1], slice(i * P // 2, (i + 1) * P // 2))
-        for i in range(2):
-            quantize_into(w1_c[:, half(i)], w1_s[:, half(i)], w1_bf[i][:])
+        for u in range(2):
+            for i, copy in enumerate((nc.vector.tensor_copy, nc.scalar.copy)):
+                round_and_deal(copy, w1_bf[i][:], w1_half[u], PAIRS[i], slice(u * P // 2, (u + 1) * P // 2))
+        for t in range(2):
+            quantize_into(w1_c[:, places(t)], w1_s[:, places(t)], w1_bf[0][:, t * PACK * P : (t + 1) * PACK * P])
+        quantize_into(w1_c[:, half(1)], w1_s[:, half(1)], w1_bf[1][:])
 
         w2_raw = w_raw
         nc.sync.dma_start(out=w2_raw, in_=w2.rearrange("(p j) c -> p j c", j=PACK))
-        res_t = tile("res_t", [P, PACK, S], F32, "w1_bf0")
+        res_t = tile("res_t", [P, PACK, S], F32, "w1_half1")
         nc.sync.dma_start(out=res_t[:], in_=res.rearrange("(p t) j -> p t j", t=PACK))
 
-        xw = tile("xw", [P, S], U32)
-        for u in range(2):
-            nc.vector.tensor_copy(out=xw[:, half(u)], in_=xw_all[:].indirect(offs_t[:, u * HALF // STRIPE : (u + 1) * HALF // STRIPE]))
+        w3w = tile("w3w", [P, 2 * D], U8, "w1_bf1")
+        nc.vector.tensor_copy(out=w3w[:].bitcast(U16).rearrange("p (t m) -> p t m", t=PACK), in_=w3w_raw[:].bitcast(U16).rearrange("p (m t) -> p t m", t=PACK))
+
         y_ps = {}
-        for t, u in ((0, 0), (1, 0), (0, 1), (1, 1)):
-            y_ps[t, u] = bank("y%d_%d" % (t, u), 2 * t + u, [P, HALF])[:]
-            product(y_ps[t, u], w1_c[:, places(t)].bitcast(FP8X4), w1_s[:, places(t)], xw[:, half(u)], xs[:, half(u)])
+        for t in range(2):
+            for u in range(2):
+                y_ps[t, u] = bank("y%d_%d" % (t, u), 2 * t + u, [P, HALF])[:]
+                product(y_ps[t, u], w1_c[:, places(t)].bitcast(FP8X4), w1_s[:, places(t)], xw[:, half(u)], xs[:, half(u)])
         for t in range(2, PACK):
             y_ps[t] = bank("y%d" % t, t + 2, [P, S])[:]
             product(y_ps[t], w1_c[:, places(t)].bitcast(FP8X4), w1_s[:, places(t)], xw[:], xs[:])
-
-        w3w = tile("w3w", [P, 2 * D], U8, "xw_all")
-        nc.vector.tensor_copy(out=w3w[:].bitcast(U16).rearrange("p (t m) -> p t m", t=PACK), in_=w3w_raw[:].bitcast(U16).rearrange("p (m t) -> p t m", t=PACK))
+            for u in range(2):
+                y_ps[t, u] = y_ps[t][:, half(u)]
 
         y = [tile("y%d" % t, [P, S], F32) for t in range(PACK)]
         ey = [tile("ey%d" % t, [P, S], F32) for t in range(PACK)]
 
-        def plain(t, u):
-            nc.scalar.copy(out=y[t][:, half(u)], in_=y_ps[t, u])
+        def scaled(t, u, factor):
+            nc.scalar.activation(out=ey[t][:, half(u)], in_=y_ps[t, u], func=COPY, scale=factor)
 
-        def scaled(t, u):
-            nc.scalar.activation(out=ey[t][:, half(u)], in_=y_ps[t, u], func=COPY, scale=eps_t[:, t, :])
-
-        plain(0, 0)
-        scaled(0, 0)
+        nc.scalar.copy(out=y[0][:, half(0)], in_=y_ps[0, 0])
+        scaled(0, 0, eps_raw[:, 0, :])
         nc.vector.tensor_copy(out=y[0][:, half(1)], in_=y_ps[0, 1])
-        plain(1, 0)
-        scaled(1, 0)
-        scaled(0, 1)
-        plain(1, 1)
-        scaled(1, 1)
-        for t in range(2, PACK):
-            nc.scalar.copy(out=y[t][:], in_=y_ps[t])
-            nc.scalar.activation(out=ey[t][:], in_=y_ps[t], func=COPY, scale=eps_t[:, t, :])
+        scaled(0, 1, z_a[:, 0, 0:1])
+        for u in range(2):
+            nc.scalar.copy(out=y[1][:, half(u)], in_=y_ps[1, u])
+        for u in range(2):
+            scaled(1, u, eps_raw[:, 1, :])
+        nc.scalar.copy(out=y[2][:], in_=y_ps[2])
+        scaled(2, 0, eps_raw[:, 2, :])
+        nc.scalar.copy(out=y[3][:], in_=y_ps[3])
+        scaled(3, 0, z_a[:, 2, 0:1])
+        for t in (2, 3):
+            scaled(t, 1, eps_raw[:, t, :])
 
-        w2_bf = tile("w2_bf", [P, PACK * D], BF16)
+        w2_bf = tile("w2_bf", [P, PACK * D], BF16, "w1_bf0")
         for i in range(2):
             round_and_deal(nc.scalar.copy, w2_bf[:, i * 2 * D : (i + 1) * 2 * D], w2_raw, PAIRS[i])
 
@@ -184,17 +189,13 @@ def tile_picked_gin8_gelu_po_kernel(tc, x_words, x_scales, w1, eps, w2, res, w3_
         def second(t):
             look_up(z_a[:, t, :], t, p2_t, 0, HALF, part[0][t])
 
-        first(0, 0)
-        first(1, 0)
-        second(0)
-        first(0, 1)
-        first(1, 1)
-        for t in range(2, PACK):
+        for t in range(2):
             first(0, t)
-            second(t - 1)
-        second(3)
-        first(1, 2)
-        first(1, 3)
+            first(1, t)
+            second(t)
+        for step in (lambda t: first(0, t), second, lambda t: first(1, t)):
+            for t in (2, 3):
+                step(t)
         w2_c, w2_s = quantize("w2", D, w2_bf[:])
         za_q = []
         za_bf = [stage[:, b * HALF : (b + 1) * HALF].bitcast(BF16) for b in range(2)]
@@ -232,7 +233,7 @@ def tile_picked_gin8_gelu_po_kernel(tc, x_words, x_scales, w1, eps, w2, res, w3_
         for b in range(2):
             hidden(b, za_q[b][0][:], za_q[b][1][:])
         for b in range(2):
-            product(bank("warm%d" % b, H_BANKS[b], [P, D])[:], w2_c[:, :P].bitcast(FP8X4), w2_s[:, :P], w1_c[:], w1_s[:])
+            product(bank("warm%d" % b, H_BANKS[b], [P, D])[:], w2_c[:, :P].bitcast(FP8X4), w2_s[:, :P], xw[:], xs[:])
         z2_bf = tile("z2_bf", [P, PACK * CHUNK], BF16, "z1_c")
         interleave(nc.scalar.copy, z2_bf[:], z_b[:, :, :CHUNK])
         last(1, 2)

@@ -25,14 +25,11 @@ SPREAD = 8
 PAIRS = (slice(0, 2), slice(2, 4))
 LINE = 4
 CHUNK = 128
+CHUNKS = S // CHUNK
 HALF = S // 2
 FIRST = T // 4
 H_BANKS = (6, 7, 0, 1)
-O_BANKS = ((2,), (3,), (4, 7), (5, 6))
-O_TAGS = ("z", "z2_c", "o2", "o3")
-
-Z_B = PACK * D - CHUNK
-PITCH = HALF + CHUNK // 2
+O_BANKS = ((2,), (3,), (4,), (5, 6))
 
 FLOPS = 3 * 2 * D * D * S
 
@@ -65,8 +62,14 @@ def tile_picked_gin8_gelu_po_kernel(tc, x_words, x_scales, w1, eps, w2, res, w3_
         def round_and_deal(copy, w_bf, w_raw, pair, share=slice(0, P)):
             copy(out=w_bf.rearrange("p (t m j) -> p m j t", m=P, j=PACK)[:, share], in_=w_raw.rearrange("p j (m t) -> p m j t", t=PACK)[:, :, :, pair])
 
+        def woven(dst, run=LINE):
+            return dst.rearrange("p (c i t) -> p c t i", t=PACK, i=run)
+
+        def by_runs(src, run=LINE):
+            return src.rearrange("p t (c i) -> p c t i", i=run)
+
         def interleave(copy, dst, src):
-            copy(out=dst.rearrange("p (c i t) -> p c t i", t=PACK, i=LINE), in_=src.rearrange("p t (c i) -> p c t i", i=LINE))
+            copy(out=woven(dst), in_=by_runs(src))
 
         def quantize_into(codes, scales, src):
             nc.vector.quantize_mx(out=codes.bitcast(FP8X4), scales=scales, in_=src)
@@ -92,14 +95,9 @@ def tile_picked_gin8_gelu_po_kernel(tc, x_words, x_scales, w1, eps, w2, res, w3_
         nc.vector.memset(warm[:, 0:1], 0.0)
         nc.scalar.activation(out=warm[:, 1:2], in_=warm[:, 0:1], func=GELU)
 
-        stage = tile("stage", [P, Z_B + 3 * PITCH + 3 * CHUNK], F32, "z")
-        z_a = stage[:, PACK * D : PACK * D + PACK * HALF].rearrange("p (s c) -> p s c", s=PACK)
-        z_b = stage[:, Z_B : Z_B + PACK * PITCH].rearrange("p (s c) -> p s c", s=PACK)
-        w_raw = stage[:, : PACK * D].rearrange("p (j c) -> p j c", j=PACK)
-        eps_raw = keep.tile([P, PACK, 1], F32, name="eps_raw")
-        nc.scalar.dma_start(out=eps_raw[:], in_=eps.rearrange("(p t) o -> p t o", t=PACK))
-        nc.vector.tensor_copy(out=z_a[:, 0:3:2, 0:1], in_=eps_raw[:, 0:4:3, :])
-        w1_half = [stage[:, : PACK * HALF].rearrange("p (j c) -> p j c", j=PACK), tile("w1_half1", [P, PACK, HALF], F32)[:]]
+        eps_t = keep.tile([P, PACK, 1], F32, name="eps_t")
+        nc.scalar.dma_start(out=eps_t[:], in_=eps.rearrange("(p t) o -> p t o", t=PACK))
+        w1_half = [tile("w1_half%d" % u, [P, PACK, HALF], F32) for u in range(2)]
         w1_rows = w1.rearrange("(p j) c -> p j c", j=PACK)
         xw_all = tile("xw_all", [P, T], U32)
         xw_rows = x_words[0].rearrange("p n t -> p (n t)").bitcast(I32)
@@ -111,7 +109,7 @@ def tile_picked_gin8_gelu_po_kernel(tc, x_words, x_scales, w1, eps, w2, res, w3_
         nc.sync.dma_start(p1_t[:], p1)
         nc.sync.dma_start(out=xw_all[:, FIRST:].bitcast(I32), in_=xw_rows[:, FIRST:])
         for u in range(2):
-            nc.sync.dma_start(out=w1_half[u], in_=w1_rows[:, :, half(u)])
+            nc.sync.dma_start(out=w1_half[u][:], in_=w1_rows[:, :, half(u)])
         nc.sync.dma_start(p2_t[:], p2)
         nc.sync.dma_start(out=w3w_raw[:].bitcast(I32), in_=w3_words[0].bitcast(I32))
 
@@ -128,94 +126,75 @@ def tile_picked_gin8_gelu_po_kernel(tc, x_words, x_scales, w1, eps, w2, res, w3_
         w1_c, w1_s = tile("w1_c", [P, D], U32), tile("w1_s", [P, D], U8)
         for u in range(2):
             for i, copy in enumerate((nc.vector.tensor_copy, nc.scalar.copy)):
-                round_and_deal(copy, w1_bf[i][:], w1_half[u], PAIRS[i], slice(u * P // 2, (u + 1) * P // 2))
+                round_and_deal(copy, w1_bf[i][:], w1_half[u][:], PAIRS[i], slice(u * P // 2, (u + 1) * P // 2))
         for t in range(2):
             quantize_into(w1_c[:, places(t)], w1_s[:, places(t)], w1_bf[0][:, t * PACK * P : (t + 1) * PACK * P])
         quantize_into(w1_c[:, half(1)], w1_s[:, half(1)], w1_bf[1][:])
 
-        w2_raw = w_raw
-        nc.sync.dma_start(out=w2_raw, in_=w2.rearrange("(p j) c -> p j c", j=PACK))
+        w2_raw = tile("w2_raw", [P, PACK, D], F32, "w1_half0")
+        nc.sync.dma_start(out=w2_raw[:], in_=w2.rearrange("(p j) c -> p j c", j=PACK))
         res_t = tile("res_t", [P, PACK, S], F32, "w1_half1")
         nc.sync.dma_start(out=res_t[:], in_=res.rearrange("(p t) j -> p t j", t=PACK))
 
         w3w = tile("w3w", [P, 2 * D], U8, "w1_bf1")
         nc.vector.tensor_copy(out=w3w[:].bitcast(U16).rearrange("p (t m) -> p t m", t=PACK), in_=w3w_raw[:].bitcast(U16).rearrange("p (m t) -> p t m", t=PACK))
 
-        y_ps = {}
-        for t in range(2):
-            for u in range(2):
-                y_ps[t, u] = bank("y%d_%d" % (t, u), 2 * t + u, [P, HALF])[:]
-                product(y_ps[t, u], w1_c[:, places(t)].bitcast(FP8X4), w1_s[:, places(t)], xw[:, half(u)], xs[:, half(u)])
-        for t in range(2, PACK):
-            y_ps[t] = bank("y%d" % t, t + 2, [P, S])[:]
-            product(y_ps[t], w1_c[:, places(t)].bitcast(FP8X4), w1_s[:, places(t)], xw[:], xs[:])
-            for u in range(2):
-                y_ps[t, u] = y_ps[t][:, half(u)]
-
         y = [tile("y%d" % t, [P, S], F32) for t in range(PACK)]
         ey = [tile("ey%d" % t, [P, S], F32) for t in range(PACK)]
-
-        def scaled(t, u, factor):
-            nc.scalar.activation(out=ey[t][:, half(u)], in_=y_ps[t, u], func=COPY, scale=factor)
-
-        nc.scalar.copy(out=y[0][:, half(0)], in_=y_ps[0, 0])
-        scaled(0, 0, eps_raw[:, 0, :])
-        nc.vector.tensor_copy(out=y[0][:, half(1)], in_=y_ps[0, 1])
-        scaled(0, 1, z_a[:, 0, 0:1])
+        y0_ps = [bank("y0_%d" % u, u, [P, HALF]) for u in range(2)]
         for u in range(2):
-            nc.scalar.copy(out=y[1][:, half(u)], in_=y_ps[1, u])
+            product(y0_ps[u][:], w1_c[:, places(0)].bitcast(FP8X4), w1_s[:, places(0)], xw[:, half(u)], xs[:, half(u)])
         for u in range(2):
-            scaled(1, u, eps_raw[:, 1, :])
-        nc.scalar.copy(out=y[2][:], in_=y_ps[2])
-        scaled(2, 0, eps_raw[:, 2, :])
-        nc.scalar.copy(out=y[3][:], in_=y_ps[3])
-        scaled(3, 0, z_a[:, 2, 0:1])
-        for t in (2, 3):
-            scaled(t, 1, eps_raw[:, t, :])
+            nc.scalar.copy(out=y[0][:, half(u)], in_=y0_ps[u][:])
+        for u in range(2):
+            nc.scalar.activation(out=ey[0][:, half(u)], in_=y0_ps[u][:], func=COPY, scale=eps_t[:, 0, :])
+        for t in range(1, PACK):
+            y_ps = bank("y%d" % t, t + 1, [P, S])
+            product(y_ps[:], w1_c[:, places(t)].bitcast(FP8X4), w1_s[:, places(t)], xw[:], xs[:])
+            nc.scalar.copy(out=y[t][:], in_=y_ps[:])
+            nc.scalar.activation(out=ey[t][:], in_=y_ps[:], func=COPY, scale=eps_t[:, t, :])
 
-        w2_bf = tile("w2_bf", [P, PACK * D], BF16, "w1_bf0")
+        def entries(list_t, cols):
+            return list_t[:, cols.start // STRIPE : cols.stop // STRIPE]
+
+        w2_bf = tile("w2_bf", [P, PACK * D], BF16)
         for i in range(2):
-            round_and_deal(nc.scalar.copy, w2_bf[:, i * 2 * D : (i + 1) * 2 * D], w2_raw, PAIRS[i])
+            round_and_deal(nc.vector.tensor_copy, w2_bf[:, i * 2 * D : (i + 1) * 2 * D], w2_raw[:], PAIRS[i])
 
-        part = [[tile("part%d_%d" % (u, t), [P, HALF], F32)[:] for t in range(PACK - 2 * u)] for u in range(2)]
-        part[1].extend([ey[3][:, half(0)], ey[2][:, half(0)]])
+        own = [tile("own%d" % u, [P, PACK, HALF], F32) for u in range(2)]
+        for t in range(PACK):
+            for u in range(2):
+                nc.vector.tensor_tensor(own[u][:, t, :], y[t][:].indirect(entries(p1_t, half(u))), ey[t][:, half(u)], ADD)
+            if t == 0:
+                w2_c, w2_s = quantize("w2", D, w2_bf[:])
 
-        def look_up(out, t, list_t, j0, n, other):
-            nc.vector.tensor_tensor(out, y[t][:].indirect(list_t[:, j0 // STRIPE : (j0 + n) // STRIPE]), other, ADD)
+        stretches = (half(0), places(2), places(3))
+        other = []
+        for n, cols in enumerate(stretches):
+            got = tile("other%d" % n, [P, PACK, cols.stop - cols.start], F32)
+            for t in range(PACK):
+                nc.scalar.activation(got[:, t, :], y[t][:].indirect(entries(p2_t, cols)), COPY)
+            other.extend(got[:, :, places(c)] for c in range((cols.stop - cols.start) // CHUNK))
 
-        def first(u, t):
-            look_up(part[u][t], t, p1_t, u * HALF, HALF, ey[t][:, half(u)])
+        z_bf = [tile("z_bf%d" % b, [P, PACK * CHUNK], BF16) for b in range(CHUNKS)]
+        h_bf = [tile("h_bf%d" % b, [P, PACK * CHUNK], BF16) for b in range(CHUNKS)]
 
-        def second(t):
-            look_up(z_a[:, t, :], t, p2_t, 0, HALF, part[0][t])
-
-        for t in range(2):
-            first(0, t)
-            first(1, t)
-            second(t)
-        for step in (lambda t: first(0, t), second, lambda t: first(1, t)):
-            for t in (2, 3):
-                step(t)
-        w2_c, w2_s = quantize("w2", D, w2_bf[:])
-        za_q = []
-        za_bf = [stage[:, b * HALF : (b + 1) * HALF].bitcast(BF16) for b in range(2)]
-        for b in range(2):
-            interleave(nc.scalar.copy, za_bf[b], z_a[:, :, places(b)])
-        for b in range(2):
-            za_q.append(quantize("z%d" % b, CHUNK, za_bf[b]))
-            look_up(z_b[:, b, :HALF], b, p2_t, HALF, HALF, part[1][b])
-
-        def last(c, t):
-            look_up(z_b[:, t, places(c)], t, p2_t, HALF + c * CHUNK, CHUNK, part[1][t][:, places(c)])
-
-        def hidden(b, z_c, z_s):
+        def hidden(b):
+            z_c, z_s = quantize("z%d" % b, CHUNK, z_bf[b][:])
             h_ps = bank("h_ps%d" % b, H_BANKS[b], [P, PACK, CHUNK])
             for t in range(PACK):
-                product(h_ps[:, t, :], w2_c[:, places(t)].bitcast(FP8X4), w2_s[:, places(t)], z_c, z_s)
-            nc.scalar.activation(out=h_bf[b].rearrange("p (j t) -> p j t", t=PACK), in_=h_ps[:].rearrange("p t j -> p j t"), func=GELU)
+                product(h_ps[:, t, :], w2_c[:, places(t)].bitcast(FP8X4), w2_s[:, places(t)], z_c[:], z_s[:])
+            nc.scalar.activation(out=h_bf[b][:].rearrange("p (j t) -> p j t", t=PACK), in_=h_ps[:].rearrange("p t j -> p j t"), func=GELU)
+
+        for u in range(2):
+            for c in range(2):
+                b = 2 * u + c
+                nc.vector.tensor_tensor(woven(z_bf[b][:], 2), by_runs(own[u][:, :, places(c)], 2), by_runs(other[b], 2), ADD)
+            for c in range(2):
+                hidden(2 * u + c)
 
         def third(b, h_c, h_s):
-            o = tile("o%d" % b, [P, PACK, CHUNK], F32, O_TAGS[b])
+            o = tile("o%d" % b, [P, PACK, CHUNK], F32)
             planes = PACK // len(O_BANKS[b])
             for i, number in enumerate(O_BANKS[b]):
                 o_ps = bank("o_ps%d_%d" % (b, i), number, [P, planes, CHUNK])
@@ -227,31 +206,14 @@ def tile_picked_gin8_gelu_po_kernel(tc, x_words, x_scales, w1, eps, w2, res, w3_
             nc.sync.dma_start(out=out_0.rearrange("(p t) j -> p t j", t=PACK)[:, :, places(b)], in_=o[:])
             return o
 
-        h_bf = [stage[:, Z_B + 3 * PITCH + CHUNK :].bitcast(BF16)] + [tile("h_bf%d" % b, [P, PACK * CHUNK], BF16)[:] for b in (1, 2, 3)]
-        for t in (2, 3):
-            last(0, t)
-        for b in range(2):
-            hidden(b, za_q[b][0][:], za_q[b][1][:])
-        for b in range(2):
-            product(bank("warm%d" % b, H_BANKS[b], [P, D])[:], w2_c[:, :P].bitcast(FP8X4), w2_s[:, :P], xw[:], xs[:])
-        z2_bf = tile("z2_bf", [P, PACK * CHUNK], BF16, "z1_c")
-        interleave(nc.scalar.copy, z2_bf[:], z_b[:, :, :CHUNK])
-        last(1, 2)
-        h_q = [quantize("h0", CHUNK, h_bf[0])]
-        last(1, 3)
-        h_q.append(quantize("h1", CHUNK, h_bf[1]))
-        z3_bf = tile("z3_bf", [P, PACK * CHUNK], BF16)
-        for i, copy in enumerate((nc.vector.tensor_copy, nc.scalar.copy)):
-            interleave(copy, z3_bf[:, half(i)], z_b[:, :, CHUNK + i * CHUNK // 2 : CHUNK + (i + 1) * CHUNK // 2])
-        z2_c, z2_s = quantize("z2", CHUNK, z2_bf[:])
-        z3_c, z3_s = quantize("z3", CHUNK, z3_bf[:])
-        hidden(2, z2_c[:], z2_s[:])
-        hidden(3, z3_c[:], z3_s[:])
-        for b in (2, 3):
-            h_q.append(quantize("h%d" % b, CHUNK, h_bf[b]))
-        o = [third(b, h_q[b][0], h_q[b][1]) for b in range(4)]
+        h_q = [quantize("h%d" % b, CHUNK, h_bf[b][:]) for b in range(CHUNKS)]
+        o = [third(b, h_q[b][0], h_q[b][1]) for b in range(CHUNKS)]
 
         out_c, out_s = tile("out_c", [P, S], U32), tile("out_s", [P, S], U8)
+        for b in range(CHUNKS - 1):
+            o_bf = tile("o_bf%d" % b, [P, PACK * CHUNK], BF16)
+            interleave(nc.scalar.copy, o_bf[:], o[b][:])
+            quantize_into(out_c[:, places(b)], out_s[:, places(b)], o_bf[:])
         width = CHUNK // 2
         o3_bf = [tile("o3_bf%d" % i, [P, PACK * width], BF16) for i in range(2)]
         for i, copy in enumerate((nc.vector.tensor_copy, nc.scalar.copy)):
@@ -259,13 +221,6 @@ def tile_picked_gin8_gelu_po_kernel(tc, x_words, x_scales, w1, eps, w2, res, w3_
         for i in range(2):
             cols = slice(3 * CHUNK + i * width, 3 * CHUNK + (i + 1) * width)
             quantize_into(out_c[:, cols], out_s[:, cols], o3_bf[i][:])
-        o01_bf = tile("o01_bf", [P, PACK * HALF], BF16)
-        for b in range(2):
-            interleave(nc.scalar.copy, o01_bf[:, b * PACK * CHUNK : (b + 1) * PACK * CHUNK], o[b][:])
-        quantize_into(out_c[:, half(0)], out_s[:, half(0)], o01_bf[:])
-        o2_bf = tile("o2_bf", [P, PACK * CHUNK], BF16)
-        interleave(nc.scalar.copy, o2_bf[:], o[2][:])
-        quantize_into(out_c[:, places(2)], out_s[:, places(2)], o2_bf[:])
 
         out_words = out_1[0].rearrange("p n t -> p (n t)").bitcast(I32)
         for u in range(2):

@@ -168,6 +168,7 @@ def tile_picked_gin8_gelu_po_kernel(tc, x_words, x_scales, w1, eps, w2, res, w3_
             if t == 0:
                 w2_c, w2_s = quantize("w2", D, w2_bf[:])
 
+        product(bank("warm", O_BANKS[0][0], [P, D])[:], w2_c[:, :P].bitcast(FP8X4), w2_s[:, :P], w2_c[:], w2_s[:])
         stretches = (half(0), places(2), places(3))
         other = []
         for n, cols in enumerate(stretches):
@@ -179,6 +180,9 @@ def tile_picked_gin8_gelu_po_kernel(tc, x_words, x_scales, w1, eps, w2, res, w3_
         z_bf = [tile("z_bf%d" % b, [P, PACK * CHUNK], BF16) for b in range(CHUNKS)]
         h_bf = [tile("h_bf%d" % b, [P, PACK * CHUNK], BF16) for b in range(CHUNKS)]
 
+        def summed(b):
+            nc.vector.tensor_tensor(woven(z_bf[b][:], 2), by_runs(own[b // 2][:, :, places(b % 2)], 2), by_runs(other[b], 2), ADD)
+
         def hidden(b):
             z_c, z_s = quantize("z%d" % b, CHUNK, z_bf[b][:])
             h_ps = bank("h_ps%d" % b, H_BANKS[b], [P, PACK, CHUNK])
@@ -186,32 +190,44 @@ def tile_picked_gin8_gelu_po_kernel(tc, x_words, x_scales, w1, eps, w2, res, w3_
                 product(h_ps[:, t, :], w2_c[:, places(t)].bitcast(FP8X4), w2_s[:, places(t)], z_c[:], z_s[:])
             nc.scalar.activation(out=h_bf[b][:].rearrange("p (j t) -> p j t", t=PACK), in_=h_ps[:].rearrange("p t j -> p j t"), func=GELU)
 
-        for u in range(2):
-            for c in range(2):
-                b = 2 * u + c
-                nc.vector.tensor_tensor(woven(z_bf[b][:], 2), by_runs(own[u][:, :, places(c)], 2), by_runs(other[b], 2), ADD)
-            for c in range(2):
-                hidden(2 * u + c)
-
-        def third(b, h_c, h_s):
-            o = tile("o%d" % b, [P, PACK, CHUNK], F32)
+        def third(b):
+            h_c, h_s = quantize("h%d" % b, CHUNK, h_bf[b][:])
             planes = PACK // len(O_BANKS[b])
+            banks = []
             for i, number in enumerate(O_BANKS[b]):
-                o_ps = bank("o_ps%d_%d" % (b, i), number, [P, planes, CHUNK])
+                banks.append(bank("o_ps%d_%d" % (b, i), number, [P, planes, CHUNK]))
                 for e in range(planes):
                     t = i * planes + e
-                    product(o_ps[:, e, :], w3w[:, 2 * t * P : 2 * (t + 1) * P].bitcast(FP4X4), w3s[:, places(t)], h_c[:], h_s[:])
+                    product(banks[i][:, e, :], w3w[:, 2 * t * P : 2 * (t + 1) * P].bitcast(FP4X4), w3s[:, places(t)], h_c[:], h_s[:])
+            return banks
+
+        def residual(b, banks):
+            o = tile("o%d" % b, [P, PACK, CHUNK], F32)
+            planes = PACK // len(banks)
+            for i, o_ps in enumerate(banks):
                 mine = slice(i * planes, (i + 1) * planes)
                 nc.vector.tensor_tensor(o[:, mine, :], o_ps[:], res_t[:, mine, places(b)], ADD)
             nc.sync.dma_start(out=out_0.rearrange("(p t) j -> p t j", t=PACK)[:, :, places(b)], in_=o[:])
             return o
 
-        h_q = [quantize("h%d" % b, CHUNK, h_bf[b][:]) for b in range(CHUNKS)]
-        o = [third(b, h_q[b][0], h_q[b][1]) for b in range(CHUNKS)]
+        for b in range(2):
+            summed(b)
+        hidden(0)
+        summed(2)
+        for b in (1, 2):
+            hidden(b)
+        summed(3)
+        o_ps = [third(0)]
+        hidden(3)
+        o = []
+        for b in range(1, CHUNKS):
+            o_ps.append(third(b))
+            o.append(residual(b - 1, o_ps[b - 1]))
+        o.append(residual(CHUNKS - 1, o_ps[CHUNKS - 1]))
 
         out_c, out_s = tile("out_c", [P, S], U32), tile("out_s", [P, S], U8)
         for b in range(CHUNKS - 1):
-            o_bf = tile("o_bf%d" % b, [P, PACK * CHUNK], BF16)
+            o_bf = tile("o_bf%d" % b, [P, PACK * CHUNK], BF16, "z3_c" if b == 0 else None)
             interleave(nc.scalar.copy, o_bf[:], o[b][:])
             quantize_into(out_c[:, places(b)], out_s[:, places(b)], o_bf[:])
         width = CHUNK // 2

@@ -181,7 +181,7 @@ def tile_picked_gin8_gelu_po_kernel(tc, x_words, x_scales, w1, eps, w2, res, w3_
         h_bf = [tile("h_bf%d" % b, [P, PACK * CHUNK], BF16) for b in range(CHUNKS)]
 
         def summed(b):
-            nc.vector.tensor_tensor(woven(z_bf[b][:], 2), by_runs(own[b // 2][:, :, places(b % 2)], 2), by_runs(other[b], 2), ADD)
+            nc.vector.tensor_tensor(woven(z_bf[b][:]), by_runs(own[b // 2][:, :, places(b % 2)]), by_runs(other[b]), ADD)
 
         def hidden(b):
             z_c, z_s = quantize("z%d" % b, CHUNK, z_bf[b][:])

@@ -29,7 +29,7 @@ CHUNKS = S // CHUNK
 HALF = S // 2
 FIRST = T // 4
 H_BANKS = (6, 7, 0, 1)
-O_BANKS = ((2,), (3,), (4,), (5, 6))
+O_BANKS = ((2, 3), (4,), (5,), (6, 7))
 
 FLOPS = 3 * 2 * D * D * S
 
@@ -131,8 +131,9 @@ def tile_picked_gin8_gelu_po_kernel(tc, x_words, x_scales, w1, eps, w2, res, w3_
             quantize_into(w1_c[:, places(t)], w1_s[:, places(t)], w1_bf[0][:, t * PACK * P : (t + 1) * PACK * P])
         quantize_into(w1_c[:, half(1)], w1_s[:, half(1)], w1_bf[1][:])
 
-        w2_raw = tile("w2_raw", [P, PACK, D], F32, "w1_half0")
-        nc.sync.dma_start(out=w2_raw[:], in_=w2.rearrange("(p j) c -> p j c", j=PACK))
+        stage = tile("stage", [P, PACK * D], F32, "w1_half0")
+        w2_raw = stage[:].rearrange("p (j c) -> p j c", j=PACK)
+        nc.sync.dma_start(out=w2_raw, in_=w2.rearrange("(p j) c -> p j c", j=PACK))
         res_t = tile("res_t", [P, PACK, S], F32, "w1_half1")
         nc.sync.dma_start(out=res_t[:], in_=res.rearrange("(p t) j -> p t j", t=PACK))
 
@@ -144,10 +145,10 @@ def tile_picked_gin8_gelu_po_kernel(tc, x_words, x_scales, w1, eps, w2, res, w3_
         y0_ps = [bank("y0_%d" % u, u, [P, HALF]) for u in range(2)]
         for u in range(2):
             product(y0_ps[u][:], w1_c[:, places(0)].bitcast(FP8X4), w1_s[:, places(0)], xw[:, half(u)], xs[:, half(u)])
-        for u in range(2):
-            nc.scalar.copy(out=y[0][:, half(u)], in_=y0_ps[u][:])
-        for u in range(2):
-            nc.scalar.activation(out=ey[0][:, half(u)], in_=y0_ps[u][:], func=COPY, scale=eps_t[:, 0, :])
+        nc.scalar.copy(out=y[0][:, half(0)], in_=y0_ps[0][:])
+        nc.scalar.activation(out=ey[0][:, half(0)], in_=y0_ps[0][:], func=COPY, scale=eps_t[:, 0, :])
+        nc.vector.tensor_copy(out=y[0][:, half(1)], in_=y0_ps[1][:])
+        nc.vector.tensor_scalar_mul(ey[0][:, half(1)], y0_ps[1][:], eps_t[:, 0, :])
         for t in range(1, PACK):
             y_ps = bank("y%d" % t, t + 1, [P, S])
             product(y_ps[:], w1_c[:, places(t)].bitcast(FP8X4), w1_s[:, places(t)], xw[:], xs[:])
@@ -158,8 +159,9 @@ def tile_picked_gin8_gelu_po_kernel(tc, x_words, x_scales, w1, eps, w2, res, w3_
             return list_t[:, cols.start // STRIPE : cols.stop // STRIPE]
 
         w2_bf = tile("w2_bf", [P, PACK * D], BF16)
-        for i in range(2):
-            round_and_deal(nc.vector.tensor_copy, w2_bf[:, i * 2 * D : (i + 1) * 2 * D], w2_raw[:], PAIRS[i])
+        round_and_deal(nc.vector.tensor_copy, w2_bf[:, : 2 * D], w2_raw, PAIRS[0])
+        for u in range(2):
+            round_and_deal(nc.vector.tensor_copy, w2_bf[:, 2 * D :], w2_raw[:, :, half(u)], PAIRS[1], slice(u * P // 2, (u + 1) * P // 2))
 
         own = [tile("own%d" % u, [P, PACK, HALF], F32) for u in range(2)]
         for t in range(PACK):
@@ -177,14 +179,14 @@ def tile_picked_gin8_gelu_po_kernel(tc, x_words, x_scales, w1, eps, w2, res, w3_
                 nc.scalar.activation(got[:, t, :], y[t][:].indirect(entries(p2_t, cols)), COPY)
             other.extend(got[:, :, places(c)] for c in range((cols.stop - cols.start) // CHUNK))
 
-        z_bf = [tile("z_bf%d" % b, [P, PACK * CHUNK], BF16) for b in range(CHUNKS)]
+        z_bf = [stage[:, b * HALF : (b + 1) * HALF].bitcast(BF16) for b in range(CHUNKS)]
         h_bf = [tile("h_bf%d" % b, [P, PACK * CHUNK], BF16) for b in range(CHUNKS)]
 
         def summed(b):
-            nc.vector.tensor_tensor(woven(z_bf[b][:]), by_runs(own[b // 2][:, :, places(b % 2)]), by_runs(other[b]), ADD)
+            nc.vector.tensor_tensor(woven(z_bf[b]), by_runs(own[b // 2][:, :, places(b % 2)]), by_runs(other[b]), ADD)
 
         def hidden(b):
-            z_c, z_s = quantize("z%d" % b, CHUNK, z_bf[b][:])
+            z_c, z_s = quantize("z%d" % b, CHUNK, z_bf[b])
             h_ps = bank("h_ps%d" % b, H_BANKS[b], [P, PACK, CHUNK])
             for t in range(PACK):
                 product(h_ps[:, t, :], w2_c[:, places(t)].bitcast(FP8X4), w2_s[:, places(t)], z_c[:], z_s[:])
@@ -210,10 +212,10 @@ def tile_picked_gin8_gelu_po_kernel(tc, x_words, x_scales, w1, eps, w2, res, w3_
             nc.sync.dma_start(out=out_0.rearrange("(p t) j -> p t j", t=PACK)[:, :, places(b)], in_=o[:])
             return o
 
-        for b in range(2):
-            summed(b)
+        summed(0)
         hidden(0)
-        summed(2)
+        for b in (1, 2):
+            summed(b)
         for b in (1, 2):
             hidden(b)
         summed(3)

@@ -26,6 +26,7 @@ PAIRS = (slice(0, 2), slice(2, 4))
 LINE = 4
 CHUNK = 128
 CHUNKS = S // CHUNK
+LAST = CHUNKS - 1
 HALF = S // 2
 FIRST = T // 4
 H_BANKS = (6, 7, 0, 1)
@@ -49,8 +50,11 @@ def tile_picked_gin8_gelu_po_kernel(tc, x_words, x_scales, w1, eps, w2, res, w3_
         def half(u):
             return slice(u * HALF, (u + 1) * HALF)
 
-        def places(t):
-            return slice(t * P, (t + 1) * P)
+        def run(n):
+            return slice(n * P, (n + 1) * P)
+
+        def entries(list_t, cols):
+            return list_t[:, cols.start // STRIPE : cols.stop // STRIPE]
 
         def load_scale_rows(scale_tile, rows):
             nc.sync.dma_start(out=scale_tile[0:P:SPREAD, :].bitcast(I32), in_=rows.bitcast(I32))
@@ -62,14 +66,14 @@ def tile_picked_gin8_gelu_po_kernel(tc, x_words, x_scales, w1, eps, w2, res, w3_
         def round_and_deal(copy, w_bf, w_raw, pair, share=slice(0, P)):
             copy(out=w_bf.rearrange("p (t m j) -> p m j t", m=P, j=PACK)[:, share], in_=w_raw.rearrange("p j (m t) -> p m j t", t=PACK)[:, :, :, pair])
 
-        def woven(dst, run=LINE):
-            return dst.rearrange("p (c i t) -> p c t i", t=PACK, i=run)
+        def woven(dst):
+            return dst.rearrange("p (c i t) -> p c t i", t=PACK, i=LINE)
 
-        def by_runs(src, run=LINE):
-            return src.rearrange("p t (c i) -> p c t i", i=run)
+        def by_lines(src):
+            return src.rearrange("p t (c i) -> p c t i", i=LINE)
 
         def interleave(copy, dst, src):
-            copy(out=woven(dst), in_=by_runs(src))
+            copy(out=woven(dst), in_=by_lines(src))
 
         def quantize_into(codes, scales, src):
             nc.vector.quantize_mx(out=codes.bitcast(FP8X4), scales=scales, in_=src)
@@ -128,7 +132,7 @@ def tile_picked_gin8_gelu_po_kernel(tc, x_words, x_scales, w1, eps, w2, res, w3_
             for i, copy in enumerate((nc.vector.tensor_copy, nc.scalar.copy)):
                 round_and_deal(copy, w1_bf[i][:], w1_half[u][:], PAIRS[i], slice(u * P // 2, (u + 1) * P // 2))
         for t in range(2):
-            quantize_into(w1_c[:, places(t)], w1_s[:, places(t)], w1_bf[0][:, t * PACK * P : (t + 1) * PACK * P])
+            quantize_into(w1_c[:, run(t)], w1_s[:, run(t)], w1_bf[0][:, t * PACK * P : (t + 1) * PACK * P])
         quantize_into(w1_c[:, half(1)], w1_s[:, half(1)], w1_bf[1][:])
 
         stage = tile("stage", [P, PACK * D], F32, "w1_half0")
@@ -144,53 +148,54 @@ def tile_picked_gin8_gelu_po_kernel(tc, x_words, x_scales, w1, eps, w2, res, w3_
         ey = [tile("ey%d" % t, [P, S], F32) for t in range(PACK)]
         y0_ps = [bank("y0_%d" % u, u, [P, HALF]) for u in range(2)]
         for u in range(2):
-            product(y0_ps[u][:], w1_c[:, places(0)].bitcast(FP8X4), w1_s[:, places(0)], xw[:, half(u)], xs[:, half(u)])
+            product(y0_ps[u][:], w1_c[:, run(0)].bitcast(FP8X4), w1_s[:, run(0)], xw[:, half(u)], xs[:, half(u)])
         nc.scalar.copy(out=y[0][:, half(0)], in_=y0_ps[0][:])
         nc.scalar.activation(out=ey[0][:, half(0)], in_=y0_ps[0][:], func=COPY, scale=eps_t[:, 0, :])
         nc.vector.tensor_copy(out=y[0][:, half(1)], in_=y0_ps[1][:])
         nc.vector.tensor_scalar_mul(ey[0][:, half(1)], y0_ps[1][:], eps_t[:, 0, :])
         for t in range(1, PACK):
             y_ps = bank("y%d" % t, t + 1, [P, S])
-            product(y_ps[:], w1_c[:, places(t)].bitcast(FP8X4), w1_s[:, places(t)], xw[:], xs[:])
+            product(y_ps[:], w1_c[:, run(t)].bitcast(FP8X4), w1_s[:, run(t)], xw[:], xs[:])
             nc.scalar.copy(out=y[t][:], in_=y_ps[:])
             nc.scalar.activation(out=ey[t][:], in_=y_ps[:], func=COPY, scale=eps_t[:, t, :])
-
-        def entries(list_t, cols):
-            return list_t[:, cols.start // STRIPE : cols.stop // STRIPE]
 
         w2_bf = tile("w2_bf", [P, PACK * D], BF16)
         round_and_deal(nc.vector.tensor_copy, w2_bf[:, : 2 * D], w2_raw, PAIRS[0])
         for u in range(2):
             round_and_deal(nc.vector.tensor_copy, w2_bf[:, 2 * D :], w2_raw[:, :, half(u)], PAIRS[1], slice(u * P // 2, (u + 1) * P // 2))
 
-        own = [tile("own%d" % u, [P, PACK, HALF], F32) for u in range(2)]
-        for t in range(PACK):
+        near1 = [tile("near1_%d" % u, [P, PACK, HALF], F32) for u in range(2)]
+
+        def first_list(t):
             for u in range(2):
-                nc.vector.tensor_tensor(own[u][:, t, :], y[t][:].indirect(entries(p1_t, half(u))), ey[t][:, half(u)], ADD)
-            if t == 0:
-                w2_c, w2_s = quantize("w2", D, w2_bf[:])
+                nc.vector.tensor_tensor(near1[u][:, t, :], y[t][:].indirect(entries(p1_t, half(u))), ey[t][:, half(u)], ADD)
+
+        first_list(0)
+        w2_c, w2_s = quantize("w2", D, w2_bf[:])
+        for t in range(1, PACK):
+            first_list(t)
 
         product(bank("warm", O_BANKS[0][0], [P, D])[:], w2_c[:, :P].bitcast(FP8X4), w2_s[:, :P], w2_c[:], w2_s[:])
-        stretches = (half(0), places(2), places(3))
-        other = []
-        for n, cols in enumerate(stretches):
-            got = tile("other%d" % n, [P, PACK, cols.stop - cols.start], F32)
+
+        near2 = []
+        for n, cols in enumerate((half(0), run(2), run(3))):
+            got = tile("near2_%d" % n, [P, PACK, cols.stop - cols.start], F32)
             for t in range(PACK):
                 nc.scalar.activation(got[:, t, :], y[t][:].indirect(entries(p2_t, cols)), COPY)
-            other.extend(got[:, :, places(c)] for c in range((cols.stop - cols.start) // CHUNK))
+            near2.extend(got[:, :, run(c)] for c in range((cols.stop - cols.start) // CHUNK))
 
-        z_bf = [stage[:, b * HALF : (b + 1) * HALF].bitcast(BF16) for b in range(CHUNKS)]
+        z_bf = [stage[:, half(b)].bitcast(BF16) for b in range(CHUNKS)]
         h_bf = [tile("h_bf%d" % b, [P, PACK * CHUNK], BF16) for b in range(CHUNKS)]
 
         def summed(b):
-            nc.vector.tensor_tensor(woven(z_bf[b]), by_runs(own[b // 2][:, :, places(b % 2)]), by_runs(other[b]), ADD)
+            nc.vector.tensor_tensor(woven(z_bf[b]), by_lines(near1[b // 2][:, :, run(b % 2)]), by_lines(near2[b]), ADD)
 
         def hidden(b):
             z_c, z_s = quantize("z%d" % b, CHUNK, z_bf[b])
             h_ps = bank("h_ps%d" % b, H_BANKS[b], [P, PACK, CHUNK])
             for t in range(PACK):
-                product(h_ps[:, t, :], w2_c[:, places(t)].bitcast(FP8X4), w2_s[:, places(t)], z_c[:], z_s[:])
-            nc.scalar.activation(out=h_bf[b][:].rearrange("p (j t) -> p j t", t=PACK), in_=h_ps[:].rearrange("p t j -> p j t"), func=GELU)
+                product(h_ps[:, t, :], w2_c[:, run(t)].bitcast(FP8X4), w2_s[:, run(t)], z_c[:], z_s[:])
+            nc.scalar.activation(out=woven(h_bf[b][:]), in_=by_lines(h_ps[:]), func=GELU)
 
         def third(b):
             h_c, h_s = quantize("h%d" % b, CHUNK, h_bf[b][:])
@@ -200,17 +205,17 @@ def tile_picked_gin8_gelu_po_kernel(tc, x_words, x_scales, w1, eps, w2, res, w3_
                 banks.append(bank("o_ps%d_%d" % (b, i), number, [P, planes, CHUNK]))
                 for e in range(planes):
                     t = i * planes + e
-                    product(banks[i][:, e, :], w3w[:, 2 * t * P : 2 * (t + 1) * P].bitcast(FP4X4), w3s[:, places(t)], h_c[:], h_s[:])
+                    product(banks[i][:, e, :], w3w[:, 2 * t * P : 2 * (t + 1) * P].bitcast(FP4X4), w3s[:, run(t)], h_c[:], h_s[:])
             return banks
 
         def residual(b, banks):
-            o = tile("o%d" % b, [P, PACK, CHUNK], F32)
+            result = tile("result%d" % b, [P, PACK, CHUNK], F32)
             planes = PACK // len(banks)
             for i, o_ps in enumerate(banks):
                 mine = slice(i * planes, (i + 1) * planes)
-                nc.vector.tensor_tensor(o[:, mine, :], o_ps[:], res_t[:, mine, places(b)], ADD)
-            nc.sync.dma_start(out=out_0.rearrange("(p t) j -> p t j", t=PACK)[:, :, places(b)], in_=o[:])
-            return o
+                nc.vector.tensor_tensor(result[:, mine, :], o_ps[:], res_t[:, mine, run(b)], ADD)
+            nc.sync.dma_start(out=out_0.rearrange("(p t) j -> p t j", t=PACK)[:, :, run(b)], in_=result[:])
+            return result
 
         summed(0)
         hidden(0)
@@ -218,27 +223,27 @@ def tile_picked_gin8_gelu_po_kernel(tc, x_words, x_scales, w1, eps, w2, res, w3_
             summed(b)
         for b in (1, 2):
             hidden(b)
-        summed(3)
-        o_ps = [third(0)]
-        hidden(3)
-        o = []
+        summed(LAST)
+        o_banks = [third(0)]
+        hidden(LAST)
+        results = []
         for b in range(1, CHUNKS):
-            o_ps.append(third(b))
-            o.append(residual(b - 1, o_ps[b - 1]))
-        o.append(residual(CHUNKS - 1, o_ps[CHUNKS - 1]))
+            o_banks.append(third(b))
+            results.append(residual(b - 1, o_banks[b - 1]))
+        results.append(residual(LAST, o_banks[LAST]))
 
         out_c, out_s = tile("out_c", [P, S], U32), tile("out_s", [P, S], U8)
-        for b in range(CHUNKS - 1):
-            o_bf = tile("o_bf%d" % b, [P, PACK * CHUNK], BF16, "z3_c" if b == 0 else None)
-            interleave(nc.scalar.copy, o_bf[:], o[b][:])
-            quantize_into(out_c[:, places(b)], out_s[:, places(b)], o_bf[:])
+        for b in range(LAST):
+            o_bf = tile("o_bf%d" % b, [P, PACK * CHUNK], BF16, None if b else "z%d_c" % LAST)
+            interleave(nc.scalar.copy, o_bf[:], results[b][:])
+            quantize_into(out_c[:, run(b)], out_s[:, run(b)], o_bf[:])
         width = CHUNK // 2
-        o3_bf = [tile("o3_bf%d" % i, [P, PACK * width], BF16) for i in range(2)]
+        last_bf = [tile("last_bf%d" % i, [P, PACK * width], BF16) for i in range(2)]
         for i, copy in enumerate((nc.vector.tensor_copy, nc.scalar.copy)):
-            interleave(copy, o3_bf[i][:], o[3][:, :, i * width : (i + 1) * width])
+            interleave(copy, last_bf[i][:], results[LAST][:, :, i * width : (i + 1) * width])
         for i in range(2):
-            cols = slice(3 * CHUNK + i * width, 3 * CHUNK + (i + 1) * width)
-            quantize_into(out_c[:, cols], out_s[:, cols], o3_bf[i][:])
+            cols = slice(LAST * CHUNK + i * width, LAST * CHUNK + (i + 1) * width)
+            quantize_into(out_c[:, cols], out_s[:, cols], last_bf[i][:])
 
         out_words = out_1[0].rearrange("p n t -> p (n t)").bitcast(I32)
         for u in range(2):

@@ -11,6 +11,7 @@ U8 = mybir.dt.uint8
 FP8X4 = mybir.dt.float8_e4m3fn_x4
 FP4X4 = mybir.dt.float4_e2m1fn_x4
 ADD = mybir.AluOpType.add
+MULT = mybir.AluOpType.mult
 COPY = mybir.ActivationFunctionType.Copy
 GELU = mybir.ActivationFunctionType.Gelu_apprx_tanh
 
@@ -29,8 +30,8 @@ CHUNKS = S // CHUNK
 LAST = CHUNKS - 1
 HALF = S // 2
 FIRST = T // 4
-H_BANKS = (6, 7, 0, 1)
-O_BANKS = ((2, 3), (4,), (5,), (6, 7))
+H_BANKS = (5, 6, 7, 0)
+O_BANKS = ((1, 2), (3,), (4,), (5, 6))
 
 FLOPS = 3 * 2 * D * D * S
 
@@ -92,8 +93,7 @@ def tile_picked_gin8_gelu_po_kernel(tc, x_words, x_scales, w1, eps, w2, res, w3_
         xs_all = tile("xs_all", [P, T], U8)
         w3s_raw = tile("w3s_raw", [P, D], U8)
         xs = tile("xs", [P, S], U8)
-        w3s = tile("w3s", [P, D], U8)
-        for zeroed in (xs_all[:], w3s_raw[:], xs[:], w3s[:]):
+        for zeroed in (xs_all[:], w3s_raw[:], xs[:]):
             nc.vector.memset(zeroed.bitcast(I32), 0)
         warm = keep.tile([P, 2], F32, name="warm")
         nc.vector.memset(warm[:, 0:1], 0.0)
@@ -105,16 +105,16 @@ def tile_picked_gin8_gelu_po_kernel(tc, x_words, x_scales, w1, eps, w2, res, w3_
         w1_rows = w1.rearrange("(p j) c -> p j c", j=PACK)
         xw_all = tile("xw_all", [P, T], U32)
         xw_rows = x_words[0].rearrange("p n t -> p (n t)").bitcast(I32)
-        w3w_raw = tile("w3w_raw", [P, 2 * D], U8)
         nc.sync.dma_start(out=xw_all[:, :FIRST].bitcast(I32), in_=xw_rows[:, :FIRST])
         nc.sync.dma_start(offs_t[:], offs)
         load_scale_rows(xs_all, x_scales[0])
         load_scale_rows(w3s_raw, w3_scales[0])
         nc.sync.dma_start(p1_t[:], p1)
+        nc.sync.dma_start(p2_t[:], p2)
         nc.sync.dma_start(out=xw_all[:, FIRST:].bitcast(I32), in_=xw_rows[:, FIRST:])
         for u in range(2):
             nc.sync.dma_start(out=w1_half[u][:], in_=w1_rows[:, :, half(u)])
-        nc.sync.dma_start(p2_t[:], p2)
+        w3w_raw = tile("w3w_raw", [P, 2 * D], U8)
         nc.sync.dma_start(out=w3w_raw[:].bitcast(I32), in_=w3_words[0].bitcast(I32))
 
         xs_spread = tile("xs_spread", [P, S], U8)
@@ -122,7 +122,6 @@ def tile_picked_gin8_gelu_po_kernel(tc, x_words, x_scales, w1, eps, w2, res, w3_
         place_scale_rows(nc.scalar, xs, xs_spread)
         w3s_spread = tile("w3s_spread", [P, D], U8, "xs_all")
         nc.vector.tensor_copy(out=w3s_spread[:].rearrange("p (t m) -> p t m", t=PACK), in_=w3s_raw[:].rearrange("p (m t) -> p t m", t=PACK))
-        place_scale_rows(nc.sync, w3s, w3s_spread)
 
         xw = tile("xw", [P, S], U32)
         nc.vector.tensor_copy(out=xw[:], in_=xw_all[:].indirect(offs_t[:]))
@@ -135,47 +134,58 @@ def tile_picked_gin8_gelu_po_kernel(tc, x_words, x_scales, w1, eps, w2, res, w3_
             quantize_into(w1_c[:, run(t)], w1_s[:, run(t)], w1_bf[0][:, t * PACK * P : (t + 1) * PACK * P])
         quantize_into(w1_c[:, half(1)], w1_s[:, half(1)], w1_bf[1][:])
 
-        stage = tile("stage", [P, PACK * D], F32, "w1_half0")
+        stage = tile("stage", [P, PACK * D], F32, "w3s_raw")
         w2_raw = stage[:].rearrange("p (j c) -> p j c", j=PACK)
         nc.sync.dma_start(out=w2_raw, in_=w2.rearrange("(p j) c -> p j c", j=PACK))
         res_t = tile("res_t", [P, PACK, S], F32, "w1_half1")
         nc.sync.dma_start(out=res_t[:], in_=res.rearrange("(p t) j -> p t j", t=PACK))
 
+        w3s = tile("w3s", [P, D], U8, "w1_bf0")
+        nc.vector.memset(w3s[:].bitcast(I32), 0)
+        place_scale_rows(nc.sync, w3s, w3s_spread)
+
         w3w = tile("w3w", [P, 2 * D], U8, "w1_bf1")
         nc.vector.tensor_copy(out=w3w[:].bitcast(U16).rearrange("p (t m) -> p t m", t=PACK), in_=w3w_raw[:].bitcast(U16).rearrange("p (m t) -> p t m", t=PACK))
 
         y = [tile("y%d" % t, [P, S], F32) for t in range(PACK)]
-        ey = [tile("ey%d" % t, [P, S], F32) for t in range(PACK)]
-        y0_ps = [bank("y0_%d" % u, u, [P, HALF]) for u in range(2)]
-        for u in range(2):
-            product(y0_ps[u][:], w1_c[:, run(0)].bitcast(FP8X4), w1_s[:, run(0)], xw[:, half(u)], xs[:, half(u)])
-        nc.scalar.copy(out=y[0][:, half(0)], in_=y0_ps[0][:])
-        nc.scalar.activation(out=ey[0][:, half(0)], in_=y0_ps[0][:], func=COPY, scale=eps_t[:, 0, :])
-        nc.vector.tensor_copy(out=y[0][:, half(1)], in_=y0_ps[1][:])
-        nc.vector.tensor_scalar_mul(ey[0][:, half(1)], y0_ps[1][:], eps_t[:, 0, :])
-        for t in range(1, PACK):
-            y_ps = bank("y%d" % t, t + 1, [P, S])
-            product(y_ps[:], w1_c[:, run(t)].bitcast(FP8X4), w1_s[:, run(t)], xw[:], xs[:])
-            nc.scalar.copy(out=y[t][:], in_=y_ps[:])
-            nc.scalar.activation(out=ey[t][:], in_=y_ps[:], func=COPY, scale=eps_t[:, t, :])
+        y_ps = [[(bank("y0_%d" % u, u, [P, HALF]), half(u)) for u in range(2)]]
+        y_ps.extend([(bank("y%d" % t, t + 1, [P, S]), slice(0, S))] for t in range(1, PACK))
+        for t in range(PACK):
+            for u, (piece, cols) in enumerate(y_ps[t]):
+                product(piece[:], w1_c[:, run(t)].bitcast(FP8X4), w1_s[:, run(t)], xw[:, cols], xs[:, cols])
+                copy = nc.vector.tensor_copy if t == u == 0 else nc.scalar.copy
+                copy(out=y[t][:, cols], in_=piece[:])
 
         w2_bf = tile("w2_bf", [P, PACK * D], BF16)
-        round_and_deal(nc.vector.tensor_copy, w2_bf[:, : 2 * D], w2_raw, PAIRS[0])
-        for u in range(2):
-            round_and_deal(nc.vector.tensor_copy, w2_bf[:, 2 * D :], w2_raw[:, :, half(u)], PAIRS[1], slice(u * P // 2, (u + 1) * P // 2))
+        for n in range(PACK):
+            places = slice(n * P // PACK, (n + 1) * P // PACK)
+            nc.gpsimd.tensor_scalar(w2_bf[:].rearrange("p (t m j) -> p t m j", m=P, j=PACK)[:, :, places], w2_raw[:, :, run(n)].rearrange("p j (m t) -> p t m j", t=PACK), 1.0, 0.0, MULT, ADD)
 
-        near1 = [tile("near1_%d" % u, [P, PACK, HALF], F32) for u in range(2)]
+        near1 = [tile("near1_%d" % t, [P, S], F32) for t in range(PACK)]
+        own = tile("own", [P, PACK, S], F32)
 
         def first_list(t):
             for u in range(2):
-                nc.vector.tensor_tensor(near1[u][:, t, :], y[t][:].indirect(entries(p1_t, half(u))), ey[t][:, half(u)], ADD)
+                looked_up = y[t][:].indirect(entries(p1_t, half(u)))
+                if t < PACK - 1:
+                    nc.vector.tensor_copy(out=near1[t][:, half(u)], in_=looked_up)
+                else:
+                    nc.scalar.activation(near1[t][:, half(u)], looked_up, COPY)
+
+        def add_own(t):
+            for piece, cols in y_ps[t]:
+                nc.vector.scalar_tensor_tensor(own[:, t, cols], piece[:], eps_t[:, t, :], near1[t][:, cols], MULT, ADD)
 
         first_list(0)
-        w2_c, w2_s = quantize("w2", D, w2_bf[:])
         for t in range(1, PACK):
             first_list(t)
+            add_own(t - 1)
+        add_own(PACK - 1)
+        w2_c, w2_s = tile("w2_c", [P, D], U32), tile("w2_s", [P, D], U8)
+        for u in range(2):
+            quantize_into(w2_c[:, half(u)], w2_s[:, half(u)], w2_bf[:, 2 * u * D : 2 * (u + 1) * D])
 
-        product(bank("warm", O_BANKS[0][0], [P, D])[:], w2_c[:, :P].bitcast(FP8X4), w2_s[:, :P], w2_c[:], w2_s[:])
+        product(bank("warm", H_BANKS[2], [P, D])[:], w2_c[:, :P].bitcast(FP8X4), w2_s[:, :P], w2_c[:], w2_s[:])
 
         near2 = []
         for n, cols in enumerate((half(0), run(2), run(3))):
@@ -184,11 +194,11 @@ def tile_picked_gin8_gelu_po_kernel(tc, x_words, x_scales, w1, eps, w2, res, w3_
                 nc.scalar.activation(got[:, t, :], y[t][:].indirect(entries(p2_t, cols)), COPY)
             near2.extend(got[:, :, run(c)] for c in range((cols.stop - cols.start) // CHUNK))
 
-        z_bf = [stage[:, half(b)].bitcast(BF16) for b in range(CHUNKS)]
+        z_bf = [w2_bf[:, b * PACK * CHUNK : (b + 1) * PACK * CHUNK] for b in range(CHUNKS)]
         h_bf = [tile("h_bf%d" % b, [P, PACK * CHUNK], BF16) for b in range(CHUNKS)]
 
         def summed(b):
-            nc.vector.tensor_tensor(woven(z_bf[b]), by_lines(near1[b // 2][:, :, run(b % 2)]), by_lines(near2[b]), ADD)
+            nc.vector.tensor_tensor(woven(z_bf[b]), by_lines(own[:, :, run(b)]), by_lines(near2[b]), ADD)
 
         def hidden(b):
             z_c, z_s = quantize("z%d" % b, CHUNK, z_bf[b])

@@ -40,6 +40,7 @@ def tile_picked_gin8_gelu_po_kernel(tc, x_words, x_scales, w1, eps, w2, res, w3_
     nc = tc.nc
     with ExitStack() as ctx:
         keep = ctx.enter_context(tc.tile_pool(name="keep", bufs=1))
+        placed = ctx.enter_context(tc.tile_pool(name="placed", bufs=1))
         psum = ctx.enter_context(tc.psum_pool(name="psum", bufs=1))
 
         def tile(name, shape, dtype, tag=None):
@@ -66,6 +67,9 @@ def tile_picked_gin8_gelu_po_kernel(tc, x_words, x_scales, w1, eps, w2, res, w3_
 
         def round_and_deal(copy, w_bf, w_raw, pair, share=slice(0, P)):
             copy(out=w_bf.rearrange("p (t m j) -> p m j t", m=P, j=PACK)[:, share], in_=w_raw.rearrange("p j (m t) -> p m j t", t=PACK)[:, :, :, pair])
+
+        def stream_copy(out, in_):
+            nc.gpsimd.tensor_scalar(out, in_, 1.0, 0.0, MULT, ADD)
 
         def woven(dst):
             return dst.rearrange("p (c i t) -> p c t i", t=PACK, i=LINE)
@@ -114,7 +118,7 @@ def tile_picked_gin8_gelu_po_kernel(tc, x_words, x_scales, w1, eps, w2, res, w3_
         nc.sync.dma_start(out=xw_all[:, FIRST:].bitcast(I32), in_=xw_rows[:, FIRST:])
         for u in range(2):
             nc.sync.dma_start(out=w1_half[u][:], in_=w1_rows[:, :, half(u)])
-        w3w_raw = tile("w3w_raw", [P, 2 * D], U8)
+        w3w_raw = placed.tile([P, 2 * D], U8, name="w3w_raw", offset=2 * PACK * D - D)
         nc.sync.dma_start(out=w3w_raw[:].bitcast(I32), in_=w3_words[0].bitcast(I32))
 
         xs_spread = tile("xs_spread", [P, S], U8)
@@ -134,14 +138,13 @@ def tile_picked_gin8_gelu_po_kernel(tc, x_words, x_scales, w1, eps, w2, res, w3_
             quantize_into(w1_c[:, run(t)], w1_s[:, run(t)], w1_bf[0][:, t * PACK * P : (t + 1) * PACK * P])
         quantize_into(w1_c[:, half(1)], w1_s[:, half(1)], w1_bf[1][:])
 
-        stage = tile("stage", [P, PACK * D], F32, "w3s_raw")
-        w2_raw = stage[:].rearrange("p (j c) -> p j c", j=PACK)
+        stage = tile("stage", [P, (2 * PACK - 1) * D + HALF], F32, "xw_all")
+        w2_raw = stage[:, : PACK * D].rearrange("p (j c) -> p j c", j=PACK)
         nc.sync.dma_start(out=w2_raw, in_=w2.rearrange("(p j) c -> p j c", j=PACK))
         res_t = tile("res_t", [P, PACK, S], F32, "w1_half1")
         nc.sync.dma_start(out=res_t[:], in_=res.rearrange("(p t) j -> p t j", t=PACK))
 
-        w3s = tile("w3s", [P, D], U8, "w1_bf0")
-        nc.vector.memset(w3s[:].bitcast(I32), 0)
+        w3s = tile("w3s", [P, D], U8, "xs_spread")
         place_scale_rows(nc.sync, w3s, w3s_spread)
 
         w3w = tile("w3w", [P, 2 * D], U8, "w1_bf1")
@@ -156,49 +159,52 @@ def tile_picked_gin8_gelu_po_kernel(tc, x_words, x_scales, w1, eps, w2, res, w3_
                 copy = nc.vector.tensor_copy if t == u == 0 else nc.scalar.copy
                 copy(out=y[t][:, cols], in_=piece[:])
 
-        w2_bf = tile("w2_bf", [P, PACK * D], BF16)
-        for n in range(PACK):
-            places = slice(n * P // PACK, (n + 1) * P // PACK)
-            nc.gpsimd.tensor_scalar(w2_bf[:].rearrange("p (t m j) -> p t m j", m=P, j=PACK)[:, :, places], w2_raw[:, :, run(n)].rearrange("p j (m t) -> p t m j", t=PACK), 1.0, 0.0, MULT, ADD)
-
-        near1 = [tile("near1_%d" % t, [P, S], F32) for t in range(PACK)]
-        own = tile("own", [P, PACK, S], F32)
-
-        def first_list(t):
-            for u in range(2):
-                looked_up = y[t][:].indirect(entries(p1_t, half(u)))
-                if t < PACK - 1:
-                    nc.vector.tensor_copy(out=near1[t][:, half(u)], in_=looked_up)
-                else:
-                    nc.scalar.activation(near1[t][:, half(u)], looked_up, COPY)
-
-        def add_own(t):
-            for piece, cols in y_ps[t]:
-                nc.vector.scalar_tensor_tensor(own[:, t, cols], piece[:], eps_t[:, t, :], near1[t][:, cols], MULT, ADD)
-
-        first_list(0)
-        for t in range(1, PACK):
-            first_list(t)
-            add_own(t - 1)
-        add_own(PACK - 1)
-        w2_c, w2_s = tile("w2_c", [P, D], U32), tile("w2_s", [P, D], U8)
+        ey0 = stage[:, (2 * PACK - 1) * D - HALF :]
+        nc.gpsimd.tensor_scalar(ey0, y[0][:], eps_t[:, 0, :], 0.0, MULT, ADD)
+        w2_bf = placed.tile([P, PACK * D], BF16, name="w2_bf", offset=0, align_bytes=64)
         for u in range(2):
-            quantize_into(w2_c[:, half(u)], w2_s[:, half(u)], w2_bf[:, 2 * u * D : 2 * (u + 1) * D])
+            round_and_deal(stream_copy, w2_bf[:, 2 * u * D : 2 * (u + 1) * D], w2_raw, PAIRS[u])
+
+        near1 = [None] + [tile("near1_%d" % t, [P, S], F32) for t in range(1, PACK)]
+        near2 = placed.tile([P, PACK, S], F32, name="near2", offset=2 * PACK * D)
+        own = stage[:, (PACK - 1) * D : (2 * PACK - 1) * D].rearrange("p (t c) -> p t c", t=PACK)
+
+        def by_vector(out, t, list_t, cols):
+            nc.vector.tensor_copy(out=out, in_=y[t][:].indirect(entries(list_t, cols)))
+
+        def by_scalar(out, t, list_t, cols):
+            nc.scalar.activation(out, y[t][:].indirect(entries(list_t, cols)), COPY)
+
+        def add_own(t, cols):
+            nc.vector.scalar_tensor_tensor(own[:, t, cols], y_ps[t][0][0][:, cols], eps_t[:, t, :], near1[t][:, cols], MULT, ADD)
+
+        for u in range(2):
+            by_vector(near2[:, 0, half(u)], 0, p2_t, half(u))
+        for u in range(2):
+            by_vector(near1[1][:, half(u)], 1, p1_t, half(u))
+        for u in range(2):
+            add_own(1, half(u))
+        for u in range(2):
+            by_scalar(near1[2][:, half(u)], 2, p1_t, half(u))
+        for u in range(2):
+            by_scalar(near1[3][:, half(u)], 3, p1_t, half(u))
+        add_own(2, slice(0, S))
+        for u in range(2):
+            nc.vector.tensor_tensor(own[:, 0, half(u)], y[0][:].indirect(entries(p1_t, half(u))), ey0[:, half(u)], ADD)
+        add_own(3, slice(0, S))
+        w2_c, w2_s = quantize("w2", D, w2_bf[:])
 
         product(bank("warm", H_BANKS[2], [P, D])[:], w2_c[:, :P].bitcast(FP8X4), w2_s[:, :P], w2_c[:], w2_s[:])
 
-        near2 = []
-        for n, cols in enumerate((half(0), run(2), run(3))):
-            got = tile("near2_%d" % n, [P, PACK, cols.stop - cols.start], F32)
-            for t in range(PACK):
-                nc.scalar.activation(got[:, t, :], y[t][:].indirect(entries(p2_t, cols)), COPY)
-            near2.extend(got[:, :, run(c)] for c in range((cols.stop - cols.start) // CHUNK))
+        for cols in (half(0), run(2), run(3)):
+            for t in range(1, PACK):
+                by_scalar(near2[:, t, cols], t, p2_t, cols)
 
-        z_bf = [w2_bf[:, b * PACK * CHUNK : (b + 1) * PACK * CHUNK] for b in range(CHUNKS)]
+        z_bf = [tile("z_bf%d" % b, [P, PACK * CHUNK], BF16)[:] for b in range(CHUNKS)]
         h_bf = [tile("h_bf%d" % b, [P, PACK * CHUNK], BF16) for b in range(CHUNKS)]
 
         def summed(b):
-            nc.vector.tensor_tensor(woven(z_bf[b]), by_lines(own[:, :, run(b)]), by_lines(near2[b]), ADD)
+            nc.vector.tensor_tensor(woven(z_bf[b]), by_lines(own[:, :, run(b)]), by_lines(near2[:, :, run(b)]), ADD)
 
         def hidden(b):
             z_c, z_s = quantize("z%d" % b, CHUNK, z_bf[b])

@@ -33,6 +33,11 @@ FIRST = T // 4
 H_BANKS = (5, 6, 7, 0)
 O_BANKS = ((1, 2), (3,), (4,), (5, 6))
 
+WARM_BANK = 3
+
+AT_W1 = 2 * PACK * D
+AT_Y = AT_W1 + 4 * D
+
 FLOPS = 3 * 2 * D * D * S
 
 
@@ -105,7 +110,7 @@ def tile_picked_gin8_gelu_po_kernel(tc, x_words, x_scales, w1, eps, w2, res, w3_
 
         eps_t = keep.tile([P, PACK, 1], F32, name="eps_t")
         nc.scalar.dma_start(out=eps_t[:], in_=eps.rearrange("(p t) o -> p t o", t=PACK))
-        w1_half = [tile("w1_half%d" % u, [P, PACK, HALF], F32) for u in range(2)]
+        w1_half = [tile("w1_half%d" % u, [P, 2, D], F32) for u in range(2)]
         w1_rows = w1.rearrange("(p j) c -> p j c", j=PACK)
         xw_all = tile("xw_all", [P, T], U32)
         xw_rows = x_words[0].rearrange("p n t -> p (n t)").bitcast(I32)
@@ -117,9 +122,9 @@ def tile_picked_gin8_gelu_po_kernel(tc, x_words, x_scales, w1, eps, w2, res, w3_
         nc.sync.dma_start(p2_t[:], p2)
         nc.sync.dma_start(out=xw_all[:, FIRST:].bitcast(I32), in_=xw_rows[:, FIRST:])
         for u in range(2):
-            nc.sync.dma_start(out=w1_half[u][:], in_=w1_rows[:, :, half(u)])
-        w3w_raw = placed.tile([P, 2 * D], U8, name="w3w_raw", offset=2 * PACK * D - D)
-        nc.sync.dma_start(out=w3w_raw[:].bitcast(I32), in_=w3_words[0].bitcast(I32))
+            nc.sync.dma_start(out=w1_half[u][:], in_=w1_rows[:, PAIRS[u], :])
+        w3w_raw = placed.tile([P, 4 * PACK * S], U8, name="w3w_raw", offset=AT_Y)[:, : 2 * D]
+        nc.sync.dma_start(out=w3w_raw.bitcast(I32), in_=w3_words[0].bitcast(I32))
 
         xs_spread = tile("xs_spread", [P, S], U8)
         nc.vector.tensor_copy(out=xs_spread[:], in_=xs_all[:].indirect(offs_t[:]))
@@ -129,17 +134,19 @@ def tile_picked_gin8_gelu_po_kernel(tc, x_words, x_scales, w1, eps, w2, res, w3_
 
         xw = tile("xw", [P, S], U32)
         nc.vector.tensor_copy(out=xw[:], in_=xw_all[:].indirect(offs_t[:]))
-        w1_bf = [tile("w1_bf%d" % i, [P, 2 * PACK * P], BF16) for i in range(2)]
-        w1_c, w1_s = tile("w1_c", [P, D], U32), tile("w1_s", [P, D], U8)
+        w1_bf = [tile("w1_bf%d" % i, [P, width], BF16) for i, width in enumerate((D, D, 2 * D))]
+        w1_c, w1_s = placed.tile([P, D], U32, name="w1_c", offset=AT_W1, align_bytes=64), tile("w1_s", [P, D], U8)
         for u in range(2):
-            for i, copy in enumerate((nc.vector.tensor_copy, nc.scalar.copy)):
-                round_and_deal(copy, w1_bf[i][:], w1_half[u][:], PAIRS[i], slice(u * P // 2, (u + 1) * P // 2))
+            rows = w1_half[u][:].rearrange("p j (m t) -> p m j t", t=PACK)
+            for t in range(2):
+                nc.vector.tensor_copy(out=w1_bf[t][:].rearrange("p (m j) -> p m j", j=PACK)[:, :, PAIRS[u]], in_=rows[:, :, :, t])
+            nc.scalar.copy(out=w1_bf[2][:].rearrange("p (t m j) -> p m j t", m=P, j=PACK)[:, :, PAIRS[u]], in_=rows[:, :, :, PAIRS[1]])
         for t in range(2):
-            quantize_into(w1_c[:, run(t)], w1_s[:, run(t)], w1_bf[0][:, t * PACK * P : (t + 1) * PACK * P])
-        quantize_into(w1_c[:, half(1)], w1_s[:, half(1)], w1_bf[1][:])
+            quantize_into(w1_c[:, run(t)], w1_s[:, run(t)], w1_bf[t][:])
+        quantize_into(w1_c[:, half(1)], w1_s[:, half(1)], w1_bf[2][:])
 
-        stage = tile("stage", [P, (2 * PACK - 1) * D + HALF], F32, "xw_all")
-        w2_raw = stage[:, : PACK * D].rearrange("p (j c) -> p j c", j=PACK)
+        stage = tile("stage", [P, (PACK - 1) * HALF + PACK * D], F32, "xw_all")
+        w2_raw = stage[:, (PACK - 1) * HALF :].rearrange("p (j c) -> p j c", j=PACK)
         nc.sync.dma_start(out=w2_raw, in_=w2.rearrange("(p j) c -> p j c", j=PACK))
         res_t = tile("res_t", [P, PACK, S], F32, "w1_half1")
         nc.sync.dma_start(out=res_t[:], in_=res.rearrange("(p t) j -> p t j", t=PACK))
@@ -147,10 +154,10 @@ def tile_picked_gin8_gelu_po_kernel(tc, x_words, x_scales, w1, eps, w2, res, w3_
         w3s = tile("w3s", [P, D], U8, "xs_spread")
         place_scale_rows(nc.sync, w3s, w3s_spread)
 
-        w3w = tile("w3w", [P, 2 * D], U8, "w1_bf1")
-        nc.vector.tensor_copy(out=w3w[:].bitcast(U16).rearrange("p (t m) -> p t m", t=PACK), in_=w3w_raw[:].bitcast(U16).rearrange("p (m t) -> p t m", t=PACK))
+        w3w = tile("w3w", [P, 2 * D], U8, "w1_half0")
+        nc.scalar.copy(out=w3w[:].bitcast(U16).rearrange("p (t m) -> p t m", t=PACK), in_=w3w_raw.bitcast(U16).rearrange("p (m t) -> p t m", t=PACK))
 
-        y = [tile("y%d" % t, [P, S], F32) for t in range(PACK)]
+        y = [placed.tile([P, S], F32, name="y%d" % t, offset=AT_Y + 4 * S * t) for t in range(PACK)]
         y_ps = [[(bank("y0_%d" % u, u, [P, HALF]), half(u)) for u in range(2)]]
         y_ps.extend([(bank("y%d" % t, t + 1, [P, S]), slice(0, S))] for t in range(1, PACK))
         for t in range(PACK):
@@ -159,52 +166,61 @@ def tile_picked_gin8_gelu_po_kernel(tc, x_words, x_scales, w1, eps, w2, res, w3_
                 copy = nc.vector.tensor_copy if t == u == 0 else nc.scalar.copy
                 copy(out=y[t][:, cols], in_=piece[:])
 
-        ey0 = stage[:, (2 * PACK - 1) * D - HALF :]
-        nc.gpsimd.tensor_scalar(ey0, y[0][:], eps_t[:, 0, :], 0.0, MULT, ADD)
         w2_bf = placed.tile([P, PACK * D], BF16, name="w2_bf", offset=0, align_bytes=64)
-        for u in range(2):
-            round_and_deal(stream_copy, w2_bf[:, 2 * u * D : 2 * (u + 1) * D], w2_raw, PAIRS[u])
+        stream_copy(out=w2_bf[:].rearrange("p (t m j) -> p m j t", m=P, j=PACK), in_=w2_raw.rearrange("p j (m t) -> p m j t", t=PACK))
 
-        near1 = [None] + [tile("near1_%d" % t, [P, S], F32) for t in range(1, PACK)]
-        near2 = placed.tile([P, PACK, S], F32, name="near2", offset=2 * PACK * D)
-        own = stage[:, (PACK - 1) * D : (2 * PACK - 1) * D].rearrange("p (t c) -> p t c", t=PACK)
+        near1 = [[tile("near1_0_%d" % t, [P, HALF], F32)[:] for t in range(PACK)]]
+        near1.append([placed.tile([P, HALF], F32, name="near1_1_%d" % t, offset=AT_W1 + 4 * HALF * (t - 1))[:] for t in (1, 2)] + [tile("near1_1_3", [P, HALF], F32)[:]])
+        on_w2 = [stage[:, i * PACK * HALF : (i + 1) * PACK * HALF].rearrange("p (t c) -> p t c", t=PACK) for i in range(2)]
+        near1[1] = [stage[:, 2 * PACK * HALF : (2 * PACK + 1) * HALF]] + near1[1]
+        near2_all = [tile("near2_0", [P, PACK, HALF], F32)[:], on_w2[1]]
+        near2 = [[near2_all[u][:, t, :] for t in range(PACK)] for u in range(2)]
+        own = [on_w2[0], placed.tile([P, PACK, HALF], F32, name="own_1", offset=0, align_bytes=64)[:]]
 
-        def by_vector(out, t, list_t, cols):
-            nc.vector.tensor_copy(out=out, in_=y[t][:].indirect(entries(list_t, cols)))
+        def by_vector(near, list_t, t, u):
+            nc.vector.tensor_copy(out=near[u][t], in_=y[t][:].indirect(entries(list_t, half(u))))
 
-        def by_scalar(out, t, list_t, cols):
-            nc.scalar.activation(out, y[t][:].indirect(entries(list_t, cols)), COPY)
+        def by_scalar(near, list_t, t, u):
+            nc.scalar.activation(near[u][t], y[t][:].indirect(entries(list_t, half(u))), COPY)
 
-        def add_own(t, cols):
-            nc.vector.scalar_tensor_tensor(own[:, t, cols], y_ps[t][0][0][:, cols], eps_t[:, t, :], near1[t][:, cols], MULT, ADD)
+        def add_own(t, u):
+            source = y_ps[t][u][0][:] if t == 0 else y_ps[t][0][0][:, half(u)]
+            nc.vector.scalar_tensor_tensor(own[u][:, t, :], source, eps_t[:, t, :], near1[u][t], MULT, ADD)
 
-        for u in range(2):
-            by_vector(near2[:, 0, half(u)], 0, p2_t, half(u))
-        for u in range(2):
-            by_vector(near1[1][:, half(u)], 1, p1_t, half(u))
-        for u in range(2):
-            add_own(1, half(u))
-        for u in range(2):
-            by_scalar(near1[2][:, half(u)], 2, p1_t, half(u))
-        for u in range(2):
-            by_scalar(near1[3][:, half(u)], 3, p1_t, half(u))
-        add_own(2, slice(0, S))
-        for u in range(2):
-            nc.vector.tensor_tensor(own[:, 0, half(u)], y[0][:].indirect(entries(p1_t, half(u))), ey0[:, half(u)], ADD)
-        add_own(3, slice(0, S))
+        for t in range(2):
+            by_vector(near1, p1_t, t, 0)
+            by_vector(near2, p2_t, t, 0)
+        nc.vector.tensor_copy(out=near2[0][2][:, run(0)], in_=y[2][:].indirect(entries(p2_t, run(0))))
+        for t in range(2, PACK):
+            by_scalar(near1, p1_t, t, 0)
+        nc.scalar.activation(near2[0][2][:, run(1)], y[2][:].indirect(entries(p2_t, run(1))), COPY)
+        by_scalar(near2, p2_t, 3, 0)
+        for t in range(PACK):
+            add_own(t, 0)
         w2_c, w2_s = quantize("w2", D, w2_bf[:])
 
-        product(bank("warm", H_BANKS[2], [P, D])[:], w2_c[:, :P].bitcast(FP8X4), w2_s[:, :P], w2_c[:], w2_s[:])
+        z_first = tile("z_first", [P, PACK * HALF], BF16)
+        nc.gpsimd.tensor_tensor(woven(z_first[:]), by_lines(own[0]), by_lines(near2_all[0]), ADD)
 
-        for cols in (half(0), run(2), run(3)):
+        for t in range(1, PACK):
+            by_scalar(near1, p1_t, t, 1)
+        for cols in (run(0), run(1)):
             for t in range(1, PACK):
-                by_scalar(near2[:, t, cols], t, p2_t, cols)
+                nc.scalar.activation(near2[1][t][:, cols], y[t][:].indirect(entries(p2_t, slice(HALF + cols.start, HALF + cols.stop))), COPY)
+        by_vector(near1, p1_t, 0, 1)
+        by_vector(near2, p2_t, 0, 1)
+        for t in range(PACK):
+            add_own(t, 1)
 
-        z_bf = [tile("z_bf%d" % b, [P, PACK * CHUNK], BF16)[:] for b in range(CHUNKS)]
+        product(bank("warm", WARM_BANK, [P, D])[:], w2_c[:, :P].bitcast(FP8X4), w2_s[:, :P], w2_c[:], w2_s[:])
+
+        z_bf = [z_first[:, b * PACK * CHUNK : (b + 1) * PACK * CHUNK] for b in range(2)]
+        z_last = tile("z_last", [P, PACK * HALF], BF16, "near2_0")
+        z_bf.extend(z_last[:, b * PACK * CHUNK : (b + 1) * PACK * CHUNK] for b in range(2))
         h_bf = [tile("h_bf%d" % b, [P, PACK * CHUNK], BF16) for b in range(CHUNKS)]
 
         def summed(b):
-            nc.vector.tensor_tensor(woven(z_bf[b]), by_lines(own[:, :, run(b)]), by_lines(near2[:, :, run(b)]), ADD)
+            nc.vector.tensor_tensor(woven(z_bf[b]), by_lines(own[1][:, :, run(b - 2)]), by_lines(near2_all[1][:, :, run(b - 2)]), ADD)
 
         def hidden(b):
             z_c, z_s = quantize("z%d" % b, CHUNK, z_bf[b])
@@ -226,20 +242,22 @@ def tile_picked_gin8_gelu_po_kernel(tc, x_words, x_scales, w1, eps, w2, res, w3_
 
         def residual(b, banks):
             result = tile("result%d" % b, [P, PACK, CHUNK], F32)
+            rows = out_0.rearrange("(p t) j -> p t j", t=PACK)[:, :, run(b)]
             planes = PACK // len(banks)
             for i, o_ps in enumerate(banks):
                 mine = slice(i * planes, (i + 1) * planes)
                 nc.vector.tensor_tensor(result[:, mine, :], o_ps[:], res_t[:, mine, run(b)], ADD)
-            nc.sync.dma_start(out=out_0.rearrange("(p t) j -> p t j", t=PACK)[:, :, run(b)], in_=result[:])
+                if b == 0:
+                    nc.sync.dma_start(out=rows[:, mine, :], in_=result[:, mine, :])
+            if b > 0:
+                nc.sync.dma_start(out=rows, in_=result[:])
             return result
 
-        summed(0)
-        hidden(0)
-        for b in (1, 2):
-            summed(b)
-        for b in (1, 2):
+        for b in (0, 1):
             hidden(b)
-        summed(LAST)
+        for b in (2, LAST):
+            summed(b)
+        hidden(2)
         o_banks = [third(0)]
         hidden(LAST)
         results = []
@@ -262,8 +280,7 @@ def tile_picked_gin8_gelu_po_kernel(tc, x_words, x_scales, w1, eps, w2, res, w3_
             quantize_into(out_c[:, cols], out_s[:, cols], last_bf[i][:])
 
         out_words = out_1[0].rearrange("p n t -> p (n t)").bitcast(I32)
-        for u in range(2):
-            nc.sync.dma_start(out=out_words[:, half(u)], in_=out_c[:, half(u)].bitcast(I32))
+        nc.sync.dma_start(out=out_words, in_=out_c[:].bitcast(I32))
         for g in range(QUADS):
             queue = nc.scalar if g % 2 else nc.sync
             queue.dma_start(out=out_2[0][4 * g : 4 * g + 4, :].bitcast(I32), in_=out_s[32 * g : 32 * g + 4, :].bitcast(I32))

@@ -33,8 +33,6 @@ FIRST = T // 4
 H_BANKS = (5, 6, 7, 0)
 O_BANKS = ((1, 2), (3,), (4,), (5, 6))
 
-WARM_BANK = 3
-
 AT_W1 = 2 * PACK * D
 AT_Y = AT_W1 + 4 * D
 
@@ -211,8 +209,6 @@ def tile_picked_gin8_gelu_po_kernel(tc, x_words, x_scales, w1, eps, w2, res, w3_
         by_vector(near2, p2_t, 0, 1)
         for t in range(PACK):
             add_own(t, 1)
-
-        product(bank("warm", WARM_BANK, [P, D])[:], w2_c[:, :P].bitcast(FP8X4), w2_s[:, :P], w2_c[:], w2_s[:])
 
         z_bf = [z_first[:, b * PACK * CHUNK : (b + 1) * PACK * CHUNK] for b in range(2)]
         z_last = tile("z_last", [P, PACK * HALF], BF16, "near2_0")

from contextlib import ExitStack

import concourse.mybir as mybir

F32 = mybir.dt.float32
BF16 = mybir.dt.bfloat16
I32 = mybir.dt.int32
U32 = mybir.dt.uint32
U16 = mybir.dt.uint16
U8 = mybir.dt.uint8
FP8X4 = mybir.dt.float8_e4m3fn_x4
FP4X4 = mybir.dt.float4_e2m1fn_x4
ADD = mybir.AluOpType.add
MULT = mybir.AluOpType.mult
COPY = mybir.ActivationFunctionType.Copy
GELU = mybir.ActivationFunctionType.Gelu_apprx_tanh

P = 128
PACK = 4
T = 2048
S = 512
D = 512
STRIPE = 16
QUADS = 4
SPREAD = 8
PAIRS = (slice(0, 2), slice(2, 4))
LINE = 4
CHUNK = 128
CHUNKS = S // CHUNK
LAST = CHUNKS - 1
HALF = S // 2
FIRST = T // 4
H_BANKS = (5, 6, 7, 0)
O_BANKS = ((1, 2), (3,), (4,), (5, 6))

AT_W1 = 2 * PACK * D
AT_Y = AT_W1 + 4 * D

FLOPS = 3 * 2 * D * D * S


def tile_picked_gin8_gelu_po_kernel(tc, x_words, x_scales, w1, eps, w2, res, w3_words, w3_scales, offs, p1, p2, out_0, out_1, out_2):
    nc = tc.nc
    with ExitStack() as ctx:
        keep = ctx.enter_context(tc.tile_pool(name="keep", bufs=1))
        placed = ctx.enter_context(tc.tile_pool(name="placed", bufs=1))
        psum = ctx.enter_context(tc.psum_pool(name="psum", bufs=1))

        def tile(name, shape, dtype, tag=None):
            return keep.tile(shape, dtype, name=name, tag=tag or name, align_bytes=64)

        def bank(name, number, shape):
            return psum.tile(shape, F32, name=name, tag="bank%d" % number)

        def half(u):
            return slice(u * HALF, (u + 1) * HALF)

        def run(n):
            return slice(n * P, (n + 1) * P)

        def entries(list_t, cols):
            return list_t[:, cols.start // STRIPE : cols.stop // STRIPE]

        def load_scale_rows(scale_tile, rows):
            nc.sync.dma_start(out=scale_tile[0:P:SPREAD, :].bitcast(I32), in_=rows.bitcast(I32))

        def place_scale_rows(queue, scale_tile, spread):
            for g in range(QUADS):
                queue.dma_start(out=scale_tile[32 * g : 32 * g + 4, :].bitcast(I32), in_=spread[32 * g : 32 * g + 32 : SPREAD, :].bitcast(I32))

        def round_and_deal(copy, w_bf, w_raw, pair, share=slice(0, P)):
            copy(out=w_bf.rearrange("p (t m j) -> p m j t", m=P, j=PACK)[:, share], in_=w_raw.rearrange("p j (m t) -> p m j t", t=PACK)[:, :, :, pair])

        def stream_copy(out, in_):
            nc.gpsimd.tensor_scalar(out, in_, 1.0, 0.0, MULT, ADD)

        def woven(dst):
            return dst.rearrange("p (c i t) -> p c t i", t=PACK, i=LINE)

        def by_lines(src):
            return src.rearrange("p t (c i) -> p c t i", i=LINE)

        def interleave(copy, dst, src):
            copy(out=woven(dst), in_=by_lines(src))

        def quantize_into(codes, scales, src):
            nc.vector.quantize_mx(out=codes.bitcast(FP8X4), scales=scales, in_=src)

        def quantize(name, width, src):
            codes, scales = tile(name + "_c", [P, width], U32), tile(name + "_s", [P, width], U8)
            quantize_into(codes[:], scales[:], src)
            return codes, scales

        def product(out, lhs_c, lhs_s, rhs_c, rhs_s):
            nc.tensor.matmul_mx(out=out, lhsT=lhs_c, lhsT_scale=lhs_s, rhs=rhs_c.bitcast(FP8X4), rhs_scale=rhs_s, start=True, stop=True)

        offs_t = keep.tile([P, S // STRIPE], U16, name="offs_t")
        p1_t = keep.tile([P, S // STRIPE], U16, name="p1_t")
        p2_t = keep.tile([P, S // STRIPE], U16, name="p2_t")
        xs_all = tile("xs_all", [P, T], U8)
        w3s_raw = tile("w3s_raw", [P, D], U8)
        xs = tile("xs", [P, S], U8)
        for zeroed in (xs_all[:], w3s_raw[:], xs[:]):
            nc.vector.memset(zeroed.bitcast(I32), 0)
        warm = keep.tile([P, 2], F32, name="warm")
        nc.vector.memset(warm[:, 0:1], 0.0)
        nc.scalar.activation(out=warm[:, 1:2], in_=warm[:, 0:1], func=GELU)

        eps_t = keep.tile([P, PACK, 1], F32, name="eps_t")
        nc.scalar.dma_start(out=eps_t[:], in_=eps.rearrange("(p t) o -> p t o", t=PACK))
        w1_half = [tile("w1_half%d" % u, [P, 2, D], F32) for u in range(2)]
        w1_rows = w1.rearrange("(p j) c -> p j c", j=PACK)
        xw_all = tile("xw_all", [P, T], U32)
        xw_rows = x_words[0].rearrange("p n t -> p (n t)").bitcast(I32)
        nc.sync.dma_start(out=xw_all[:, :FIRST].bitcast(I32), in_=xw_rows[:, :FIRST])
        nc.sync.dma_start(offs_t[:], offs)
        load_scale_rows(xs_all, x_scales[0])
        load_scale_rows(w3s_raw, w3_scales[0])
        nc.sync.dma_start(p1_t[:], p1)
        nc.sync.dma_start(p2_t[:], p2)
        nc.sync.dma_start(out=xw_all[:, FIRST:].bitcast(I32), in_=xw_rows[:, FIRST:])
        for u in range(2):
            nc.sync.dma_start(out=w1_half[u][:], in_=w1_rows[:, PAIRS[u], :])
        w3w_raw = placed.tile([P, 4 * PACK * S], U8, name="w3w_raw", offset=AT_Y)[:, : 2 * D]
        nc.sync.dma_start(out=w3w_raw.bitcast(I32), in_=w3_words[0].bitcast(I32))

        xs_spread = tile("xs_spread", [P, S], U8)
        nc.vector.tensor_copy(out=xs_spread[:], in_=xs_all[:].indirect(offs_t[:]))
        place_scale_rows(nc.scalar, xs, xs_spread)
        w3s_spread = tile("w3s_spread", [P, D], U8, "xs_all")
        nc.vector.tensor_copy(out=w3s_spread[:].rearrange("p (t m) -> p t m", t=PACK), in_=w3s_raw[:].rearrange("p (m t) -> p t m", t=PACK))

        xw = tile("xw", [P, S], U32)
        nc.vector.tensor_copy(out=xw[:], in_=xw_all[:].indirect(offs_t[:]))
        w1_bf = [tile("w1_bf%d" % i, [P, width], BF16) for i, width in enumerate((D, D, 2 * D))]
        w1_c, w1_s = placed.tile([P, D], U32, name="w1_c", offset=AT_W1, align_bytes=64), tile("w1_s", [P, D], U8)
        for u in range(2):
            rows = w1_half[u][:].rearrange("p j (m t) -> p m j t", t=PACK)
            for t in range(2):
                nc.vector.tensor_copy(out=w1_bf[t][:].rearrange("p (m j) -> p m j", j=PACK)[:, :, PAIRS[u]], in_=rows[:, :, :, t])
            nc.scalar.copy(out=w1_bf[2][:].rearrange("p (t m j) -> p m j t", m=P, j=PACK)[:, :, PAIRS[u]], in_=rows[:, :, :, PAIRS[1]])
        for t in range(2):
            quantize_into(w1_c[:, run(t)], w1_s[:, run(t)], w1_bf[t][:])
        quantize_into(w1_c[:, half(1)], w1_s[:, half(1)], w1_bf[2][:])

        stage = tile("stage", [P, (PACK - 1) * HALF + PACK * D], F32, "xw_all")
        w2_raw = stage[:, (PACK - 1) * HALF :].rearrange("p (j c) -> p j c", j=PACK)
        nc.sync.dma_start(out=w2_raw, in_=w2.rearrange("(p j) c -> p j c", j=PACK))
        res_t = tile("res_t", [P, PACK, S], F32, "w1_half1")
        nc.sync.dma_start(out=res_t[:], in_=res.rearrange("(p t) j -> p t j", t=PACK))

        w3s = tile("w3s", [P, D], U8, "xs_spread")
        place_scale_rows(nc.sync, w3s, w3s_spread)

        w3w = tile("w3w", [P, 2 * D], U8, "w1_half0")
        nc.scalar.copy(out=w3w[:].bitcast(U16).rearrange("p (t m) -> p t m", t=PACK), in_=w3w_raw.bitcast(U16).rearrange("p (m t) -> p t m", t=PACK))

        y = [placed.tile([P, S], F32, name="y%d" % t, offset=AT_Y + 4 * S * t) for t in range(PACK)]
        y_ps = [[(bank("y0_%d" % u, u, [P, HALF]), half(u)) for u in range(2)]]
        y_ps.extend([(bank("y%d" % t, t + 1, [P, S]), slice(0, S))] for t in range(1, PACK))
        for t in range(PACK):
            for u, (piece, cols) in enumerate(y_ps[t]):
                product(piece[:], w1_c[:, run(t)].bitcast(FP8X4), w1_s[:, run(t)], xw[:, cols], xs[:, cols])
                copy = nc.vector.tensor_copy if t == u == 0 else nc.scalar.copy
                copy(out=y[t][:, cols], in_=piece[:])

        w2_bf = placed.tile([P, PACK * D], BF16, name="w2_bf", offset=0, align_bytes=64)
        stream_copy(out=w2_bf[:].rearrange("p (t m j) -> p m j t", m=P, j=PACK), in_=w2_raw.rearrange("p j (m t) -> p m j t", t=PACK))

        near1 = [[tile("near1_0_%d" % t, [P, HALF], F32)[:] for t in range(PACK)]]
        near1.append([placed.tile([P, HALF], F32, name="near1_1_%d" % t, offset=AT_W1 + 4 * HALF * (t - 1))[:] for t in (1, 2)] + [tile("near1_1_3", [P, HALF], F32)[:]])
        on_w2 = [stage[:, i * PACK * HALF : (i + 1) * PACK * HALF].rearrange("p (t c) -> p t c", t=PACK) for i in range(2)]
        near1[1] = [stage[:, 2 * PACK * HALF : (2 * PACK + 1) * HALF]] + near1[1]
        near2_all = [tile("near2_0", [P, PACK, HALF], F32)[:], on_w2[1]]
        near2 = [[near2_all[u][:, t, :] for t in range(PACK)] for u in range(2)]
        own = [on_w2[0], placed.tile([P, PACK, HALF], F32, name="own_1", offset=0, align_bytes=64)[:]]

        def by_vector(near, list_t, t, u):
            nc.vector.tensor_copy(out=near[u][t], in_=y[t][:].indirect(entries(list_t, half(u))))

        def by_scalar(near, list_t, t, u):
            nc.scalar.activation(near[u][t], y[t][:].indirect(entries(list_t, half(u))), COPY)

        def add_own(t, u):
            source = y_ps[t][u][0][:] if t == 0 else y_ps[t][0][0][:, half(u)]
            nc.vector.scalar_tensor_tensor(own[u][:, t, :], source, eps_t[:, t, :], near1[u][t], MULT, ADD)

        for t in range(2):
            by_vector(near1, p1_t, t, 0)
            by_vector(near2, p2_t, t, 0)
        nc.vector.tensor_copy(out=near2[0][2][:, run(0)], in_=y[2][:].indirect(entries(p2_t, run(0))))
        for t in range(2, PACK):
            by_scalar(near1, p1_t, t, 0)
        nc.scalar.activation(near2[0][2][:, run(1)], y[2][:].indirect(entries(p2_t, run(1))), COPY)
        by_scalar(near2, p2_t, 3, 0)
        for t in range(PACK):
            add_own(t, 0)
        w2_c, w2_s = quantize("w2", D, w2_bf[:])

        z_first = tile("z_first", [P, PACK * HALF], BF16)
        nc.gpsimd.tensor_tensor(woven(z_first[:]), by_lines(own[0]), by_lines(near2_all[0]), ADD)

        for t in range(1, PACK):
            by_scalar(near1, p1_t, t, 1)
        for cols in (run(0), run(1)):
            for t in range(1, PACK):
                nc.scalar.activation(near2[1][t][:, cols], y[t][:].indirect(entries(p2_t, slice(HALF + cols.start, HALF + cols.stop))), COPY)
        by_vector(near1, p1_t, 0, 1)
        by_vector(near2, p2_t, 0, 1)
        for t in range(PACK):
            add_own(t, 1)

        z_bf = [z_first[:, b * PACK * CHUNK : (b + 1) * PACK * CHUNK] for b in range(2)]
        z_last = tile("z_last", [P, PACK * HALF], BF16, "near2_0")
        z_bf.extend(z_last[:, b * PACK * CHUNK : (b + 1) * PACK * CHUNK] for b in range(2))
        h_bf = [tile("h_bf%d" % b, [P, PACK * CHUNK], BF16) for b in range(CHUNKS)]

        def summed(b):
            nc.vector.tensor_tensor(woven(z_bf[b]), by_lines(own[1][:, :, run(b - 2)]), by_lines(near2_all[1][:, :, run(b - 2)]), ADD)

        def hidden(b):
            z_c, z_s = quantize("z%d" % b, CHUNK, z_bf[b])
            h_ps = bank("h_ps%d" % b, H_BANKS[b], [P, PACK, CHUNK])
            for t in range(PACK):
                product(h_ps[:, t, :], w2_c[:, run(t)].bitcast(FP8X4), w2_s[:, run(t)], z_c[:], z_s[:])
            nc.scalar.activation(out=woven(h_bf[b][:]), in_=by_lines(h_ps[:]), func=GELU)

        def third(b):
            h_c, h_s = quantize("h%d" % b, CHUNK, h_bf[b][:])
            planes = PACK // len(O_BANKS[b])
            banks = []
            for i, number in enumerate(O_BANKS[b]):
                banks.append(bank("o_ps%d_%d" % (b, i), number, [P, planes, CHUNK]))
                for e in range(planes):
                    t = i * planes + e
                    product(banks[i][:, e, :], w3w[:, 2 * t * P : 2 * (t + 1) * P].bitcast(FP4X4), w3s[:, run(t)], h_c[:], h_s[:])
            return banks

        def residual(b, banks):
            result = tile("result%d" % b, [P, PACK, CHUNK], F32)
            rows = out_0.rearrange("(p t) j -> p t j", t=PACK)[:, :, run(b)]
            planes = PACK // len(banks)
            for i, o_ps in enumerate(banks):
                mine = slice(i * planes, (i + 1) * planes)
                nc.vector.tensor_tensor(result[:, mine, :], o_ps[:], res_t[:, mine, run(b)], ADD)
                if b == 0:
                    nc.sync.dma_start(out=rows[:, mine, :], in_=result[:, mine, :])
            if b > 0:
                nc.sync.dma_start(out=rows, in_=result[:])
            return result

        for b in (0, 1):
            hidden(b)
        for b in (2, LAST):
            summed(b)
        hidden(2)
        o_banks = [third(0)]
        hidden(LAST)
        results = []
        for b in range(1, CHUNKS):
            o_banks.append(third(b))
            results.append(residual(b - 1, o_banks[b - 1]))
        results.append(residual(LAST, o_banks[LAST]))

        out_c, out_s = tile("out_c", [P, S], U32), tile("out_s", [P, S], U8)
        for b in range(LAST):
            o_bf = tile("o_bf%d" % b, [P, PACK * CHUNK], BF16, None if b else "z%d_c" % LAST)
            interleave(nc.scalar.copy, o_bf[:], results[b][:])
            quantize_into(out_c[:, run(b)], out_s[:, run(b)], o_bf[:])
        width = CHUNK // 2
        last_bf = [tile("last_bf%d" % i, [P, PACK * width], BF16) for i in range(2)]
        for i, copy in enumerate((nc.vector.tensor_copy, nc.scalar.copy)):
            interleave(copy, last_bf[i][:], results[LAST][:, :, i * width : (i + 1) * width])
        for i in range(2):
            cols = slice(LAST * CHUNK + i * width, LAST * CHUNK + (i + 1) * width)
            quantize_into(out_c[:, cols], out_s[:, cols], last_bf[i][:])

        out_words = out_1[0].rearrange("p n t -> p (n t)").bitcast(I32)
        nc.sync.dma_start(out=out_words, in_=out_c[:].bitcast(I32))
        for g in range(QUADS):
            queue = nc.scalar if g % 2 else nc.sync
            queue.dma_start(out=out_2[0][4 * g : 4 * g + 4, :].bitcast(I32), in_=out_s[32 * g : 32 * g + 4, :].bitcast(I32))
